import numpy as np, ml_dtypes
CORES = [9,25,41,57]
N = 4
BF = ml_dtypes.bfloat16
W, B, L, J, VIS, ST = 3584, 2560, 256, 1024, 5, 2
def pick(rng, share, *tail):
    v = rng.integers(0, W, (N, 8) + tail); pool = rng.integers(0, W, (N, 8, 64)); ix = rng.integers(0, 64, (N, 8) + tail)
    h = np.take_along_axis(pool, ix.reshape(N, 8, -1), 2).reshape(v.shape)
    return np.where(rng.random(v.shape) < np.reshape(share, (N, 8) + (1,) * len(tail)), h, v)
def thread(rng, par, share, out):
    ft = np.full((N, 8, J), W, np.int64); a = np.arange(N)[:, None]; g = np.arange(8)[None, :]
    order = B + np.argsort(rng.random((N, 8, J)), axis=-1)
    for s in range(J):
        n = order[:, :, s]; base = rng.integers(0, B, (N, 8)); o = rng.random((N, 8)) < out
        x = np.where(rng.random((N, 8)) < (share if s else 0.0), order[a, g, rng.integers(0, max(s, 1), (N, 8))], base)
        up = par[a, g, x]
        par[a, g, n] = np.where(o, base, up); par[a, g, x] = np.where(o, up, n); ft[a, g, n - B] = np.where(o, W, x)
        v = np.maximum(up - B, 0); cur = ft[a, g, v]
        ft[a, g, v] = np.where(~o & (up >= B) & (cur == x), n, cur)
    return ft
def parts(rng):
    sh = np.array([0.05, 0.1, 0.3, 0.5])
    x = rng.integers(0, 256, (N, 8, 16, W)); kn = np.zeros((N, 8, 16, W), np.int64)
    kn[:, :, 1:] = pick(rng, rng.choice(sh, (N, 8)), 15, W)
    par = np.zeros((N, 8, W), np.int64); par[:, :, :B] = (rng.random((N, 8, B)) * np.arange(B)).astype(np.int64)
    ft = thread(rng, par, rng.choice(np.array([0.2, 0.5, 0.8]), (N, 8)), 0.0625); kn[:, :, 0] = par
    tr = pick(rng, rng.choice(sh, (N, 8)), W); b = pick(rng, rng.choice(sh, (N, 8)), L); z = rng.integers(0, 256, (N, 8, 16, L))
    m = rng.random((N, 8, L)) < 0.08
    oj = B + L * np.arange(N)[:, None, None] + rng.integers(0, L, (N, 8, L))
    near = np.take_along_axis(x, oj[:, :, None, :], 3) + rng.integers(-9, 10, z.shape)
    b = np.where(m, oj, b); z = np.where(m[:, :, None, :], np.minimum(np.maximum(near, 0), 255), z)
    return x, kn, tr, ft, z, b
def pack(x, kn, tr, ft, z, b):
    return {"x0": np.ascontiguousarray(x.reshape(N, 128, W)).astype(np.float32).astype(BF), "kn": np.ascontiguousarray(kn.reshape(N, 128, W)).astype(np.int32), "tr": tr.astype(np.int32),
            "ft": ft.astype(np.int32), "z0": np.ascontiguousarray(z.reshape(N, 128, L)).astype(np.float32).astype(BF), "bs": b.astype(np.int32)}
def setup_inputs(rng):
    return pack(*parts(rng))
def uneven(rng, top, p, *shape):
    return np.minimum((top * rng.random(shape) ** p).astype(np.int64), top - 1)
def setup_inputs_spread(rng):
    x, kn, tr, ft, z, b = parts(rng); ps = np.array([0.25, 0.5, 1.0, 2.0, 4.0, 8.0])
    x = uneven(rng, 256, rng.choice(ps, (N, 8, 1, W)), N, 8, 16, W); z = uneven(rng, 256, rng.choice(ps, (N, 8, 1, L)), N, 8, 16, L)
    k2 = uneven(rng, W, rng.choice(ps, (N, 8, 16, 1)), N, 8, 16, W); kn[:, :, 1:] = k2[:, :, 1:]; kn[:, 1::2, 0] = k2[:, 1::2, 0]
    f2 = uneven(rng, W + 1, rng.choice(ps, (N, 8, 1)), N, 8, J); ft[:, 1::2] = f2[:, 1::2]
    tr = uneven(rng, W, rng.choice(ps, (N, 8, 1)), N, 8, W); b = uneven(rng, W, rng.choice(ps, (N, 8, 1)), N, 8, L)
    return pack(x, kn, tr, ft, z, b)
def two(rng, lo, hi, *shape):
    return np.where(rng.random(shape) < 0.5, lo, hi)
def setup_inputs_ends(rng):
    x, kn, tr, ft, z, b = parts(rng); e = np.array([0, W - 1])
    x = np.where(rng.random((N, 8, 1, W)) < 0.5, two(rng, 0, 255, N, 8, 1, W), two(rng, 0, 255, N, 8, 16, W))
    z = np.where(rng.random((N, 8, 1, L)) < 0.6, two(rng, 0, 255, N, 8, 1, L), two(rng, 0, 255, N, 8, 16, L))
    kn = np.where(rng.random((N, 8, 16, W)) < 0.72, two(rng, 0, W - 1, N, 8, 16, W), kn)
    tr = np.where(rng.random((N, 8, W)) < 0.7, two(rng, 0, W - 1, N, 8, W), tr)
    ft = np.where(rng.random((N, 8, J)) < 0.7, two(rng, 0, W, N, 8, J), ft)
    b = np.where(rng.random((N, 8, L)) < 0.7, two(rng, 0, W - 1, N, 8, L), b)
    s = int(rng.integers(0, 4))
    for q in range(N):
        for g in range(8):
            c = (q + g + s) % 4
            x[q, g, :, 0] = 255 * (c & 1); x[q, g, :, W - 1] = 255 * (c >> 1)
        v = 255 * ((q + s) & 1); w = (q >> 1) & 1
        x[q, 7, :, 0] = v; x[q, 7, :, W - 1] = v
        kn[q, 7][:, e] = two(rng, 0, W - 1, 16, 2); kn[q, 7, 14, e] = 0; kn[q, 7, 15, e] = W - 1
        z[q, 7, :, w::2] = 255 - v; z[q, 7, :, 1 - w::2] = v
        b[q, 7, :] = two(rng, 0, W - 1, L); b[q, 7, L - 2:] = W - 1
        z[q, :, :, L - 1] = np.where(np.arange(8)[:, None] % 2 == q % 2, 0, 255)
        lo = B + L * ((q - 1) % N)
        x[q, 6] = 255 * (q & 1); z[q, 6] = 255 * (q & 1); tr[q, 6] = 0
        kn[q, 6, :, 0] = rng.integers(lo, lo + L, 16); b[q, 6] = np.where(b[q, 6] == 0, W - 1, b[q, 6])
    return pack(x, kn, tr, ft, z, b)
def chain(par, fo, seq, x):
    up = int(par[x]); par[x] = seq[0]; fo[seq[0] - B] = x
    par[seq[:-1]] = seq[1:]; fo[seq[1:] - B] = seq[:-1]; par[seq[-1]] = up
def setup_inputs_corners(rng):
    x, kn, tr, ft, z, b = parts(rng); sh = int(rng.integers(0, 8)); jn = B + np.arange(J); sits = []
    kinj = B + L * rng.integers(0, N, (N, 8, 1, W)) + rng.integers(0, L, (N, 8, 15, W))
    kn[:, :, 1:] = np.where(rng.random((N, 8, 1, W)) < 0.15, kinj, kn[:, :, 1:])
    for q in range(N):
        nx = L * ((q + 1) % N)
        for g in range(8):
            c = (q + g + sh) % 8; par = kn[q, g, 0]; fo = ft[q, g]
            if c == 7: continue
            par[:] = rng.integers(0, B, W); fo[:] = W; p = rng.permutation(B)[:J]
            if c == 0:
                m = rng.random(W) < 0.1; kn[q, g][:, m] = B + L * rng.integers(0, N, (1, W))[:, m] + rng.integers(0, L, (16, W))[:, m]
            if c == 1: chain(par, fo, jn, int(rng.integers(0, B)))
            if c == 2: chain(par, fo, np.ascontiguousarray(jn.reshape(N, L).T).reshape(-1), int(rng.integers(0, B)))
            if c == 3:
                up = par[p].copy(); par[p] = jn; fo[:] = p; par[B:] = up
                if q % 2 == 0: sits.append((q, g, np.arange(L), p[nx:nx + L]))
            if c == 4:
                fo[:] = rng.integers(0, W + 1, J); par[B:] = rng.integers(0, W, J)
                i = int(rng.integers(0, L)); m = L * min(q, N - 2) + i
                fo[m] = W; par[B + m] = rng.integers(0, B); par[W - 1] = B + m
                if q > 0:
                    n = L * q + (i + 1) % (L - 1); y = int(rng.integers(1, B))
                    fo[n] = y; par[y] = B + n; par[B + n] = rng.integers(0, B)
                    fo[0] = B + n; par[B] = B + 1; fo[1] = W; x[q, g, :, B] = 255 * (np.arange(16) % 2)
            if c == 5:
                fo[:] = 0; par[0] = B + rng.integers(0, J); par[B:] = two(rng, 0, B - 1, J)
            if c == 6:
                w = np.arange(J) % 3
                fo[:] = np.where(w == 0, jn, np.where(w == 1, W, p)); par[p[w == 2]] = jn[w == 2]
                par[B:] = np.where(w == 1, jn, np.where(w == 2, B + (np.arange(J) + L) % J, par[B:]))
                ls = rng.permutation(np.nonzero(w[L * q:L * q + L] == 2)[0])[:8]; js = B + nx + ls
                fo[js - B] = js; par[js] = js; sits.append((q, g, ls, js))
    ch = rng.integers(0, 5, (N, 8, L)); ro = B + L * np.arange(N)[:, None, None] + 0 * ch
    b = np.choose(ch, [0 * ch, 0 * ch + W - 1, ro + np.arange(L), ro + rng.integers(0, L, (N, 8, L)), b])
    h = rng.integers(0, 4, (N, 8, W)); tr = np.choose(h, [rng.integers(B, W, (N, 8, W)), two(rng, 0, W - 1, N, 8, W), tr, tr])
    for q, g, i, v in sits:
        b[q, g, i] = v; z[q, g][:, i] = x[q, g][:, v]
    return pack(x, kn, tr, ft, z, b)
def setup_inputs_crowd(rng):
    x, kn, tr, ft, z, b = parts(rng); hs = np.zeros((N, 8), np.int64)
    for q in range(N):
        own = B + L * q
        kn[q, :, 0, own:own + L] = rng.integers(0, B, (8, L)); ft[q, :, L * q:L * q + L] = W
        for g in range(8):
            h = int(rng.integers(1, B - 1)); h2 = h + 1; c = (g + q) % 4; hs[q, g] = h
            if q < 2:
                b[q, g] = h; kn[q, g, :, h] = h; kn[q, g, :, h2] = h2
                if q == 1 and g % 2: b[q, g, int(rng.integers(0, L))] = h2
            elif q == N - 1:
                b[q, g] = W - 1; kn[q, g, 1:, W - 1] = rng.integers(own, own + L, 15)
                up = int(kn[q, g, 0, W - 1]); x[q, g, :, up] = x[q, g, :, W - 1]
            elif q == 2:
                s = rng.permutation(B)[:L]; b[q, g] = s; kn[q, g][:, s] = s
            else: b[q, g] = rng.choice(np.array([0, h, h2, W - 1]), L)
            if c == 0: tr[q, g] = W - 1
            if c == 1: tr[q, g] = two(rng, 0, h, W)
            if c == 2: tr[q, g] = h
    for g in range(8):
        h = int(hs[0, g]); e = (h + 3) % B; e2 = (h + 4) % B
        kn[0, g, :, e] = e2; kn[0, g, :, e2] = e2; x[0, g, :, e2] = x[0, g, :, e]; tr[N - 1, g, W - 1] = e
    for g in (3, 7):
        h = int(hs[0, g]); e = (int(hs[1, g]) + 3) % B; js = B + rng.permutation(L)[:16]
        z[0, g] = 0; x[0, g, :, h] = 0; tr[0, g, h] = e
        x[1, g, :, e] = 255; kn[1, g, :, e] = js; x[1, g][:, js] = 0; ft[1, g, js[0] - B] = W
    return pack(x, kn, tr, ft, z, b)
def setup_inputs_ties(rng):
    x, kn, tr, ft, z, b = parts(rng)
    lo = rng.integers(0, 247, (N, 8, 1, 1)); sp = np.array([1, 2, 4, 9])[(np.arange(8)[None, :] + rng.integers(0, 4, (N, 1))) % 4].reshape(N, 8, 1, 1)
    x = lo + (rng.random((N, 8, 16, W)) * sp).astype(np.int64); z = lo + (rng.random((N, 8, 16, L)) * sp).astype(np.int64)
    x[..., 1::2] = np.where(rng.random((N, 8, 1, W // 2)) < 0.5, x[..., ::2], x[..., 1::2])
    kn[:, :, 9:] = np.where(rng.random((N, 8, 7, W)) < 0.5, kn[:, :, 2:9], kn[:, :, 9:])
    return pack(x, kn, tr, ft, z, b)
def check_inputs(d):
    bad = []
    for k, lo, hi in (("x0", 0, 255), ("kn", 0, W - 1), ("tr", 0, W - 1), ("ft", 0, W), ("z0", 0, 255), ("bs", 0, W - 1)):
        a = np.asarray(d[k]).astype(np.float64)
        if not (np.min(a) >= lo and np.max(a) <= hi): bad.append("range of " + k)
        elif np.any(np.floor(a) != a): bad.append("whole numbers in " + k)
    return bad
def own(v, r):
    return (v >= B + L * r) & (v < B + L * r + L)
def lowest(key):
    return np.argmax(key[:, :, None] == key[:, None, :], axis=2) == np.arange(L)
def reference(x0, kn, tr, ft, z0, bs):
    X = x0.astype(np.float32).astype(np.int32).reshape(N, 8, 16, W); KN = kn.astype(np.int64).reshape(N, 8, 16, W)
    TR = tr.astype(np.int64); FT = ft.astype(np.int64)
    z = z0.astype(np.float32).astype(np.int32).reshape(N, 8, 16, L); b = bs.astype(np.int64); b0 = np.zeros((N, 8, L), np.int64); A = [0] * N
    g = np.arange(8)[:, None]; lane = np.arange(L)
    for t in range(VIS):
        for q in range(N):
            r = (q - t) % N; lo = B + L * r; Xq = X[q]; Kq = KN[q]; par = Kq[:, 0]; fo = FT[q]; zz = z[r].copy(); s = b[r].copy()
            n = lo + lane; y = fo[:, L * r:L * r + L].copy(); u = par[:, lo:lo + L].copy()
            live = ~own(y, r) & ~own(u, r)
            held = live & (y < W) & (par[g, np.minimum(y, W - 1)] == n)
            uj = np.maximum(u - B, 0); turn = held & (u >= B) & (fo[g, uj] == n)
            gi, li = np.nonzero(held); par[gi, y[gi, li]] = u[gi, li]
            gi, li = np.nonzero(turn); fo[gi, uj[gi, li]] = y[gi, li]
            fo[:, L * r:L * r + L] = np.where(live, W, y)
            for step in range(ST):
                c = Kq[g, :, s]
                xc = np.take_along_axis(Xq, c.reshape(8, 1, L * 16), 2).reshape(8, 16, L, 16)
                d = np.where(own(c, r), 2 ** 20, np.add.reduce(np.abs(xc - zz[:, :, :, None]), axis=1))
                k = np.argmin(d, axis=2)[:, :, None]
                best = np.take_along_axis(d, k, 2)[:, :, 0]; cand = np.take_along_axis(c, k, 2)[:, :, 0]
                here = np.add.reduce(np.abs(np.take_along_axis(Xq, s[:, None, :], 2) - zz), axis=1)
                s = np.where(best < here + (A[r] & 31), cand, s)
            may = live & ~own(s, r); seat = may & lowest(np.where(may, s, W + lane))
            xs = np.take_along_axis(Xq, s[:, None, :], 2)
            gi, li = np.nonzero(seat); m = s[gi, li]; nn = lo + li
            cols = Kq[gi, :, m]; up = cols[:, 0].copy()
            hit = (up >= B) & (fo[gi, np.maximum(up - B, 0)] == m)
            Kq[gi, :, nn] = cols; par[gi, m] = nn
            fo[gi[hit], up[hit] - B] = nn[hit]; fo[gi, nn - B] = m
            Xq[gi, :, nn] = (xs[gi, :, li] + zz[gi, :, li]) >> 1
            A[r] = int(np.sum(live & ~seat))
            z[r] = (zz + xs) >> 1; b[r] = s
        if t > 0:
            for q in range(N):
                r = (q - t) % N; o = b0[r]; gi, li = np.nonzero(lowest(o))
                TR[(q - 1) % N][gi, o[gi, li]] = b[r][gi, li]
        b0 = b.copy()
        if t < VIS - 1:
            for q in range(N):
                r = (q - t) % N; b[r] = np.take_along_axis(TR[q], b0[r], 1)
    zq = np.stack([z[(q - VIS + 1) % N] for q in range(N)])
    return {"yk": np.ascontiguousarray(KN[:, :, :, B:]).reshape(N, 128, J).astype(np.float32), "yp": np.ascontiguousarray(KN[:, :, 0, :B]).astype(np.float32), "yf": FT.astype(np.float32),
            "yt": TR.astype(np.float32), "yx": np.ascontiguousarray(X[:, :, :, B:]).reshape(N, 128, J).astype(np.float32).astype(BF), "yz": zq.reshape(N, 128, L).astype(np.float32).astype(BF)}

@@ -1,0 +1,759 @@
+import numpy as np
+from concourse.bass import DstId, RemoteDMATransfer
+from concourse.mybir import AluOpType as ALU, ActivationFunctionType as ACT
+
+W_, B_, L_, VIS = 3584, 2560, 256, 5
+KW_, DK = 3856, 3600
+FW_, FO, DF = 1296, 2552, 1032
+MID = 1792.0
+WT = 2176.0
+SPLIT = [[(0, 4), (0, 4)], [(64, 8), (32, 8)]]
+CUTS = (32, 64, 96, 128)
+BOOST = {'Vv16u': 1400, 'Ppd0s': 2100, 'Sc3210': -600, 'Ppk101': -100, 'VZ111': -600, 'VE11': -1150, 'Ppwp': -600,
+         'VAq11': -1750, 'Sc32t': 1400, 'Vws': 950, 'VbUs': -150, 'Sxb00': 2100, 'Sypu': -600, 'SXCt': 1500, 'VTTu': 850,
+         'VZ101': -600, 'VAq00': -250, 'Sm0b00': 1400, 'SHCs': 100, 'Sx1b01': 100, 'Ppk010.24': -950, 'Sx1b11': 3000,
+         'Vcui.1': 900, 'Vws.3': 1250, 'Vv16u.1': 550, 'SKNt.1': 250, 'Vcwi': -1500, 'VKNo.1': 500, 'VbUs.1': -100,
+         'Vm1b01.8': 450, 'Sxb00.1': -750, 'Vcfi.6': 2100, 'Sm0b00.1': -1550, 'Vm0b00.8': -700, 'VbU00.1': 700,
+         'Vcfi': 1850, 'VFTi': -600, 'VBDi.1': 600, 'VCKi': 350, 'SFWn11': 1500, 'Vuo': -250, 'Ppk010.32': -450,
+         'Ppk010': 200, 'Sphip': -1500, 'Vg16o.1': 600, 'Vt16s.1': 50, 'VbU01.1': -2100, 'Ppk000.11': -1200,
+         'VTTs.1': -250, 'Vwt.4': 100, 'VZRi': -1500, 'VKNi.1': 1500, 'VR01': 100, 'VcU11': -1500, 'Vm1b01': 150,
+         'Vm1b01.1': 600, 'VZ000.1': -2350, 'Vm0b00.1': 700, 'Ppw00': 500, 'Ppk010.36': -100, 'Sxb01.1': 250,
+         'Ppd111.1': -250, 'Veqo.2': -1500, 'Syku.3': -250, 'VQai': 3350, 'VBDi': 250, 'Vm1b01.4': -850,
+         'Sx0b10.2': -250, 'VPF0i': 250, 'Vcfi.8': 1500, 'Vg16o': 100, 'VREi.1': 600, 'Ppco': 150, 'VPFi': 1500,
+         'Vp16p.1': 100, 'Vup.3': -600, 'SXCt.1': 250, 'Sx1b01.1': -150, 'SFTu.1': -700, 'Sx0b00.4': 600,
+         'Ppk1s.1': 600, 'Ppk000.35': -250, 'Vcii.2': 600, 'Sc32t.1': 500, 'Vut.1': -250, 'Vcfi.5': -600, 'Vwt.1': 100,
+         'Vtmpbi.1': 100, 'VcUt.1': -600, 'Sc32i.1': -600}
+
+SB, F32, BF, F16, I32, U16 = "sbuf", "float32", "bfloat16", "float16", "int32", "uint16"
+SCRATCH = {}
+for _d, _l in ((I32, "kst 3584 fst 1280 trs 224 ci 8"),
+               (F32, "KN 3856 ID 3584 TT 3856 FT 1296 trf 224 onef 128 PF 136 PF0 136 tmpc 544 cf 32 cw 96 c17 16 d0 272 "
+                     "ain 40 aout 40 acc 8 b0 256 bF 16 c32 256 R 544 Aq 32 colY 256 urow 256 nrow 1024 colM 256 KS 256 "
+                     "FWn 768 KWn 512 bb 256 w 512"),
+               (BF, "X 3584 XC 3584 ones 272 Ib 128 Ih 128 In 128 Pm 128 Qb 144 Qa 144 TM 2048 BD 48 ZR 272 CK 544 PH 272 "
+                    "PH0 272 SH 16 RE 32 cq 256 tmpb 272 zin 1280 zp 256 b0h 256 chi 256 x0b 2048 x1b 2048 m0b 2048 m1b 2048 "
+                    "xb 256 mb 256 xs 256 D 32 Z0 288 Z1 288 eq 512 HH 256 HC 256 E 4352 XS 256 XWn 2560 phi 256 xp 256 mp 256"),
+               (F16, "Qh 144 SF 8 g16 512 v16 256 t16 256 p16 256"),
+               (U16, "cu 32 bin 80 oin 80 bU 32 bO 80 cU 256 brow 256 u 256 oT 80")):
+    _l = _l.split()
+    for _n, _c in zip(_l[::2], _l[1::2]):
+        SCRATCH[_n] = (SB, [128, int(_c)], _d)
+for _n in ("tin", "tout", "tback"):
+    SCRATCH[_n] = ("dram", [128, 224], F32)
+for _n in ("pk0", "pk1", "pz", "pd0", "pd1", "pw", "pc", "pn"):
+    SCRATCH[_n] = ("psum", [128, 512], F32)
+SEMAPHORES = ["eV", "eS", "eP", "eG", "sent"] + ["d%d" % i for i in range(70)] + ["r%d" % i for i in range(20)]
+
+GA, SC, PE, HOP, XW, SW = 1.56, 3.8, 0.5, 2600, 110, 70
+
+
+def build(T, topo, core, rank):
+    ops = []
+    tag = ["i"]
+    seen = {}
+    N = len(T.cores)
+    nxt, prv = T.cores[(rank + 1) % N], T.cores[(rank - 1) % N]
+
+    def A(name, a=0, b=None, s=1, p=None):
+        if b is None:
+            b = SCRATCH[name][1][1]
+        ps = slice(None) if p is None else slice(*p)
+        ap = T[name][ps, a:b] if s == 1 else T[name][ps, a:b:s]
+        return (ap, [(name, a, b)], len(range(a, b, s)), SCRATCH[name][2], SCRATCH[name][0])
+
+    def I(win, off):
+        return (win[0].indirect(off[0]), win[1] + off[1], off[2] * 16, win[3], "ind", off[1])
+
+    def add(eng, fn, r, w, cost, kind="c", extra=None):
+        name = eng + (w[0][0] if w else "") + tag[0]
+        seen[name] = seen.get(name, 0) + 1
+        ops.append({"e": eng, "f": [fn], "r": r, "w": w, "c": float(cost), "k": kind, "x": extra,
+                    "t": name, "u": "%s.%d" % (name, seen[name])})
+        return len(ops) - 1
+
+    def merge(n):
+        o = ops[-n]
+        for p in ops[len(ops) - n + 1:]:
+            o["f"] = o["f"] + p["f"]
+            o["r"] = o["r"] + [x for x in p["r"] if x not in o["r"]]
+            o["w"] = o["w"] + [x for x in p["w"] if x not in o["w"]]
+            o["c"] += p["c"]
+        del ops[len(ops) - n + 1:]
+
+    chains = {}
+
+    def chain(key):
+        if key in chains:
+            ops[-1]["after"] = chains[key]
+        chains[key] = len(ops) - 1
+
+    def rw(out, ins):
+        r = []
+        for i in ins:
+            if isinstance(i, tuple):
+                r = r + i[1]
+        if out[4] == "ind":
+            return r + out[5], out[1][:1]
+        return r, out[1]
+
+    def vcost(out, in0, in1=None):
+        if out[4] == "ind":
+            return 60 + SC * out[2]
+        if in0[4] == "ind":
+            return 60 + GA * out[2]
+        n = out[2]
+        if in1 is not None:
+            n = n * (2 if in0[4] == SB and in1[4] == SB else 1)
+        elif out[3] not in (F32, I32) and in0[3] not in (F32, I32):
+            n = n / 2
+        return max(64, n) + 10
+
+    def sv(s):
+        return s[0] if isinstance(s, tuple) else s
+
+    def cp(out, in_):
+        r, w = rw(out, [in_])
+        add("V", lambda q: q.tensor_copy(out[0], in_[0]), r, w, vcost(out, in_))
+
+    def tt(out, in0, in1, op):
+        r, w = rw(out, [in0, in1])
+        add("V", lambda q: q.tensor_tensor(out[0], in0[0], in1[0], op), r, w, vcost(out, in0, in1))
+
+    def ts(out, in0, s1, op0, s2=None, op1=None):
+        r, w = rw(out, [in0, s1, s2])
+        if op1 is None:
+            f = lambda q: q.tensor_scalar(out[0], in0[0], sv(s1), None, op0)
+        else:
+            f = lambda q: q.tensor_scalar(out[0], in0[0], sv(s1), sv(s2), op0, op1)
+        add("V", f, r, w, vcost(out, in0))
+
+    def ms(out, val):
+        add("V", lambda q: q.memset(out[0], val), [], out[1], max(64, out[2] * (1 if out[3] in (F32, I32) else 0.5)))
+
+    def scan(out, a, b):
+        r, w = rw(out, [a, b])
+        add("V", lambda q: q.tensor_tensor_scan(out[0], a[0], b[0], 0.0, ALU.add, ALU.min), r, w, out[2] + 10)
+
+    def act(out, in_, bias=0.0, scale=1.0, func=None, accum=None):
+        r, w = rw(out, [in_, bias, scale])
+        fu = ACT.Identity if func is None else func
+        if accum is None:
+            f = lambda q: q.activation(out[0], in_[0], fu, bias=sv(bias), scale=sv(scale))
+        else:
+            w = w + accum[1]
+            f = lambda q: q.activation(out[0], in_[0], fu, bias=sv(bias), scale=sv(scale), accum_out=accum[0])
+        add("S", f, r, w, 80 + GA * out[2] if in_[4] == "ind" else max(64, out[2]) + 30)
+
+    def mm(out, lhsT, rhs, start, stop):
+        c = max(min(64, lhsT[2]), rhs[2]) * (4 if lhsT[3] == F32 else 1) * PE
+        add("P", lambda q: q.matmul(out[0], lhsT[0], rhs[0], start, stop), lhsT[1] + rhs[1], out[1], c)
+
+    def iota(out, pat, base, cm):
+        if out[3] == I32:
+            f = lambda q: q.iota(out[0], pat, base, cm)
+        else:
+            f = lambda q: q.iota(out[0], pat, base, cm, allow_small_or_imprecise_dtypes=True)
+        add("G", f, [], out[1], 160 + 2 * out[2])
+
+    def asel(out, in_, pat, base, cm):
+        add("G", lambda q: q.affine_select(out[0], in_[0], pat, ALU.is_equal, 0.0, base, cm), in_[1], out[1], 200 + 2 * out[2])
+
+    def dma(eng, out, in_, cost):
+        add(eng, lambda q: q.dma_start(out[0], in_[0]), in_[1], out[1], cost, "d")
+
+    def ext(name, a=None, b=None, rows=slice(None)):
+        if a is None:
+            return (T[name][:], [(name, 0, 1)], 0, "", "hbm")
+        return (T[name][rows, a:b], [(name, a, b)], 0, "", "hbm")
+
+    nr = [0]
+
+    def send(dst, pairs, cost):
+        rid, pid, _ = topo.addr(dst)
+        eng = topo.engines(core, dst)
+        k = len(eng) // len(pairs)
+        sems = []
+        r = []
+        for o, i in pairs:
+            sems.append("r%d" % nr[0])
+            nr[0] += 1
+            r = r + i[1]
+        if len(pairs) == 1:
+            o, i = pairs[0]
+            f = lambda q: q.remote_dma(o[0], i[0], T.sem[sems[0]], T.sem.sent, pid, rid, topo.mask(core, dst))
+        else:
+            def f(q):
+                tr = []
+                for j, (o, i) in enumerate(pairs):
+                    m = sum(1 << e for e in eng[j * k:(j + 1) * k])
+                    tr.append(RemoteDMATransfer(dst_ids=[DstId(rid=rid, pnc=pid)], dma_engine_mask=m,
+                                                remote_sem=T.sem[sems[j]], src=i[0], dst=o[0]))
+                return q.remote_dma_fused(tr, local_sem=T.sem.sent)
+        s = add("G", f, r, [], 150, "s", k * len(pairs))
+        for j, (o, i) in enumerate(pairs):
+            add("R", None, [], o[1], cost, "r", (sems[j], k, s))
+
+    EQ, LT, GT, MUL, ADD, SUB, MAX = ALU.is_equal, ALU.is_lt, ALU.is_gt, ALU.mult, ALU.add, ALU.subtract, ALU.max
+    row0 = (0, 128, 16)
+
+    for j, (a, b) in enumerate(((2560, 3584), (0, 896), (896, 1792), (1792, 2560))):
+        dma("Y" if j % 2 == 0 else "S", A("kst", a, b), ext("kn", a, b), 3500 + 2000 * j)
+        chain("load")
+        cp(A("KN", a, b), A("kst", a, b))
+    ms(A("fst"), 0)
+    dma("Y", A("fst", 0, 1024, 1, row0), ext("ft"), 2600)
+    dma("Y", A("fst", 1024, 1280, 1, row0), ext("bs"), 2600)
+    dma("S", A("zin", 0, 256), ext("z0"), 2600)
+    dma("Y", A("XC"), ext("x0"), 12500)
+    chain("load")
+    dma("Y", A("X"), ext("x0"), 15500)
+    chain("load")
+    dma("Y", A("trs"), ext("tr"), 16000)
+    chain("load")
+    cp(A("trf"), A("trs"))
+    send(nxt, [(ext("tin"), A("trf"))], 6000)
+    for a in range(0, KW_, 964):
+        iota(A("TT", a, a + 964), [[0, 964]], 0, 0)
+    dma("Y", A("TT", 0, W_, 1, row0), ext("tin"), 4000)
+    ms(A("KN", W_, KW_), -1.0)
+    ms(A("FT", 0, 8), -1.0)
+    ms(A("FT", DF, FW_), -1.0)
+    cp(A("FT", 8, DF), A("fst", 0, 1024))
+    cp(A("b0"), A("fst", 1024, 1280))
+
+    iota(A("ID", B_, W_), [[1, 1024]], B_, 0)
+    ms(A("ones"), 1.0)
+    ms(A("onef"), 1.0)
+    asel(A("Qb"), A("ones", 0, 144), [[-16, 9], [-1000, 16]], 16, 1)
+    cp(A("Qh"), A("Qb"))
+    asel(A("Ib"), A("ones", 0, 128), [[-1, 128]], 0, 1)
+    ts(A("Ih"), A("Ib"), 0.5, MUL)
+    ts(A("In"), A("Ib"), -1.0, MUL)
+    iota(A("ci", 0, 1), [[0, 1]], 0, 1)
+    ts(A("ci", 1, 2), A("ci", 0, 1), 15, ALU.bitwise_and)
+    ts(A("ci", 2, 3), A("ci", 0, 1), 4, ALU.arith_shift_right)
+    ts(A("ci", 3, 4), A("ci", 0, 1), 7, ALU.bitwise_and)
+    ts(A("ci", 4, 5), A("ci", 1, 2), 3, ALU.arith_shift_right)
+    ts(A("ci", 5, 6), A("ci", 0, 1), 1, ALU.bitwise_and)
+    ts(A("ci", 6, 7), A("ci", 1, 2), 1, ALU.arith_shift_right)
+    cp(A("cf", 0, 7), A("ci", 0, 7))
+    cP, cR, cG, c7, cV, cE, cS = [A("cf", j, j + 1) for j in range(7)]
+    m0, m1 = A("cf", 8, 9), A("cf", 9, 10)
+    ts(m0, cR, 0.5, GT)
+    ts(m1, cR, 0.5, LT)
+    ts(A("cf", 10, 11), cV, 144.0, MUL, 1.0, ADD)
+    ts(A("cf", 11, 12), c7, 16.0, MUL, A("cf", 10, 11), ADD)
+    ts(A("cf", 12, 13), cG, 2.0, MUL, A("cf", 11, 12), ADD)
+    zl, pl = A("cu", 0, 1), A("cu", 16, 32)
+    cp(zl, A("cf", 12, 13))
+    ts(A("cf", 13, 14), cS, 16.0, MUL, cE, ADD)
+    ts(A("cf", 14, 15), cG, 2.0, MUL, A("cf", 13, 14), ADD)
+    iota(A("tmpc", 0, 128), [[1, 128]], 0, 0)
+    ts(A("Pm"), A("tmpc", 0, 128), A("cf", 14, 15), EQ)
+    iota(A("tmpc", 128, 144), [[128, 2], [2, 8]], 0, 0)
+    ts(pl, A("tmpc", 128, 144), A("cf", 13, 14), ADD)
+    iota(A("tmpc", 160, 176), [[16, 16]], 0, 0)
+    iW, spK, spF = A("cw", 0, 16), A("cw", 16, 32), A("cw", 32, 48)
+    ts(iW, A("tmpc", 160, 176), cR, ADD)
+    ts(spK, iW, float(DK), ADD)
+    ts(spF, iW, float(DF), ADD)
+    ts(A("cw", 64, 80), iW, DK - MID, ADD)
+    ts(A("cw", 80, 96), iW, DF + FO - MID, ADD)
+    ms(A("c17"), WT)
+    iota(A("tmpc", 176, 192), [[0, 2], [1, 8]], 0, 0)
+    two, neg, one = A("BD", 0, 16), A("BD", 16, 32), A("BD", 32, 48)
+    for o, v in ((two, 2 * WT), (neg, -WT), (one, WT)):
+        ts(o, A("tmpc", 176, 192), cG, EQ, v, MUL)
+    iota(A("tmpc", 272, 544), [[0, 2], [1, 8], [0, 17]], 0, 0)
+    ts(A("ZR"), A("tmpc", 272, 544), cG, EQ, -WT, MUL)
+    asel(A("tmpb"), A("ones"), [[0, 2], [-16, 8], [-1, 17]], 1, 1)
+    ms(A("tmpb", 0, 272, 17), 0.0)
+    ts(A("PH", 0, 136), A("tmpb", 0, 136), 1.0 / 32, MUL)
+    ts(A("PH", 136, 272), A("tmpb", 136, 272), -1.0, MUL)
+    cp(A("PF"), A("tmpb", 0, 136))
+    ts(A("PH0"), A("PH"), m0, MUL)
+    ts(A("PF0"), A("PF"), m0, MUL)
+    asel(A("cq", 0, 8), A("ones", 0, 8), [[-16, 8]], 0, 1)
+    ts(A("SH", 0, 8), A("cq", 0, 8), 1.0 / 32, MUL)
+    ts(A("SH", 8, 16), A("cq", 0, 8), -1.0, MUL)
+    cp(A("SF"), A("cq", 0, 8))
+    ms(A("CK"), 0.0)
+    ms(A("CK", 0, 544, 1, (0, 1)), 4194304.0)
+    iota(A("R"), [[0, 32], [128, 17]], 0, 0)
+    cp(A("CK", 0, 544, 1, (32, 33)), A("R", 0, 544, 1, (32, 33)))
+    for s in range(2):
+        ms(A("CK", 272 * s, 272 * s + 136, 1, (64, 65)), -184.0)
+        ms(A("CK", 272 * s + 136, 272 * s + 272, 1, (64, 65)), 4096.0)
+    ms(A("CK", 272, 544, 17, (64, 65)), 0.0)
+    ms(A("CK", 136, 272, 17, (96, 97)), MID)
+    ms(A("CK", 137, 272, 17, (96, 97)), MID)
+    ms(A("d0"), 0.0)
+    ms(A("d0", 0, 272, 17), 67108864.0)
+    iota(A("tmpc", 192, 208), [[1, 2], [2, 8]], 0, 0)
+    ts(A("RE", 0, 16), A("tmpc", 192, 208), cR, EQ, 32.0, MUL)
+    ts(A("RE", 16, 32), A("tmpc", 192, 208), cR, EQ)
+    ms(A("Z0"), 0.0)
+    ms(A("Z1"), 0.0)
+    iota(A("tmpc", 208, 217), [[1, 9]], -1, 0)
+    ms(A("Qa"), 0.0)
+    ts(A("Qa", 0, 144, 16), A("tmpc", 208, 217), cG, EQ)
+    iota(A("tmpc", 224, 240), [[1, 16]], 0, 0)
+    ts(A("cf", 16, 32), A("tmpc", 224, 240), cR, GT)
+    for r in range(16):
+        ts(A("TM", 128 * r, 128 * r + 128), A("Qa", 16 - r, 144 - r), A("cf", 16 + r, 17 + r), MUL)
+    merge(16)
+    ms(A("cq"), -0.25 / 128)
+    ms(A("HC", 0, 16), 0.0)
+    ms(A("FWn", 256, 512), float(W_))
+    ms(A("aout"), 0.0)
+    act(A("nrow"), A("ID", B_, W_), scale=m1)
+    for a in range(0, B_, 640):
+        iota(A("ID", a, a + 640), [[1, 640]], a, 0)
+
+    def conv(bank, c0, Q, name, n, start=True):
+        for r in range(16):
+            mm(A(bank, c0, c0 + n // 16), A(Q, 16 - r, 144 - r), A(name, r, n, 16), start and r == 0, r == 15)
+        merge(16)
+
+    def kin(h, bu):
+        c32 = A("c32", 128 * h, 128 * h + 128)
+        act(c32, I(A("KN", 0, W_), bu))
+        cp(A("cU", 128 * h, 128 * h + 128), c32)
+        act(A("chi", 128 * h, 128 * h + 128), c32, bias=4096.0)
+
+    def starts():
+        conv("pk1", 0, "Qh", "t16", 256)
+        ts(A("bU", 0, 16), A("pk1", 0, 16), MID, ADD)
+
+    def early_kin(t):
+        lo = B_ + L_ * ((rank - t) % N)
+        iota(A("XC", lo, lo + 256), [[0, 256]], 8192, 0)
+        for h in range(2):
+            kin(h, A("bU", 8 * h, 8 * h + 8))
+
+    ts(A("t16"), A("b0"), MID, SUB)
+    act(A("b0h"), A("b0"), bias=4096.0)
+    starts()
+    early_kin(0)
+    nd = [0]
+    wv = lambda j, n=16: A("w", 16 * j, 16 * j + n)
+    uv = lambda j, n=16: A("u", 16 * j, 16 * j + n)
+
+    for t in range(VIS):
+        last = t == VIS - 1
+        r_ = (rank - t) % N
+        lo = B_ + L_ * r_
+        fl = lo - FO
+        nG = A("ID", lo, lo + 256)
+        z = lambda a=0, b=256: A("zin", 256 * t + a, 256 * t + b)
+        xw = 512 * t
+        tag[0] = "o"
+        seen.clear()
+        ts(A("g16", 256, 512), A("KN", lo, lo + 256), MID, SUB)
+        ts(A("g16", 0, 256), A("FT", fl, fl + 256), MID, SUB)
+        conv("pc", 0, "Qh", "g16", 512)
+        ts(uv(0), A("pc", 0, 16), MID, ADD)
+        ts(uv(1), A("pc", 16, 32), MID - FO, ADD, 0.0, MAX)
+        tt(wv(2, 32), A("pc", 0, 32), A("cw", 64, 96), SUB)
+        merge(3)
+        act(wv(0, 32), A("pc", 0, 32), bias=MID - lo - 127.5, func=ACT.Abs)
+        ts(wv(4, 32), wv(0, 32), 128.0, GT)
+        live = wv(6)
+        tt(live, wv(4), wv(5), MUL)
+        tt(wv(7), wv(2), live, MUL)
+        tt(A("eq", 0, 256), I(A("KN"), uv(0)), nG, EQ)
+        tt(A("eq", 256, 512), I(A("FT"), uv(1)), nG, EQ)
+        act(A("colY"), I(A("KN"), uv(0)), scale=m0)
+        act(A("urow"), A("KN", lo, lo + 256), scale=m1)
+        dma("Y", A("FWn", 0, 256), A("FT", fl, fl + 256), 3000)
+        dma("Y", A("XWn", xw, xw + 256), A("X", lo, lo + 256), 3000)
+        conv("pc", 0, "Qb", "eq", 512)
+        tt(wv(8), A("pc", 0, 16), wv(7), MUL)
+        tt(wv(9), A("pc", 0, 16), live, MUL)
+        tt(wv(10), A("pc", 16, 32), wv(3), MUL)
+        tt(wv(11), wv(8), spK, ADD)
+        cp(uv(2), wv(11))
+        tt(I(A("KN"), uv(2)), A("colY"), A("urow"), ADD)
+        tag[0] = "p"
+        ts(A("p16"), I(A("KN", 0, W_), A("bU", 0, 16)), MID, SUB)
+        act(A("phi"), I(A("KN", 0, W_), A("bU", 0, 16)), bias=4096.0)
+        dma("Y", A("KWn", 0, 256), A("KN", lo, lo + 256), 3000)
+        tt(wv(12), wv(10), wv(9), MUL)
+        tt(wv(13), wv(12), spF, ADD)
+        cp(uv(3), wv(13))
+        cp(I(A("FT"), uv(3)), A("FWn", 0, 256))
+        act(wv(14), live, scale=256.0, accum=None if last else A("acc", 0, 1))
+        tt(wv(15), wv(14), iW, ADD)
+        cp(uv(4), wv(15))
+        act(A("FT", fl, fl + 256), I(A("FWn", 0, 512), uv(4)))
+        act(wv(16), live, scale=511.0, bias=1.0)
+        if last:
+            for j in range(N):
+                if j != r_:
+                    a = B_ + 256 * j
+                    dma("Y", ext("yk", 256 * j, 256 * j + 256), A("KN", a, a + 256), 3000)
+                    dma("Y", ext("yx", 256 * j, 256 * j + 256), A("X", a, a + 256), 3000)
+        if t > 0:
+            a0 = A("ain", 8 * t, 8 * t + 1)
+            ts(A("acc", 2, 3), a0, 402653184.0, ADD, 402653184.0, SUB)
+            ts(A("acc", 3, 4), a0, A("acc", 2, 3), SUB, 15.5, ADD)
+            act(A("d0", 1, 272, 17), A("c17"), scale=A("acc", 3, 4))
+        act(A("zp"), I(z(), pl))
+        mm(A("pz", 0, 256), A("Ib"), z(), True, True)
+        conv("pw", 48, "Qh", "p16", 256)
+        ts(uv(10), A("pw", 48, 64), MID, ADD)
+        act(A("xp"), I(A("XC"), uv(10)))
+        for s in range(2):
+            for h in range(2):
+                tag[0] = "%d%d" % (s, h)
+                hs = 128 * h
+                H = lambda name: A(name, hs, hs + 128)
+                zz = z(hs, hs + 128) if s == 0 else H("zp")
+                zP = A("pz", 256 * s + hs, 256 * s + hs + 128)
+                bu = A("bU", 16 * s + 8 * h, 16 * s + 8 * h + 8)
+                pk, xn, mn, Zn = "pk%d" % h, "x%db" % h, "m%db" % h, "Z%d" % h
+                xk = lambda k: A(xn, k, 2048, 16)
+                mk = lambda k, n=1: A(mn, 128 * k, 128 * (k + n))
+                if s == 1:
+                    kin(h, bu)
+                    if h == 0:
+                        mm(A("pz", 256, 512), A("Ib"), A("zp"), True, True)
+                nv, ks = SPLIT[s][h]
+                if nv:
+                    cp(A(xn, 0, 16 * nv), I(A("XC"), A("cU", hs, hs + nv)))
+                l0 = nv
+                for l1 in CUTS:
+                    if l1 > l0:
+                        act(A(xn, 16 * l0, 16 * l1), I(A("XC"), A("cU", hs + l0, hs + l1)))
+                        chain("S")
+                        l0 = l1
+                act(H("xb"), I(A("X"), bu))
+                tt(H("mb"), H("xb"), zP, MAX)
+                kv = list(range(1 - s, 16 - ks))
+                parts = [[k for k in kv if k // 4 == j] for j in range(4 - ks // 4)]
+                for part in parts:
+                    for k in part:
+                        tt(mk(k), xk(k), zP, MAX)
+                    merge(len(part))
+                    chain("V")
+                if s == 0:
+                    tt(H("mp"), H("xp"), zP, MAX)
+                for k0 in range(16 - ks, 16, 4):
+                    pd = "pd%d" % (nd[0] % 2)
+                    nd[0] += 1
+                    for j in range(4):
+                        mm(A(pd, 128 * j, 128 * j + 128), A("In"), zz, True, False)
+                        mm(A(pd, 128 * j, 128 * j + 128), A("Ib"), xk(k0 + j), False, True)
+                    merge(8)
+                    act(mk(k0, 4), A(pd), func=ACT.Abs)
+                key = A(pk, 0, 272)
+                col = lambda j: A(pk, j, 272, 17)
+                mm(key, A("ones", 0, 128), A("CK", 272 * s, 272 * s + 272), True, False)
+                mm(key, zz, A("ZR"), False, False)
+                for k in range(16 - ks, 16):
+                    mm(col(1 + k), zz, one, False, False)
+                merge(2 + ks)
+                mm(key, H("chi"), A("PH" if s else "PH0"), False, False)
+                mm(A(pk, 136, 272), H("c32"), A("PF" if s else "PF0"), False, False)
+                if s == 0:
+                    mm(col(0), H("b0h"), A("SH"), False, False)
+                    mm(col(136), H("t16"), A("SF"), False, False)
+                else:
+                    mm(col(0), A("Pm"), A("D", 16 * h, 16 * h + 16), False, False)
+                merge(4 - s)
+                for k in kv:
+                    mm(col(1 + k), xk(k), neg, False, False)
+                merge(len(kv))
+                mm(col(0), H("xb"), neg, False, False)
+                mm(col(0), H("mb"), two, False, False)
+                merge(2)
+                for part in parts + [list(range(k0, k0 + 4)) for k0 in range(16 - ks, 16, 4)]:
+                    for k in part:
+                        mm(col(1 + k), mk(k), two if k in kv else one, False, s == 1 and k == 15)
+                    merge(len(part))
+                if s == 0:
+                    mm(col(1), H("phi"), A("SH"), False, False)
+                    mm(col(137), H("p16"), A("SF"), False, False)
+                    mm(col(1), H("xp"), neg, False, False)
+                    mm(col(1), H("mp"), two, False, True)
+                    merge(4)
+                scan(A("R", 272 * h, 272 * h + 272), A("d0"), key)
+                ends = A("R", 272 * h + 16, 272 * h + 272, 17)
+                aq, dd = A("Aq", 16 * h, 16 * h + 16), A("D", 16 * h, 16 * h + 16)
+                ts(aq, ends, 1610612736.0, ADD, 1610612736.0, SUB)
+                tt(dd, ends, aq, SUB)
+                cp(I(A(Zn), zl), dd)
+                bP = A("pw", 8 * h, 8 * h + 8)
+                for v in range(2):
+                    for e in range(2):
+                        mm(bP, A(Zn, 144 * v + 1 - e, 144 * v + 129 - e), A("RE", 16 * v + 8 * e, 16 * v + 8 * e + 8),
+                           v + e == 0, v + e == 2)
+                merge(4)
+                if s == 0:
+                    ts(A("bU", 16 + 8 * h, 24 + 8 * h), bP, MID, ADD)
+                    continue
+                boh = A("bO", 16 * t + 8 * h, 16 * t + 8 * h + 8)
+                ts(boh, bP, MID, ADD)
+                ts(A("bF", 8 * h, 8 * h + 8), bP, MID, ADD)
+                merge(2)
+                act(A("FWn", 512 + hs, 640 + hs), I(A("ID"), boh))
+                cp(H("brow"), A("FWn", 512 + hs, 640 + hs))
+                if h == 0:
+                    mm(A("pn", 16, 256), A("TM", 0, 128), A("ones", 0, 240), True, False)
+                for c0 in range(0, 8 * h + 8, 4):
+                    for c in range(c0, c0 + 4):
+                        a = max(16 * c, hs)
+                        ts(A("E", 256 * c + a, 256 * c + hs + 128), A("brow", a, hs + 128), A("bF", c, c + 1), EQ,
+                           A("w", 256 + c, 257 + c), MUL)
+                    merge(4)
+                    cs = [c for c in range(c0, c0 + 4) if 16 * c + 16 < hs + 128]
+                    for c in cs:
+                        a = max(16 * c + 16, hs)
+                        mm(A("pn", a, hs + 128), A("Qa", 16, 144), A("E", 256 * c + a, 256 * c + hs + 128), False, c == 14)
+                    merge(len(cs))
+        tag[0] = "s"
+        bo = A("bO", 16 * t, 16 * t + 16)
+        bi = A("bin", 16 * t, 16 * t + 16)
+        send(prv if last else nxt, [(bi, bo)], HOP)
+        bG = A("FWn", 512, 768)
+        act(A("xs"), I(A("X"), bo))
+        act(A("KWn", 256, 512), I(A("KN", 0, W_), bo))
+        mm(A("pd0", 0, 256), A("ones", 0, 128), A("cq"), True, False)
+        mm(A("pd0", 0, 256), A("Ih"), z(), False, False)
+        merge(2)
+        mm(A("pd0", 0, 256), A("Ih"), A("xs"), False, True)
+        zn = A("XWn", xw + 256, xw + 512)
+        ts(zn, A("pd0", 0, 256), 12582912.0, ADD, 12582912.0, SUB)
+        if last:
+            dma("Y", ext("yz"), zn, 2600)
+        else:
+            send(nxt, [(A("zin", 256 * t + 256, 256 * t + 512), zn)], HOP + 400)
+        if 0 < t < VIS - 1:
+            cp(I(A("TT"), A("oin", 16 * t, 16 * t + 16)), bG)
+        if not last:
+            ts(A("t16"), I(A("TT", 0, W_), bi), MID, SUB)
+            act(A("b0h"), I(A("TT", 0, W_), bi), bias=4096.0)
+            starts()
+        if t == VIS - 2:
+            dma("Y", ext("tout"), A("TT", 0, W_, 1, row0), 4000)
+            send(prv, [(ext("tback"), ext("tout"))], 5000)
+            dma("Y", A("TT", 0, W_, 1, row0), ext("tback"), 4000)
+        act(wv(18), A("bF"), bias=-lo - 127.5, func=ACT.Abs)
+        ts(wv(19), wv(18), 128.0, GT, 512.0, MUL)
+        tt(wv(20), wv(19), live, MUL)
+        tt(wv(21), A("bF"), spK, SUB)
+        act(A("HC", 16, 256), A("pn", 16, 256))
+        for r in range(16):
+            mm(A("pc", 0, 16), A("TM", 128 * r, 128 * r + 128), A("E", r, 16 * 272, 272), r == 0, False)
+        merge(16)
+        conv("pc", 0, "Qb", "HC", 256, start=False)
+        tag[0] = "t"
+        cnt, seat = A("pc", 0, 16), wv(23)
+        tt(seat, cnt, wv(20), LT)
+        ts(wv(26), seat, 256.0, MUL)
+        tt(wv(27), seat, wv(21), MUL)
+        merge(2)
+        tt(wv(28, 32), wv(26, 32), A("cw", 0, 32), ADD)
+        cp(uv(6, 32), wv(28, 32))
+        if last:
+            act(A("KS"), I(A("KWn"), uv(6)))
+            act(A("XS"), I(A("XWn", xw, xw + 512), uv(6)))
+            dma("Y", ext("yk", 256 * r_, 256 * r_ + 256), A("KS"), 3000)
+            dma("Y", ext("yx", 256 * r_, 256 * r_ + 256), A("XS"), 3000)
+        else:
+            ts(wv(25), cnt, 0.5, LT)
+            act(A("KN", lo, lo + 256), I(A("KWn"), uv(6)))
+            act(A("XC", lo, lo + 256), I(A("XWn", xw, xw + 512), uv(6)))
+            early_kin(t + 1)
+            dma("Y", A("X", lo, lo + 256), A("XC", lo, lo + 256), 2600)
+        tag[0] = "u"
+        act(A("colM"), A("KWn", 256, 512), scale=m0)
+        tt(I(A("KN"), uv(7)), A("colM"), A("nrow", 256 * r_, 256 * r_ + 256), ADD)
+        ts(A("v16"), A("KWn", 256, 512), MID, SUB)
+        conv("pk0", 0, "Qh", "v16", 256)
+        ts(uv(5), A("pk0", 0, 16), MID - FO, ADD, 0.0, MAX)
+        tt(wv(17), A("pk0", 0, 16), A("cw", 80, 96), SUB)
+        merge(2)
+        tt(A("HH"), I(A("FT"), uv(5)), bG, EQ)
+        conv("pk0", 0, "Qb", "HH", 256)
+        tt(wv(24), A("pk0", 0, 16), wv(17), MUL)
+        tt(wv(30), wv(26), wv(15), ADD)
+        tt(wv(22), wv(24), seat, MUL)
+        tt(wv(31), wv(22), spF, ADD)
+        cp(uv(8), wv(30))
+        act(A("FT", fl, fl + 256), I(A("FWn"), uv(8)))
+        cp(uv(9), wv(31))
+        cp(I(A("FT"), uv(9)), nG)
+        if not last:
+            act(wv(1), seat, scale=-256.0, accum=A("acc", 1, 2))
+            mm(A("pd1", 0, 1), A("onef"), A("acc", 0, 1), True, False)
+            mm(A("pd1", 0, 1), A("onef"), A("acc", 1, 2), False, True)
+            merge(2)
+            act(A("aout", 8 * t, 8 * t + 1), A("pd1", 0, 1), scale=1.0 / 256, bias=-15.5)
+            tt(wv(19), wv(25), wv(21), MUL)
+            tt(wv(18), wv(19), spK, ADD)
+            ot = A("oT", 16 * t, 16 * t + 16)
+            cp(ot, wv(18))
+            pa = (A("ain", 8 * t + 8, 8 * t + 16), A("aout", 8 * t, 8 * t + 8))
+            send(nxt, [pa] if t == VIS - 2 else [pa, (A("oin", 16 * t + 16, 16 * t + 32), ot)], HOP)
+        else:
+            act(A("bb"), I(A("ID"), bi))
+            cp(I(A("TT"), A("oT", 16 * t - 16, 16 * t)), A("bb"))
+            dma("Y", ext("yt"), A("TT", 0, W_, 1, row0), 3000)
+            dma("S", ext("yp"), A("KN", 0, B_, 1, row0), 3000)
+            for j in range(N):
+                if j != r_:
+                    dma("S", ext("yk", 256 * j, 256 * j + 256, slice(*row0)),
+                        A("KN", B_ + 256 * j, B_ + 256 * j + 256, 1, row0), 2600)
+            dma("Y", ext("yf"), A("FT", 8, DF, 1, row0), 2600)
+    return ops
+
+
+def plan(ops):
+    n = len(ops)
+    hist = {}
+    bank = lambda name: name in SCRATCH and SCRATCH[name][0] == "psum"
+    for i, o in enumerate(ops):
+        dep = {}
+        for acc, wr in ((o["r"], False), (o["w"], True)):
+            for name, a, b in acc:
+                for j, wj, aj, bj in hist.get(name, ()):
+                    other = ops[j]["e"] != o["e"] or ops[j]["k"] != "c" or o["k"] != "c"
+                    if bank(name) and other:
+                        dep[j] = True
+                    elif a < bj and aj < b and (wr or wj):
+                        dep[j] = dep.get(j, False) or other or o["e"] != "P"
+                    elif bank(name):
+                        dep[j] = dep.get(j, False)
+        for acc, wr in ((o["r"], False), (o["w"], True)):
+            for name, a, b in acc:
+                h = hist.setdefault(name, [])
+                if bank(name):
+                    h[:] = []
+                elif wr:
+                    h[:] = [e for e in h if not (a <= e[2] and e[3] <= b)]
+                h.append((i, wr, a, b))
+        dep.pop(i, None)
+        if "after" in o:
+            dep[o["after"]] = dep.get(o["after"], False)
+        if o["k"] == "r":
+            dep = {o["x"][2]: False}
+        o["dep"] = dep
+    dur = [0.0 if o["k"] == "r" else 60.0 if o["k"] == "d" else o["c"] for o in ops]
+    before = [[(j, ops[j]["c"] + (SW if ops[j]["e"] == o["e"] else XW) if w else dur[j]) for j, w in o["dep"].items()]
+              for o in ops]
+
+    def run(boost):
+        level = [0.0] * n
+        floor = [0.0] * n
+        for i in range(n - 1, -1, -1):
+            level[i] = max(level[i] + ops[i]["c"] + boost.get(ops[i]["t"], 0) + boost.get(ops[i]["u"], 0), floor[i])
+            for j, l in before[i]:
+                level[j] = max(level[j], level[i] + l - ops[j]["c"])
+                floor[j] = max(floor[j], level[i] + 0.01)
+        busy = {}
+        at = [0.0] * n
+        for i in sorted(range(n), key=lambda i: (-level[i], i)):
+            s = 0.0
+            for j, l in before[i]:
+                if at[j] + l > s:
+                    s = at[j] + l
+            d = dur[i]
+            if d:
+                lst = busy.setdefault(ops[i]["e"], [])
+                a, b = 0, len(lst)
+                while a < b:
+                    m = (a + b) // 2
+                    if lst[m][1] <= s:
+                        a = m + 1
+                    else:
+                        b = m
+                while a < len(lst) and s + d > lst[a][0]:
+                    s = max(s, lst[a][1])
+                    a += 1
+                lst.insert(a, (s, s + d))
+            at[i] = s
+        return at
+
+    return run(BOOST), run
+
+
+def emit(g, T, ops, start):
+    queue = {"V": g.vector, "S": g.scalar, "P": g.tensor, "G": g, "Y": g.sync}
+    order = sorted(range(len(ops)), key=lambda i: (start[i], i))
+    place = {}
+    seq = {}
+    for i in order:
+        if ops[i]["k"] == "c":
+            seq[ops[i]["e"]] = seq.get(ops[i]["e"], 0) + 1
+            place[i] = seq[ops[i]["e"]]
+    known = {e: {} for e in queue}
+    clock = {}
+    waits = {}
+    marked = set()
+    for i in order:
+        o = ops[i]
+        if o["k"] == "r":
+            clock[i] = {("o", i): 1}
+            continue
+        kn = known[o["e"]]
+        wl = []
+        for j in sorted(o["dep"], key=lambda j: -start[j]):
+            if not o["dep"][j]:
+                continue
+            key, val = (ops[j]["e"], place[j]) if ops[j]["k"] == "c" else (("o", j), 1)
+            if kn.get(key, 0) >= val:
+                continue
+            wl.append(j)
+            marked.add(j)
+            for k2, v2 in clock[j].items():
+                if kn.get(k2, 0) < v2:
+                    kn[k2] = v2
+        waits[i] = wl
+        c = dict(kn)
+        if o["k"] == "c":
+            c[o["e"]] = place[i]
+        else:
+            c[("o", i)] = 1
+        clock[i] = c
+    count = {}
+    target = {}
+    nd = 0
+    sent = 0
+    for i in order:
+        o = ops[i]
+        if o["k"] == "r":
+            target[i] = (o["x"][0], o["x"][1])
+        elif o["k"] == "d":
+            target[i] = ("d%d" % nd, 16)
+            nd += 1
+        elif o["k"] == "c" and i in marked:
+            count[o["e"]] = count.get(o["e"], 0) + 1
+            target[i] = ("e" + o["e"], count[o["e"]])
+    for i in order:
+        o = ops[i]
+        if o["k"] == "r":
+            continue
+        q = queue[o["e"]]
+        for j in waits[i]:
+            q.wait_ge(T.sem[target[j][0]], target[j][1])
+        for f in o["f"]:
+            ins = f(q)
+        if o["k"] == "d":
+            ins.then_inc(T.sem[target[i][0]], 16)
+        elif o["k"] == "s":
+            sent += o["x"]
+        elif i in marked:
+            ins.then_inc(T.sem[target[i][0]], 1)
+    g.wait_ge(T.sem.sent, sent)
+    for i in order:
+        if ops[i]["k"] in ("d", "r") and i not in marked:
+            g.sync.wait_ge(T.sem[target[i][0]], target[i][1])
+
+
+def rank_program(g, core, T, topo):
+    rank = T.rank_of(core)
+    if rank is None:
+        return
+    ops = build(T, topo, core, rank)
+    emit(g, T, ops, plan(ops)[0])

@@ -3,54 +3,44 @@ from concourse.bass import DstId, RemoteDMATransfer
 from concourse.mybir import AluOpType as ALU, ActivationFunctionType as ACT
 
 W_, B_, L_, VIS = 3584, 2560, 256, 5
-KW_, DK = 3856, 3600
-FW_, FO, DF = 1296, 2552, 1032
+F0, DK = 3856, 3600
+FW, FO, DF = 1296, 2552, 1032
+FB = F0 - FO
 MID = 1792.0
 WT = 2176.0
-SPLIT = [[(0, 4), (0, 4)], [(64, 8), (32, 8)]]
-CUTS = (32, 64, 96, 128)
-BOOST = {'Vv16u': 1400, 'Ppd0s': 2100, 'Sc3210': -600, 'Ppk101': -100, 'VZ111': -600, 'VE11': -1150, 'Ppwp': -600,
-         'VAq11': -1750, 'Sc32t': 1400, 'Vws': 950, 'VbUs': -150, 'Sxb00': 2100, 'Sypu': -600, 'SXCt': 1500, 'VTTu': 850,
-         'VZ101': -600, 'VAq00': -250, 'Sm0b00': 1400, 'SHCs': 100, 'Sx1b01': 100, 'Ppk010.24': -950, 'Sx1b11': 3000,
-         'Vcui.1': 900, 'Vws.3': 1250, 'Vv16u.1': 550, 'SKNt.1': 250, 'Vcwi': -1500, 'VKNo.1': 500, 'VbUs.1': -100,
-         'Vm1b01.8': 450, 'Sxb00.1': -750, 'Vcfi.6': 2100, 'Sm0b00.1': -1550, 'Vm0b00.8': -700, 'VbU00.1': 700,
-         'Vcfi': 1850, 'VFTi': -600, 'VBDi.1': 600, 'VCKi': 350, 'SFWn11': 1500, 'Vuo': -250, 'Ppk010.32': -450,
-         'Ppk010': 200, 'Sphip': -1500, 'Vg16o.1': 600, 'Vt16s.1': 50, 'VbU01.1': -2100, 'Ppk000.11': -1200,
-         'VTTs.1': -250, 'Vwt.4': 100, 'VZRi': -1500, 'VKNi.1': 1500, 'VR01': 100, 'VcU11': -1500, 'Vm1b01': 150,
-         'Vm1b01.1': 600, 'VZ000.1': -2350, 'Vm0b00.1': 700, 'Ppw00': 500, 'Ppk010.36': -100, 'Sxb01.1': 250,
-         'Ppd111.1': -250, 'Veqo.2': -1500, 'Syku.3': -250, 'VQai': 3350, 'VBDi': 250, 'Vm1b01.4': -850,
-         'Sx0b10.2': -250, 'VPF0i': 250, 'Vcfi.8': 1500, 'Vg16o': 100, 'VREi.1': 600, 'Ppco': 150, 'VPFi': 1500,
-         'Vp16p.1': 100, 'Vup.3': -600, 'SXCt.1': 250, 'Sx1b01.1': -150, 'SFTu.1': -700, 'Sx0b00.4': 600,
-         'Ppk1s.1': 600, 'Ppk000.35': -250, 'Vcii.2': 600, 'Sc32t.1': 500, 'Vut.1': -250, 'Vcfi.5': -600, 'Vwt.1': 100,
-         'Vtmpbi.1': 100, 'VcUt.1': -600, 'Sc32i.1': -600}
+SPLIT = [[(0, 3, 0), (16, 2, 1)], [(32, 0, 0), (16, 2, 0)]]
+SPLIT0 = [[(64, 1, 1), (32, 1, 0)], [(32, 0, 0), (0, 2, 1)]]
+CUTS = (64, 128)
+OPT = {"brow": 1, "q": 32, "xc": 0, "e0": 0}
+BOOST = {'Vseat': -3500, 'PB01': 2000, 'Sgt00': 2500, 'Vmp00': 500, 'Vt0': 1200, 'Vkin00': -1000, 'VE3': 500, 'Pneg01': 4000, 'SC00': 200, 'Vmb11': 300, 'PAout': 8000, 'GAout': 6000, 'Gdec11': 2500, 'Gdec10': 3000, 'SA01': -2000, 'Pdec11': 500, 'Vturn': -500, 'YKN': 700, 'Vt1': -500, 'Pvl': -500, 'Vgv11': -500, 'Vparts01': -2000, 'Sfar': 4000, 'SXC': 1000, 'Vparts11': 500, 'PE1': -500}
+PASSES = 1
 
 SB, F32, BF, F16, I32, U16 = "sbuf", "float32", "bfloat16", "float16", "int32", "uint16"
 SCRATCH = {}
-for _d, _l in ((I32, "kst 3584 fst 1280 trs 224 ci 8"),
-               (F32, "KN 3856 ID 3584 TT 3856 FT 1296 trf 224 onef 128 PF 136 PF0 136 tmpc 544 cf 32 cw 96 c17 16 d0 272 "
-                     "ain 40 aout 40 acc 8 b0 256 bF 16 c32 256 R 544 Aq 32 colY 256 urow 256 nrow 1024 colM 256 KS 256 "
-                     "FWn 768 KWn 512 bb 256 w 512"),
-               (BF, "X 3584 XC 3584 ones 272 Ib 128 Ih 128 In 128 Pm 128 Qb 144 Qa 144 TM 2048 BD 48 ZR 272 CK 544 PH 272 "
-                    "PH0 272 SH 16 RE 32 cq 256 tmpb 272 zin 1280 zp 256 b0h 256 chi 256 x0b 2048 x1b 2048 m0b 2048 m1b 2048 "
-                    "xb 256 mb 256 xs 256 D 32 Z0 288 Z1 288 eq 512 HH 256 HC 256 E 4352 XS 256 XWn 2560 phi 256 xp 256 mp 256"),
-               (F16, "Qh 144 SF 8 g16 512 v16 256 t16 256 p16 256"),
-               (U16, "cu 32 bin 80 oin 80 bU 32 bO 80 cU 256 brow 256 u 256 oT 80")):
+for _d, _l in ((I32, "kst 3856 fst 1280 trs 224 trt 224 ci 8"),
+               (F32, "KN 5152 ID 3584 TT 3856 trf 224 onef 128 tmpc 256 cf 32 cw 96 c17 16 d0 272 "
+                     "ain 40 aout 40 acc 8 b0 256 bF 16 R 544 Aq 32 colY 256 urow 256 nrow 1024 colM 256 KS 256 "
+                     "FWn 768 KWn 768 bb 256 w 512 q0 128 q1 128 q2 128 o0 64 o1 64 o2 64"),
+               (BF, "X 3584 XC 3584 ones 272 Ib 128 Ih 128 In 128 I8 128 Pm 128 Qb 144 Qa 144 TM 2048 BD 48 CK 544 PH 272 "
+                    "PH0 272 SH 16 RE 64 cq 256 tmpb 272 zin 1280 zp 256 b0h 256 chi 256 x0b 2048 x1b 2048 m0b 2048 m1b 2048 "
+                    "xb 256 mb 256 xs 256 D 32 Z 1152 HC 512 E 4352 XS 256 XWn 3840 phi 256 xp 256 mp 256 lv 16 c64 16 ZR 1904"),
+               (F16, "Qh 144 If 128 SF 8 PF 136 PF0 136 g16 512 e16 512 v16 256 t16 256 p16 256 c16 256 nW 128 brow 256"),
+               (U16, "cu 32 bin 80 oin 80 bU 32 bO 80 cU 256 u 256 sl 320")):
     _l = _l.split()
     for _n, _c in zip(_l[::2], _l[1::2]):
         SCRATCH[_n] = (SB, [128, int(_c)], _d)
-for _n in ("tin", "tout", "tback"):
-    SCRATCH[_n] = ("dram", [128, 224], F32)
-for _n in ("pk0", "pk1", "pz", "pd0", "pd1", "pw", "pc", "pn"):
+for _n, _d in (("tin", I32), ("tback", F32)):
+    SCRATCH[_n] = ("dram", [128, 224], _d)
+for _n in ("pk0", "pk1", "pz0", "pz1", "pd", "pw", "pc", "pn"):
     SCRATCH[_n] = ("psum", [128, 512], F32)
-SEMAPHORES = ["eV", "eS", "eP", "eG", "sent"] + ["d%d" % i for i in range(70)] + ["r%d" % i for i in range(20)]
+SEMAPHORES = ["eV", "eS", "eP", "eG", "sent"] + ["d%d" % i for i in range(80)] + ["r%d" % i for i in range(36)]
 
-GA, SC, PE, HOP, XW, SW = 1.56, 3.8, 0.5, 2600, 110, 70
+GA, SC, PE, HOP, XW, SW, FIX, DL = 1.56, 3.8, 0.55, 4000, 130, 80, 25, 2600
 
 
 def build(T, topo, core, rank):
     ops = []
-    tag = ["i"]
-    seen = {}
+    tag = ["init", -1]
     N = len(T.cores)
     nxt, prv = T.cores[(rank + 1) % N], T.cores[(rank - 1) % N]
 
@@ -65,11 +55,14 @@ def build(T, topo, core, rank):
         return (win[0].indirect(off[0]), win[1] + off[1], off[2] * 16, win[3], "ind", off[1])
 
     def add(eng, fn, r, w, cost, kind="c", extra=None):
-        name = eng + (w[0][0] if w else "") + tag[0]
-        seen[name] = seen.get(name, 0) + 1
         ops.append({"e": eng, "f": [fn], "r": r, "w": w, "c": float(cost), "k": kind, "x": extra,
-                    "t": name, "u": "%s.%d" % (name, seen[name])})
+                    "t": eng + (w[0][0] if w else "") + "." + tag[0], "b": tag[0], "v": tag[1]})
         return len(ops) - 1
+
+    def at(name, t=None):
+        tag[0] = name
+        if t is not None:
+            tag[1] = t
 
     def merge(n):
         o = ops[-n]
@@ -106,7 +99,7 @@ def build(T, topo, core, rank):
             n = n * (2 if in0[4] == SB and in1[4] == SB else 1)
         elif out[3] not in (F32, I32) and in0[3] not in (F32, I32):
             n = n / 2
-        return max(64, n) + 10
+        return max(64, n) + FIX
 
     def sv(s):
         return s[0] if isinstance(s, tuple) else s
@@ -130,9 +123,9 @@ def build(T, topo, core, rank):
     def ms(out, val):
         add("V", lambda q: q.memset(out[0], val), [], out[1], max(64, out[2] * (1 if out[3] in (F32, I32) else 0.5)))
 
-    def scan(out, a, b):
+    def scan(out, a, b, op0, op1):
         r, w = rw(out, [a, b])
-        add("V", lambda q: q.tensor_tensor_scan(out[0], a[0], b[0], 0.0, ALU.add, ALU.min), r, w, out[2] + 10)
+        add("V", lambda q: q.tensor_tensor_scan(out[0], a[0], b[0], 0.0, op0, op1), r, w, max(64, out[2]) + FIX)
 
     def act(out, in_, bias=0.0, scale=1.0, func=None, accum=None):
         r, w = rw(out, [in_, bias, scale])
@@ -142,7 +135,7 @@ def build(T, topo, core, rank):
         else:
             w = w + accum[1]
             f = lambda q: q.activation(out[0], in_[0], fu, bias=sv(bias), scale=sv(scale), accum_out=accum[0])
-        add("S", f, r, w, 80 + GA * out[2] if in_[4] == "ind" else max(64, out[2]) + 30)
+        add("S", f, r, w, 80 + GA * out[2] if in_[4] == "ind" else max(64, out[2]) + 30 + FIX)
 
     def mm(out, lhsT, rhs, start, stop):
         c = max(min(64, lhsT[2]), rhs[2]) * (4 if lhsT[3] == F32 else 1) * PE
@@ -158,7 +151,7 @@ def build(T, topo, core, rank):
     def asel(out, in_, pat, base, cm):
         add("G", lambda q: q.affine_select(out[0], in_[0], pat, ALU.is_equal, 0.0, base, cm), in_[1], out[1], 200 + 2 * out[2])
 
-    def dma(eng, out, in_, cost):
+    def dma(eng, out, in_, cost=DL):
         add(eng, lambda q: q.dma_start(out[0], in_[0]), in_[1], out[1], cost, "d")
 
     def ext(name, a=None, b=None, rows=slice(None)):
@@ -193,147 +186,182 @@ def build(T, topo, core, rank):
         for j, (o, i) in enumerate(pairs):
             add("R", None, [], o[1], cost, "r", (sems[j], k, s))
 
-    EQ, LT, GT, MUL, ADD, SUB, MAX = ALU.is_equal, ALU.is_lt, ALU.is_gt, ALU.mult, ALU.add, ALU.subtract, ALU.max
+    EQ, LT, GT, MUL, ADD, SUB, MAX, MIN = (ALU.is_equal, ALU.is_lt, ALU.is_gt, ALU.mult, ALU.add, ALU.subtract, ALU.max, ALU.min)
     row0 = (0, 128, 16)
+    KIN, KINS, FEET = A("KN", 0, W_), A("KN", 0, F0), A("KN", F0, F0 + FW)
+
+    def fill(out, val, p=None):
+        act(out, A("KN", W_, W_ + out[2], 1, p), bias=val, scale=0.0)
 
     for j, (a, b) in enumerate(((2560, 3584), (0, 896), (896, 1792), (1792, 2560))):
-        dma("Y" if j % 2 == 0 else "S", A("kst", a, b), ext("kn", a, b), 3500 + 2000 * j)
+        dma("Y", A("kst", a, b), ext("kn", a, b), (3700, 4800, 6900, 8700)[j])
         chain("load")
         cp(A("KN", a, b), A("kst", a, b))
-    ms(A("fst"), 0)
-    dma("Y", A("fst", 0, 1024, 1, row0), ext("ft"), 2600)
-    dma("Y", A("fst", 1024, 1280, 1, row0), ext("bs"), 2600)
-    dma("S", A("zin", 0, 256), ext("z0"), 2600)
-    dma("Y", A("XC"), ext("x0"), 12500)
+        if j == 0:
+            ms(A("fst", 1024, 1280), 0)
+            dma("S", A("fst", 1024, 1280, 1, row0), ext("bs"), 3500)
+            ms(A("fst", 0, 1024), 0)
+            dma("Y", A("fst", 0, 1024, 1, row0), ext("ft"), 2700)
+            chain("load")
+            dma("S", A("zin", 0, 256), ext("z0"), 3900)
+    dma("Y", A("XC"), ext("x0"), 12700)
     chain("load")
-    dma("Y", A("X"), ext("x0"), 15500)
+    dma("Y", A("trs"), ext("tr"), 13200)
     chain("load")
-    dma("Y", A("trs"), ext("tr"), 16000)
+    dma("Y", A("X"), ext("x0"), 17000)
     chain("load")
-    cp(A("trf"), A("trs"))
-    send(nxt, [(ext("tin"), A("trf"))], 6000)
-    for a in range(0, KW_, 964):
-        iota(A("TT", a, a + 964), [[0, 964]], 0, 0)
-    dma("Y", A("TT", 0, W_, 1, row0), ext("tin"), 4000)
-    ms(A("KN", W_, KW_), -1.0)
-    ms(A("FT", 0, 8), -1.0)
-    ms(A("FT", DF, FW_), -1.0)
-    cp(A("FT", 8, DF), A("fst", 0, 1024))
+    send(nxt, [(ext("tin"), A("trs"))], 6000)
+    ms(A("KN", W_, F0 + 8), -1.0)
+    fill(A("KN", FB + W_, F0 + FW), -1.0)
+    dma("Y", A("kst", 0, W_, 1, row0), ext("tin"), 4000)
+    cp(A("KN", FB + B_, FB + W_), A("fst", 0, 1024))
     cp(A("b0"), A("fst", 1024, 1280))
 
     iota(A("ID", B_, W_), [[1, 1024]], B_, 0)
     ms(A("ones"), 1.0)
-    ms(A("onef"), 1.0)
+    fill(A("onef"), -1.0)
     asel(A("Qb"), A("ones", 0, 144), [[-16, 9], [-1000, 16]], 16, 1)
     cp(A("Qh"), A("Qb"))
     asel(A("Ib"), A("ones", 0, 128), [[-1, 128]], 0, 1)
-    ts(A("Ih"), A("Ib"), 0.5, MUL)
-    ts(A("In"), A("Ib"), -1.0, MUL)
+    act(A("Ih"), A("Ib"), scale=0.5)
+    act(A("In"), A("Ib"), scale=-1.0)
+    act(A("I8"), A("Ib"), scale=-8192.0)
+    cp(A("If"), A("Ib"))
     iota(A("ci", 0, 1), [[0, 1]], 0, 1)
     ts(A("ci", 1, 2), A("ci", 0, 1), 15, ALU.bitwise_and)
     ts(A("ci", 2, 3), A("ci", 0, 1), 4, ALU.arith_shift_right)
     ts(A("ci", 3, 4), A("ci", 0, 1), 7, ALU.bitwise_and)
     ts(A("ci", 4, 5), A("ci", 1, 2), 3, ALU.arith_shift_right)
-    ts(A("ci", 5, 6), A("ci", 0, 1), 1, ALU.bitwise_and)
-    ts(A("ci", 6, 7), A("ci", 1, 2), 1, ALU.arith_shift_right)
-    cp(A("cf", 0, 7), A("ci", 0, 7))
-    cP, cR, cG, c7, cV, cE, cS = [A("cf", j, j + 1) for j in range(7)]
+    cp(A("cf", 0, 5), A("ci", 0, 5))
+    cP, cR, cG, c7, cV = [A("cf", j, j + 1) for j in range(5)]
     m0, m1 = A("cf", 8, 9), A("cf", 9, 10)
     ts(m0, cR, 0.5, GT)
     ts(m1, cR, 0.5, LT)
     ts(A("cf", 10, 11), cV, 144.0, MUL, 1.0, ADD)
     ts(A("cf", 11, 12), c7, 16.0, MUL, A("cf", 10, 11), ADD)
-    ts(A("cf", 12, 13), cG, 2.0, MUL, A("cf", 11, 12), ADD)
-    zl, pl = A("cu", 0, 1), A("cu", 16, 32)
-    cp(zl, A("cf", 12, 13))
-    ts(A("cf", 13, 14), cS, 16.0, MUL, cE, ADD)
-    ts(A("cf", 14, 15), cG, 2.0, MUL, A("cf", 13, 14), ADD)
+    zl = [A("cu", 0, 1), A("cu", 2, 3)]
+    ts(zl[0], cG, 7.0, ADD, A("cf", 11, 12), ADD)
+    ts(zl[1], cG, 2.0, MUL, A("cf", 11, 12), ADD)
+    ts(A("cf", 14, 15), cR, 8.0, MUL, cG, ADD)
     iota(A("tmpc", 0, 128), [[1, 128]], 0, 0)
     ts(A("Pm"), A("tmpc", 0, 128), A("cf", 14, 15), EQ)
-    iota(A("tmpc", 128, 144), [[128, 2], [2, 8]], 0, 0)
-    ts(pl, A("tmpc", 128, 144), A("cf", 13, 14), ADD)
-    iota(A("tmpc", 160, 176), [[16, 16]], 0, 0)
-    iW, spK, spF = A("cw", 0, 16), A("cw", 16, 32), A("cw", 32, 48)
-    ts(iW, A("tmpc", 160, 176), cR, ADD)
-    ts(spK, iW, float(DK), ADD)
-    ts(spF, iW, float(DF), ADD)
-    ts(A("cw", 64, 80), iW, DK - MID, ADD)
-    ts(A("cw", 80, 96), iW, DF + FO - MID, ADD)
-    ms(A("c17"), WT)
-    iota(A("tmpc", 176, 192), [[0, 2], [1, 8]], 0, 0)
+    iota(A("tmpc", 160, 192), [[0, 2], [16, 16]], 0, 0)
+    iW, spK, spM = A("cw", 0, 16), A("cw", 32, 48), A("cw", 64, 96)
+    ts(A("cw", 0, 32), A("tmpc", 160, 192), cR, ADD)
+    act(spK, iW, bias=float(DK))
+    act(A("cw", 64, 80), iW, bias=DK - MID)
+    act(A("cw", 80, 96), iW, bias=DF + FO - MID)
+    for j in range(N):
+        ts(A("nW", 32 * j, 32 * j + 32), A("cw", 0, 32), -1.0, MUL, MID - B_ - L_ * j, ADD)
+    for name in ("o0", "q0"):
+        fill(A(name), 0.0)
+    act(A("o1", 1, 32, 2), iW, bias=float(DK))
+    act(A("o1", 33, 64, 2), iW, bias=float(DF))
+    fill(A("q1", 0, 32, 2), 256.0)
+    act(A("q1", 33, 96, 2), A("cw", 0, 32), bias=float(DK))
+    act(A("q1", 97, 128, 2), iW, bias=float(DF))
+    fill(A("c17"), WT)
+    fill(A("c64"), 64.0)
+    iota(A("tmpc", 192, 208), [[0, 2], [1, 8]], 0, 0)
     two, neg, one = A("BD", 0, 16), A("BD", 16, 32), A("BD", 32, 48)
     for o, v in ((two, 2 * WT), (neg, -WT), (one, WT)):
-        ts(o, A("tmpc", 176, 192), cG, EQ, v, MUL)
-    iota(A("tmpc", 272, 544), [[0, 2], [1, 8], [0, 17]], 0, 0)
-    ts(A("ZR"), A("tmpc", 272, 544), cG, EQ, -WT, MUL)
+        ts(o, A("tmpc", 192, 208), cG, EQ, v, MUL)
     asel(A("tmpb"), A("ones"), [[0, 2], [-16, 8], [-1, 17]], 1, 1)
     ms(A("tmpb", 0, 272, 17), 0.0)
-    ts(A("PH", 0, 136), A("tmpb", 0, 136), 1.0 / 32, MUL)
-    ts(A("PH", 136, 272), A("tmpb", 136, 272), -1.0, MUL)
+    act(A("PH", 0, 136), A("tmpb", 0, 136), scale=1.0 / 32)
+    act(A("PH", 136, 272), A("tmpb", 136, 272), scale=-1.0)
     cp(A("PF"), A("tmpb", 0, 136))
-    ts(A("PH0"), A("PH"), m0, MUL)
+    act(A("PH0"), A("PH"), scale=m0)
     ts(A("PF0"), A("PF"), m0, MUL)
     asel(A("cq", 0, 8), A("ones", 0, 8), [[-16, 8]], 0, 1)
-    ts(A("SH", 0, 8), A("cq", 0, 8), 1.0 / 32, MUL)
-    ts(A("SH", 8, 16), A("cq", 0, 8), -1.0, MUL)
+    act(A("SH", 0, 8), A("cq", 0, 8), scale=1.0 / 32)
+    act(A("SH", 8, 16), A("cq", 0, 8), scale=-1.0)
     cp(A("SF"), A("cq", 0, 8))
-    ms(A("CK"), 0.0)
-    ms(A("CK", 0, 544, 1, (0, 1)), 4194304.0)
-    iota(A("R"), [[0, 32], [128, 17]], 0, 0)
-    cp(A("CK", 0, 544, 1, (32, 33)), A("R", 0, 544, 1, (32, 33)))
+    iota(A("CK"), [[0, 32], [4, 17]], 0, 0)
+    ms(A("CK", 0, 544, 1, (0, 32)), -1179648.0 / 32)
     for s in range(2):
-        ms(A("CK", 272 * s, 272 * s + 136, 1, (64, 65)), -184.0)
-        ms(A("CK", 272 * s + 136, 272 * s + 272, 1, (64, 65)), 4096.0)
-    ms(A("CK", 272, 544, 17, (64, 65)), 0.0)
-    ms(A("CK", 136, 272, 17, (96, 97)), MID)
-    ms(A("CK", 137, 272, 17, (96, 97)), MID)
-    ms(A("d0"), 0.0)
-    ms(A("d0", 0, 272, 17), 67108864.0)
-    iota(A("tmpc", 192, 208), [[1, 2], [2, 8]], 0, 0)
-    ts(A("RE", 0, 16), A("tmpc", 192, 208), cR, EQ, 32.0, MUL)
-    ts(A("RE", 16, 32), A("tmpc", 192, 208), cR, EQ)
-    ms(A("Z0"), 0.0)
-    ms(A("Z1"), 0.0)
-    iota(A("tmpc", 208, 217), [[1, 9]], -1, 0)
-    ms(A("Qa"), 0.0)
-    ts(A("Qa", 0, 144, 16), A("tmpc", 208, 217), cG, EQ)
+        ms(A("CK", 272 * s, 272 * s + 136, 1, (64, 128)), -184.0 / 64)
+        ms(A("CK", 272 * s + 136, 272 * s + 272, 1, (64, 128)), (4096.0 + MID) / 64)
+    ms(A("CK", 272, 544, 17, (64, 128)), 0.0)
+    fill(A("d0"), 0.0)
+    fill(A("d0", 0, 272, 17), 67108864.0)
+    iota(A("tmpc", 208, 224), [[1, 2], [2, 8]], 0, 0)
     iota(A("tmpc", 224, 240), [[1, 16]], 0, 0)
+    for s in range(2):
+        ts(A("RE", 32 * s, 32 * s + 16), A("tmpc", 208 + 16 * s, 224 + 16 * s), cR, EQ, 32.0, MUL)
+        ts(A("RE", 32 * s + 16, 32 * s + 32), A("tmpc", 208 + 16 * s, 224 + 16 * s), cR, EQ)
+    for a in range(0, 1152, 288):
+        ms(A("Z", a, a + 288), 0.0)
+    iota(A("tmpc", 240, 249), [[1, 9]], -1, 0)
+    fill(A("Qa"), 0.0)
+    ts(A("Qa", 0, 144, 16), A("tmpc", 240, 249), cG, EQ)
     ts(A("cf", 16, 32), A("tmpc", 224, 240), cR, GT)
     for r in range(16):
-        ts(A("TM", 128 * r, 128 * r + 128), A("Qa", 16 - r, 144 - r), A("cf", 16 + r, 17 + r), MUL)
-    merge(16)
-    ms(A("cq"), -0.25 / 128)
-    ms(A("HC", 0, 16), 0.0)
-    ms(A("FWn", 256, 512), float(W_))
-    ms(A("aout"), 0.0)
+        act(A("TM", 128 * r, 128 * r + 128), A("Qa", 16 - r, 144 - r), scale=A("cf", 16 + r, 17 + r))
+        if r % 4 == 3:
+            merge(4)
+    fill(A("cq"), -0.25 / 128)
+    fill(A("HC", 0, 16), 0.0)
+    fill(A("FWn", 256, 512), float(W_))
+    fill(A("aout"), 0.0)
+    fill(A("urow"), 0.0)
     act(A("nrow"), A("ID", B_, W_), scale=m1)
     for a in range(0, B_, 640):
         iota(A("ID", a, a + 640), [[1, 640]], a, 0)
 
-    def conv(bank, c0, Q, name, n, start=True):
+    zr = {}
+    for split in SPLIT0 + SPLIT:
+        for nv, ks, own in split:
+            if (ks, own) not in zr and 1 < ks + own < 5:
+                a = 272 * len(zr)
+                zr[ks, own] = A("ZR", a, a + 272)
+                mm(A("pd", 0, 272), A("TM", 0, 128), A("ones"), True, False)
+                cols = [1 + k for k in range(16) if k % 4 >= 4 - ks] + [0] * own
+                for c in cols:
+                    mm(A("pd", c, 272, 17), A("Ib"), one, False, c == cols[-1])
+                merge(1 + len(cols))
+                act(zr[ks, own], A("pd", 0, 272))
+
+    def conv(bank, c0, Q, name, n, start=True, a=0):
         for r in range(16):
-            mm(A(bank, c0, c0 + n // 16), A(Q, 16 - r, 144 - r), A(name, r, n, 16), start and r == 0, r == 15)
+            mm(A(bank, c0, c0 + n // 16), A(Q, 16 - r, 144 - r), A(name, a + r, a + n, 16), start and r == 0, r == 15)
         merge(16)
 
     def kin(h, bu):
-        c32 = A("c32", 128 * h, 128 * h + 128)
-        act(c32, I(A("KN", 0, W_), bu))
-        cp(A("cU", 128 * h, 128 * h + 128), c32)
-        act(A("chi", 128 * h, 128 * h + 128), c32, bias=4096.0)
+        cp(A("cU", 128 * h, 128 * h + 128), I(KIN, bu))
 
-    def starts():
-        conv("pk1", 0, "Qh", "t16", 256)
-        ts(A("bU", 0, 16), A("pk1", 0, 16), MID, ADD)
+    def parts(a, b):
+        ts(A("c16", a, b), A("cU", a, b), MID, SUB)
+        ts(A("chi", a, b), A("cU", a, b), 4096.0, ADD)
+        merge(2)
+
+    def starts(h):
+        pz = "pk%d" % h
+        conv(pz, 0, "Qh", "t16", 128, a=128 * h)
+        ts(A("bU", 8 * h, 8 * h + 8), A(pz, 0, 8), MID, ADD)
+        ts(A("b0h", 128 * h, 128 * h + 128), A("t16", 128 * h, 128 * h + 128), MID + 4096.0, ADD)
 
     def early_kin(t):
         lo = B_ + L_ * ((rank - t) % N)
-        iota(A("XC", lo, lo + 256), [[0, 256]], 8192, 0)
-        for h in range(2):
-            kin(h, A("bU", 8 * h, 8 * h + 8))
+        at("far")
+        if t:
+            iota(A("XC", lo, lo + 256), [[0, 256]], 8192, 0)
+        else:
+            act(A("xb"), I(A("XC"), A("bU", 0, 16)))
+            ms(A("XC", lo, lo + 256), 8192.0)
+        if t or OPT["e0"]:
+            first_kin(1)
+
+    def first_kin(h):
+        at("kin0%d" % h)
+        kin(h, A("bU", 8 * h, 8 * h + 8))
+        at("parts0%d" % h)
+        parts(128 * h, 128 * h + 128)
 
     ts(A("t16"), A("b0"), MID, SUB)
-    act(A("b0h"), A("b0"), bias=4096.0)
-    starts()
+    for h in (1, 0):
+        at("t%d" % h)
+        starts(h)
     early_kin(0)
     nd = [0]
     wv = lambda j, n=16: A("w", 16 * j, 16 * j + n)
@@ -343,269 +371,361 @@ def build(T, topo, core, rank):
         last = t == VIS - 1
         r_ = (rank - t) % N
         lo = B_ + L_ * r_
-        fl = lo - FO
+        fl = FB + lo
         nG = A("ID", lo, lo + 256)
         z = lambda a=0, b=256: A("zin", 256 * t + a, 256 * t + b)
-        xw = 512 * t
-        tag[0] = "o"
-        seen.clear()
+        xw = 768 * t
+        at("yu", t)
+        early = t > 0 or OPT["e0"]
+        if early:
+            first_kin(0)
+        at("yu")
+        if t:
+            dma("Y", A("urow", 0, 256, 1, row0), A("KN", lo, lo + 256, 1, row0))
+            dma("Y", A("FWn", 0, 256), A("KN", fl, fl + 256))
+        else:
+            act(A("urow"), A("KN", lo, lo + 256), scale=m1)
+            act(A("FWn", 0, 256), A("KN", fl, fl + 256))
         ts(A("g16", 256, 512), A("KN", lo, lo + 256), MID, SUB)
-        ts(A("g16", 0, 256), A("FT", fl, fl + 256), MID, SUB)
+        ts(A("g16", 0, 256), A("KN", fl, fl + 256), MID, SUB)
         conv("pc", 0, "Qh", "g16", 512)
         ts(uv(0), A("pc", 0, 16), MID, ADD)
-        ts(uv(1), A("pc", 16, 32), MID - FO, ADD, 0.0, MAX)
-        tt(wv(2, 32), A("pc", 0, 32), A("cw", 64, 96), SUB)
+        ts(uv(1), A("pc", 16, 32), MID + FB, ADD, float(F0), MAX)
+        tt(A("o1", 0, 64, 2), A("pc", 0, 32), spM, SUB)
         merge(3)
+        at("own")
         act(wv(0, 32), A("pc", 0, 32), bias=MID - lo - 127.5, func=ACT.Abs)
-        ts(wv(4, 32), wv(0, 32), 128.0, GT)
-        live = wv(6)
-        tt(live, wv(4), wv(5), MUL)
-        tt(wv(7), wv(2), live, MUL)
-        tt(A("eq", 0, 256), I(A("KN"), uv(0)), nG, EQ)
-        tt(A("eq", 256, 512), I(A("FT"), uv(1)), nG, EQ)
-        act(A("colY"), I(A("KN"), uv(0)), scale=m0)
-        act(A("urow"), A("KN", lo, lo + 256), scale=m1)
-        dma("Y", A("FWn", 0, 256), A("FT", fl, fl + 256), 3000)
-        dma("Y", A("XWn", xw, xw + 256), A("X", lo, lo + 256), 3000)
-        conv("pc", 0, "Qb", "eq", 512)
-        tt(wv(8), A("pc", 0, 16), wv(7), MUL)
-        tt(wv(9), A("pc", 0, 16), live, MUL)
-        tt(wv(10), A("pc", 16, 32), wv(3), MUL)
-        tt(wv(11), wv(8), spK, ADD)
-        cp(uv(2), wv(11))
-        tt(I(A("KN"), uv(2)), A("colY"), A("urow"), ADD)
-        tag[0] = "p"
-        ts(A("p16"), I(A("KN", 0, W_), A("bU", 0, 16)), MID, SUB)
-        act(A("phi"), I(A("KN", 0, W_), A("bU", 0, 16)), bias=4096.0)
-        dma("Y", A("KWn", 0, 256), A("KN", lo, lo + 256), 3000)
-        tt(wv(12), wv(10), wv(9), MUL)
-        tt(wv(13), wv(12), spF, ADD)
-        cp(uv(3), wv(13))
-        cp(I(A("FT"), uv(3)), A("FWn", 0, 256))
-        act(wv(14), live, scale=256.0, accum=None if last else A("acc", 0, 1))
-        tt(wv(15), wv(14), iW, ADD)
-        cp(uv(4), wv(15))
-        act(A("FT", fl, fl + 256), I(A("FWn", 0, 512), uv(4)))
-        act(wv(16), live, scale=511.0, bias=1.0)
+        at("live")
+        tt(wv(4), wv(0), wv(1), MIN)
+        live = A("lv")
+        ts(live, wv(4), 128.0, GT)
+        at("e16")
+        ts(A("e16"), I(A("KN"), uv(0, 32)), MID, SUB)
+        at("colY")
+        act(A("colY"), I(KINS, uv(0)), scale=m0)
+        for j in range(2):
+            dma("Y", A("XWn", xw + 256 * j, xw + 256 * j + 256), A("X", lo, lo + 256))
+        at("held")
+        mm(A("pc", 0, 32), A("If"), A("nW", 32 * r_, 32 * r_ + 32), True, False)
+        mm(A("pc", 0, 16), A("ones", 0, 128), A("c64"), False, False)
+        mm(A("pc", 0, 16), A("I8"), live, False, False)
+        merge(3)
+        conv("pc", 0, "Qh", "e16", 512, start=False)
+        ts(A("o0", 1, 64, 2), A("pc", 0, 32), 0.0, EQ)
+        tt(A("o0", 33, 64, 2), A("o0", 33, 64, 2), A("o0", 1, 32, 2), MUL)
+        scan(A("o2"), A("o0"), A("o1"), MUL, ADD)
+        cp(uv(2, 32), A("o2", 1, 64, 2))
+        tt(I(KINS, uv(2)), A("colY"), A("urow"), ADD)
+        if early:
+            at("p16")
+            ts(A("p16"), I(KIN, A("bU", 0, 16)), MID, SUB)
+            at("phi")
+            ts(A("phi"), A("p16"), MID + 4096.0, ADD)
+        else:
+            first_kin(1)
+            first_kin(0)
+        at("phi")
+        for j in range(2):
+            dma("Y", A("KWn", 256 * j, 256 * j + 256), A("KN", lo, lo + 256))
+        at("turn")
+        cp(I(FEET, uv(3)), A("FWn", 0, 256))
+        at("wts")
+        act(wv(14), live, scale=256.0)
+        tt(A("q1", 1, 32, 2), wv(14), iW, ADD)
+        act(wv(16), live, scale=255.0, bias=1.0)
         if last:
             for j in range(N):
                 if j != r_:
                     a = B_ + 256 * j
                     dma("Y", ext("yk", 256 * j, 256 * j + 256), A("KN", a, a + 256), 3000)
                     dma("Y", ext("yx", 256 * j, 256 * j + 256), A("X", a, a + 256), 3000)
+        at("Ain")
         if t > 0:
             a0 = A("ain", 8 * t, 8 * t + 1)
             ts(A("acc", 2, 3), a0, 402653184.0, ADD, 402653184.0, SUB)
             ts(A("acc", 3, 4), a0, A("acc", 2, 3), SUB, 15.5, ADD)
             act(A("d0", 1, 272, 17), A("c17"), scale=A("acc", 3, 4))
-        act(A("zp"), I(z(), pl))
-        mm(A("pz", 0, 256), A("Ib"), z(), True, True)
-        conv("pw", 48, "Qh", "p16", 256)
-        ts(uv(10), A("pw", 48, 64), MID, ADD)
-        act(A("xp"), I(A("XC"), uv(10)))
+        for h in (1, 0):
+            at("zp%d" % h)
+            for c in range(8):
+                asel(A("zp", 128 * h + c, 128 * h + 128, 8), z(128 * h + 16 * c, 128 * h + 16 * c + 16), [[0, 16]], 0, 0)
+                if c % 2:
+                    merge(2)
+        if early:
+            at("p16")
+            conv("pw", 48, "Qh", "p16", 256)
+            ts(uv(10), A("pw", 48, 64), MID, ADD)
+            for h in (1, 0):
+                at("xp%d" % h)
+                act(A("xp", 128 * h, 128 * h + 128), I(A("XC"), A("u", 160 + 8 * h, 168 + 8 * h)))
+        at("xb0")
+        if t:
+            act(A("xb"), I(A("X"), A("bU", 0, 16)))
         for s in range(2):
-            for h in range(2):
-                tag[0] = "%d%d" % (s, h)
+            for h in (1, 0):
+                on = lambda name: at("%s%d%d" % (name, s, h))
+                apart = early and s == 0
                 hs = 128 * h
                 H = lambda name: A(name, hs, hs + 128)
                 zz = z(hs, hs + 128) if s == 0 else H("zp")
-                zP = A("pz", 256 * s + hs, 256 * s + hs + 128)
+                pz, pk, xn, mn, zo = "pz%d" % h, "pk%d" % h, "x%db" % h, "m%db" % h, 288 * (2 * s + h)
+                zP = A(pz, 0, 512, 4)
                 bu = A("bU", 16 * s + 8 * h, 16 * s + 8 * h + 8)
-                pk, xn, mn, Zn = "pk%d" % h, "x%db" % h, "m%db" % h, "Z%d" % h
-                xk = lambda k: A(xn, k, 2048, 16)
-                mk = lambda k, n=1: A(mn, 128 * k, 128 * (k + n))
+                nv, ks, own = (SPLIT if t else SPLIT0)[s][1 - h]
                 if s == 1:
+                    on("kin")
                     kin(h, bu)
-                    if h == 0:
-                        mm(A("pz", 256, 512), A("Ib"), A("zp"), True, True)
-                nv, ks = SPLIT[s][h]
+                    on("parts")
+                    parts(hs, hs + 128)
+                    on("xb")
+                    act(H("xb"), I(A("X"), bu))
+                on("z")
+                nz = 4 if ks < 4 else 1 - own
+                for j in range(nz):
+                    mm(A(pz, j, 512, 4), A("Ib"), zz, True, True)
+                if nz:
+                    merge(nz)
+                on("gv")
                 if nv:
                     cp(A(xn, 0, 16 * nv), I(A("XC"), A("cU", hs, hs + nv)))
+                on("gs")
                 l0 = nv
                 for l1 in CUTS:
                     if l1 > l0:
                         act(A(xn, 16 * l0, 16 * l1), I(A("XC"), A("cU", hs + l0, hs + l1)))
-                        chain("S")
                         l0 = l1
-                act(H("xb"), I(A("X"), bu))
-                tt(H("mb"), H("xb"), zP, MAX)
-                kv = list(range(1 - s, 16 - ks))
-                parts = [[k for k in kv if k // 4 == j] for j in range(4 - ks // 4)]
-                for part in parts:
-                    for k in part:
-                        tt(mk(k), xk(k), zP, MAX)
-                    merge(len(part))
-                    chain("V")
-                if s == 0:
-                    tt(H("mp"), H("xp"), zP, MAX)
-                for k0 in range(16 - ks, 16, 4):
-                    pd = "pd%d" % (nd[0] % 2)
+                    on("gt")
+                xs_ = lambda j: A(xn, j, 2048, 4)
+                mj = lambda j: A(mn, 512 * j, 512 * j + 512)
+                ks_ = lambda j: [k for k in range(j, 16, 4) if k or not apart]
+                mk = lambda k: A(mn, 512 * (k % 4) + k // 4, 512 * (k % 4) + 512, 4)
+                sv_, ss_ = list(range(4 - ks)), list(range(4 - ks, 4))
+                banks = ("pd", "pc" if s else "pn")
+
+                def diff(x, m, n):
+                    pd = banks[nd[0] % 2]
                     nd[0] += 1
-                    for j in range(4):
-                        mm(A(pd, 128 * j, 128 * j + 128), A("In"), zz, True, False)
-                        mm(A(pd, 128 * j, 128 * j + 128), A("Ib"), xk(k0 + j), False, True)
-                    merge(8)
-                    act(mk(k0, 4), A(pd), func=ACT.Abs)
+                    for j in range(n):
+                        mm(A(pd, j, 128 * n, n), A("In"), zz, j == 0, False)
+                    merge(n)
+                    mm(A(pd, 0, 128 * n), A("Ib"), x, False, True)
+                    act(m, A(pd, 0, 128 * n), func=ACT.Abs)
+
+                on("mb")
+                if own:
+                    diff(H("xb"), H("mb"), 1)
+                else:
+                    tt(H("mb"), H("xb"), zP, MAX)
+                for j in sv_:
+                    on("ABCD"[j])
+                    tt(mj(j), xs_(j), A(pz), MAX)
+                for j in ss_:
+                    on("ABCD"[j])
+                    diff(xs_(j), mj(j), 4)
+                on("mp")
+                if apart:
+                    if own:
+                        diff(H("xp"), H("mp"), 1)
+                    else:
+                        tt(H("mp"), H("xp"), zP, MAX)
+                on("key")
                 key = A(pk, 0, 272)
                 col = lambda j: A(pk, j, 272, 17)
                 mm(key, A("ones", 0, 128), A("CK", 272 * s, 272 * s + 272), True, False)
-                mm(key, zz, A("ZR"), False, False)
-                for k in range(16 - ks, 16):
-                    mm(col(1 + k), zz, one, False, False)
-                merge(2 + ks)
-                mm(key, H("chi"), A("PH" if s else "PH0"), False, False)
-                mm(A(pk, 136, 272), H("c32"), A("PF" if s else "PF0"), False, False)
+                zc = [1 + k for j in ss_ for k in ks_(j)] + ([0, 1][:1 + apart] if own else [])
+                if ks + own == 5:
+                    zc = []
+                elif (ks, own) in zr:
+                    zc = [1] if apart and own != (ks == 4) else []
+                    mm(key, zz, zr[ks, own], False, False)
+                    merge(2)
+                for c in zc:
+                    mm(col(c), zz, neg if ks == 4 else one, False, False)
+                merge(1 + len(zc))
+                mm(key, H("chi"), A("PH0" if apart else "PH"), False, False)
+                mm(A(pk, 136, 272), H("c16"), A("PF0" if apart else "PF"), False, False)
                 if s == 0:
                     mm(col(0), H("b0h"), A("SH"), False, False)
                     mm(col(136), H("t16"), A("SF"), False, False)
                 else:
                     mm(col(0), A("Pm"), A("D", 16 * h, 16 * h + 16), False, False)
                 merge(4 - s)
+                on("neg")
+                kv = [k for j in sv_ for k in ks_(j)]
                 for k in kv:
-                    mm(col(1 + k), xk(k), neg, False, False)
-                merge(len(kv))
-                mm(col(0), H("xb"), neg, False, False)
-                mm(col(0), H("mb"), two, False, False)
-                merge(2)
-                for part in parts + [list(range(k0, k0 + 4)) for k0 in range(16 - ks, 16, 4)]:
-                    for k in part:
-                        mm(col(1 + k), mk(k), two if k in kv else one, False, s == 1 and k == 15)
-                    merge(len(part))
-                if s == 0:
+                    mm(col(1 + k), A(xn, k, 2048, 16), neg, False, False)
+                if kv:
+                    merge(len(kv))
+                turn = sorted(range(4), key=lambda j: (sv_.index(j) if j in sv_ else ss_.index(j), j))
+                for j in turn:
+                    on("ABCD"[j])
+                    if j == turn[-1]:
+                        if not own:
+                            mm(col(0), H("xb"), neg, False, False)
+                        mm(col(0), H("mb"), one if own else two, False, False)
+                        merge(1 if own else 2)
+                    for k in ks_(j):
+                        mm(col(1 + k), mk(k), two if j in sv_ else one, False, not apart and j == turn[-1] and k == j + 12)
+                    merge(len(ks_(j)))
+                on("dec")
+                if apart:
                     mm(col(1), H("phi"), A("SH"), False, False)
                     mm(col(137), H("p16"), A("SF"), False, False)
-                    mm(col(1), H("xp"), neg, False, False)
-                    mm(col(1), H("mp"), two, False, True)
-                    merge(4)
-                scan(A("R", 272 * h, 272 * h + 272), A("d0"), key)
+                    if not own:
+                        mm(col(1), H("xp"), neg, False, False)
+                    mm(col(1), H("mp"), one if own else two, False, True)
+                    merge(3 if own else 4)
+                scan(A("R", 272 * h, 272 * h + 272), A("d0"), key, ADD, MIN)
                 ends = A("R", 272 * h + 16, 272 * h + 272, 17)
                 aq, dd = A("Aq", 16 * h, 16 * h + 16), A("D", 16 * h, 16 * h + 16)
                 ts(aq, ends, 1610612736.0, ADD, 1610612736.0, SUB)
                 tt(dd, ends, aq, SUB)
-                cp(I(A(Zn), zl), dd)
-                bP = A("pw", 8 * h, 8 * h + 8)
+                cp(I(A("Z", zo, zo + 288), zl[s]), dd)
+                bP = A(pk, 288, 296)
                 for v in range(2):
                     for e in range(2):
-                        mm(bP, A(Zn, 144 * v + 1 - e, 144 * v + 129 - e), A("RE", 16 * v + 8 * e, 16 * v + 8 * e + 8),
-                           v + e == 0, v + e == 2)
+                        a = zo + 144 * v + (1 - e) * (1 if s else 8)
+                        c = 32 * s + 16 * v + 8 * e
+                        mm(bP, A("Z", a, a + 128), A("RE", c, c + 8), v + e == 0, v + e == 2)
                 merge(4)
                 if s == 0:
                     ts(A("bU", 16 + 8 * h, 24 + 8 * h), bP, MID, ADD)
                     continue
                 boh = A("bO", 16 * t + 8 * h, 16 * t + 8 * h + 8)
                 ts(boh, bP, MID, ADD)
-                ts(A("bF", 8 * h, 8 * h + 8), bP, MID, ADD)
+                send(prv if last else nxt, [(A("bin", 16 * t + 8 * h, 16 * t + 8 * h + 8), boh)], HOP)
+                at("zn%d" % h)
+                act(H("xs"), I(A("X"), boh))
+                mm(A(pz, 0, 128), A("ones", 0, 128), A("cq", 0, 128), True, False)
+                mm(A(pz, 0, 128), A("Ih"), z(hs, hs + 128), False, False)
                 merge(2)
+                mm(A(pz, 0, 128), A("Ih"), H("xs"), False, True)
+                zn = A("XWn", xw + 512 + hs, xw + 640 + hs)
+                ts(zn, A(pz, 0, 128), 12582912.0, ADD, 12582912.0, SUB)
+                if not last:
+                    send(nxt, [(A("zin", 256 * t + 256 + hs, 256 * t + 384 + hs), zn)], HOP + 300)
+                at("bG%d" % h)
                 act(A("FWn", 512 + hs, 640 + hs), I(A("ID"), boh))
-                cp(H("brow"), A("FWn", 512 + hs, 640 + hs))
-                if h == 0:
+                at("brow%d" % h)
+                ts(H("brow"), A("FWn", 512 + hs, 640 + hs) if h or not OPT["brow"] else I(A("ID"), boh), MID, SUB)
+                at("v%d" % h)
+                act(A("KWn", 512 + hs, 640 + hs), I(KIN, boh))
+                ts(H("v16"), A("KWn", 512 + hs, 640 + hs), MID, SUB)
+                at("E2")
+                if h == 1:
                     mm(A("pn", 16, 256), A("TM", 0, 128), A("ones", 0, 240), True, False)
-                for c0 in range(0, 8 * h + 8, 4):
+                for c0 in range(8 * h, 8 * h + 8, 4):
+                    at("E%d" % (c0 // 4))
                     for c in range(c0, c0 + 4):
-                        a = max(16 * c, hs)
-                        ts(A("E", 256 * c + a, 256 * c + hs + 128), A("brow", a, hs + 128), A("bF", c, c + 1), EQ,
-                           A("w", 256 + c, 257 + c), MUL)
+                        ts(A("E", 272 * c, 256 * c + 256), A("brow", 16 * c, 256), A(pk, 288 + c % 8, 289 + c % 8),
+                           EQ, A("w", 256 + c, 257 + c), MUL)
                     merge(4)
-                    cs = [c for c in range(c0, c0 + 4) if 16 * c + 16 < hs + 128]
+                    cs = [c for c in range(c0, c0 + 4) if c < 15]
                     for c in cs:
-                        a = max(16 * c + 16, hs)
-                        mm(A("pn", a, hs + 128), A("Qa", 16, 144), A("E", 256 * c + a, 256 * c + hs + 128), False, c == 14)
+                        mm(A("pn", 16 * c + 16, 256), A("Qa", 16, 144), A("E", 272 * c + 16, 256 * c + 256), False, c == 7)
                     merge(len(cs))
-        tag[0] = "s"
+                at("may")
+                act(A("bF", 8 * h, 8 * h + 8), bP, bias=MID)
+        at("zn0")
         bo = A("bO", 16 * t, 16 * t + 16)
-        bi = A("bin", 16 * t, 16 * t + 16)
-        send(prv if last else nxt, [(bi, bo)], HOP)
+        bi = lambda h: A("bin", 16 * t + 8 * h, 16 * t + 8 * h + 8)
         bG = A("FWn", 512, 768)
-        act(A("xs"), I(A("X"), bo))
-        act(A("KWn", 256, 512), I(A("KN", 0, W_), bo))
-        mm(A("pd0", 0, 256), A("ones", 0, 128), A("cq"), True, False)
-        mm(A("pd0", 0, 256), A("Ih"), z(), False, False)
-        merge(2)
-        mm(A("pd0", 0, 256), A("Ih"), A("xs"), False, True)
-        zn = A("XWn", xw + 256, xw + 512)
-        ts(zn, A("pd0", 0, 256), 12582912.0, ADD, 12582912.0, SUB)
+        kb = A("KWn", 512, 768)
         if last:
-            dma("Y", ext("yz"), zn, 2600)
-        else:
-            send(nxt, [(A("zin", 256 * t + 256, 256 * t + 512), zn)], HOP + 400)
+            dma("Y", ext("yz"), A("XWn", xw + 512, xw + 768))
         if 0 < t < VIS - 1:
-            cp(I(A("TT"), A("oin", 16 * t, 16 * t + 16)), bG)
+            for h in (1, 0):
+                at("T%d" % h)
+                cp(I(A("kst"), A("oin", 16 * t + 8 * h, 16 * t + 8 * h + 8)), A("FWn", 512 + 128 * h, 640 + 128 * h))
         if not last:
-            ts(A("t16"), I(A("TT", 0, W_), bi), MID, SUB)
-            act(A("b0h"), I(A("TT", 0, W_), bi), bias=4096.0)
-            starts()
+            for h in (1, 0):
+                at("t%d" % h)
+                ts(A("t16", 128 * h, 128 * h + 128), I(A("kst", 0, W_), bi(h)), MID, SUB)
+                starts(h)
         if t == VIS - 2:
-            dma("Y", ext("tout"), A("TT", 0, W_, 1, row0), 4000)
-            send(prv, [(ext("tback"), ext("tout"))], 5000)
+            at("home")
+            dma("Y", A("trt"), A("kst", 0, W_, 1, row0), 4000)
+            cp(A("trf"), A("trt"))
+            send(prv, [(ext("tback"), A("trf"))], HOP + 2000)
             dma("Y", A("TT", 0, W_, 1, row0), ext("tback"), 4000)
+        at("may")
         act(wv(18), A("bF"), bias=-lo - 127.5, func=ACT.Abs)
-        ts(wv(19), wv(18), 128.0, GT, 512.0, MUL)
-        tt(wv(20), wv(19), live, MUL)
-        tt(wv(21), A("bF"), spK, SUB)
+        act(wv(19), wv(18), bias=-128.0, func=ACT.Sign)
+        tt(wv(20), wv(19), wv(14), MUL)
+        tt(A("q1", 32, 64, 2), A("bF"), spK, SUB)
+        if not last:
+            act(A("q1", 64, 96, 2), A("q1", 32, 64, 2))
+        at("colM")
+        act(A("colM"), kb, scale=m0)
+        at("cnt")
         act(A("HC", 16, 256), A("pn", 16, 256))
         for r in range(16):
             mm(A("pc", 0, 16), A("TM", 128 * r, 128 * r + 128), A("E", r, 16 * 272, 272), r == 0, False)
         merge(16)
         conv("pc", 0, "Qb", "HC", 256, start=False)
-        tag[0] = "t"
-        cnt, seat = A("pc", 0, 16), wv(23)
-        tt(seat, cnt, wv(20), LT)
-        ts(wv(26), seat, 256.0, MUL)
-        tt(wv(27), seat, wv(21), MUL)
+        cnt = A("pc", 0, 16)
+        at("seat")
+        n = 64 if last else 96
+        tt(A("q0", 1, 32, 2), cnt, wv(20), LT)
+        tt(A("q0", 33, 64, 2), cnt, wv(20), LT)
+        if not last:
+            ts(A("q0", 65, 96, 2), cnt, 0.5, LT)
+        merge(n // 32)
+        scan(A("q2", 0, n), A("q0", 0, n), A("q1", 0, n), MUL, ADD)
+        cp(A("sl", 64 * t, 64 * t + n // 2), A("q2", 1, n, 2))
+        at("vl")
+        conv("pw", 0, "Qh", "v16", 256)
+        ts(uv(5), A("pw", 0, 16), MID - FO, ADD, 0.0, MAX)
+        tt(wv(17), A("pw", 0, 16), A("cw", 80, 96), SUB)
         merge(2)
-        tt(wv(28, 32), wv(26, 32), A("cw", 0, 32), ADD)
-        cp(uv(6, 32), wv(28, 32))
+        tt(A("q1", 96, 128, 2), wv(17), A("q0", 1, 32, 2), MUL)
+        at("hit")
+        tt(A("HC", 256, 512), I(FEET, uv(5)), bG, EQ)
+        conv("pc", 0, "Qb", "HC", 256, a=256)
+        at("seat2")
+        cp(A("q0", 97, 128, 2), A("pc", 0, 16))
+        scan(A("q2", 96, 128), A("q0", 96, 128), A("q1", 96, 128), MUL, ADD)
+        cp(A("sl", 64 * t + 48, 64 * t + 64), A("q2", 97, 128, 2))
+        sl = lambda j, t=t: A("sl", 64 * t + 16 * j, 64 * t + 16 * j + 16)
+        at("KN")
         if last:
-            act(A("KS"), I(A("KWn"), uv(6)))
-            act(A("XS"), I(A("XWn", xw, xw + 512), uv(6)))
+            act(A("KS"), I(A("KWn"), sl(0)))
+            act(A("XS"), I(A("XWn", xw, xw + 768), sl(0)))
             dma("Y", ext("yk", 256 * r_, 256 * r_ + 256), A("KS"), 3000)
             dma("Y", ext("yx", 256 * r_, 256 * r_ + 256), A("XS"), 3000)
         else:
-            ts(wv(25), cnt, 0.5, LT)
-            act(A("KN", lo, lo + 256), I(A("KWn"), uv(6)))
-            act(A("XC", lo, lo + 256), I(A("XWn", xw, xw + 512), uv(6)))
+            act(A("KN", lo, lo + 256), I(A("KWn"), sl(0)))
+            at("XC")
+            (cp if OPT["xc"] else act)(A("XC", lo, lo + 256), I(A("XWn", xw, xw + 768), sl(0)))
+            dma("Y", A("X", lo, lo + 256), A("XC", lo, lo + 256))
             early_kin(t + 1)
-            dma("Y", A("X", lo, lo + 256), A("XC", lo, lo + 256), 2600)
-        tag[0] = "u"
-        act(A("colM"), A("KWn", 256, 512), scale=m0)
-        tt(I(A("KN"), uv(7)), A("colM"), A("nrow", 256 * r_, 256 * r_ + 256), ADD)
-        ts(A("v16"), A("KWn", 256, 512), MID, SUB)
-        conv("pk0", 0, "Qh", "v16", 256)
-        ts(uv(5), A("pk0", 0, 16), MID - FO, ADD, 0.0, MAX)
-        tt(wv(17), A("pk0", 0, 16), A("cw", 80, 96), SUB)
-        merge(2)
-        tt(A("HH"), I(A("FT"), uv(5)), bG, EQ)
-        conv("pk0", 0, "Qb", "HH", 256)
-        tt(wv(24), A("pk0", 0, 16), wv(17), MUL)
-        tt(wv(30), wv(26), wv(15), ADD)
-        tt(wv(22), wv(24), seat, MUL)
-        tt(wv(31), wv(22), spF, ADD)
-        cp(uv(8), wv(30))
-        act(A("FT", fl, fl + 256), I(A("FWn"), uv(8)))
-        cp(uv(9), wv(31))
-        cp(I(A("FT"), uv(9)), nG)
+        at("par")
+        tt(I(KINS, sl(1)), A("colM"), A("nrow", 256 * r_, 256 * r_ + 256), ADD)
+        at("FT")
+        act(A("KN", fl, fl + 256), I(A("FWn"), sl(0)))
+        at("foot")
+        cp(I(FEET, sl(3)), nG)
+        at("Aout")
         if not last:
-            act(wv(1), seat, scale=-256.0, accum=A("acc", 1, 2))
-            mm(A("pd1", 0, 1), A("onef"), A("acc", 0, 1), True, False)
-            mm(A("pd1", 0, 1), A("onef"), A("acc", 1, 2), False, True)
+            mm(A("pw", 32, 48), A("ones", 0, 128), live, True, False)
+            mm(A("pw", 32, 48), A("onef"), A("q0", 1, 32, 2), False, True)
             merge(2)
-            act(A("aout", 8 * t, 8 * t + 1), A("pd1", 0, 1), scale=1.0 / 256, bias=-15.5)
-            tt(wv(19), wv(25), wv(21), MUL)
-            tt(wv(18), wv(19), spK, ADD)
-            ot = A("oT", 16 * t, 16 * t + 16)
-            cp(ot, wv(18))
+            act(wv(21), A("pw", 32, 48), bias=-15.5 / 16, accum=A("aout", 8 * t, 8 * t + 1))
             pa = (A("ain", 8 * t + 8, 8 * t + 16), A("aout", 8 * t, 8 * t + 8))
-            send(nxt, [pa] if t == VIS - 2 else [pa, (A("oin", 16 * t + 16, 16 * t + 32), ot)], HOP)
+            send(nxt, [pa] if t == VIS - 2 else [pa, (A("oin", 16 * t + 16, 16 * t + 32), sl(2))], HOP)
         else:
-            act(A("bb"), I(A("ID"), bi))
-            cp(I(A("TT"), A("oT", 16 * t - 16, 16 * t)), A("bb"))
+            for h in (1, 0):
+                at("t%d" % h)
+                bb, a = A("bb", 128 * h, 128 * h + 128), 64 * t - 32 + 8 * h
+                act(bb, I(A("ID"), bi(h)))
+                cp(I(A("TT"), A("sl", a, a + 8)), bb)
             dma("Y", ext("yt"), A("TT", 0, W_, 1, row0), 3000)
             dma("S", ext("yp"), A("KN", 0, B_, 1, row0), 3000)
             for j in range(N):
                 if j != r_:
                     dma("S", ext("yk", 256 * j, 256 * j + 256, slice(*row0)),
-                        A("KN", B_ + 256 * j, B_ + 256 * j + 256, 1, row0), 2600)
-            dma("Y", ext("yf"), A("FT", 8, DF, 1, row0), 2600)
+                        A("KN", B_ + 256 * j, B_ + 256 * j + 256, 1, row0))
+            dma("Y", ext("yf"), A("KN", FB + B_, FB + W_, 1, row0))
     return ops
 
 
@@ -639,23 +759,26 @@ def plan(ops):
         if o["k"] == "r":
             dep = {o["x"][2]: False}
         o["dep"] = dep
+    return arrange(ops)
+
+
+def arrange(ops):
+    n = len(ops)
     dur = [0.0 if o["k"] == "r" else 60.0 if o["k"] == "d" else o["c"] for o in ops]
     before = [[(j, ops[j]["c"] + (SW if ops[j]["e"] == o["e"] else XW) if w else dur[j]) for j, w in o["dep"].items()]
               for o in ops]
 
-    def run(boost):
-        level = [0.0] * n
-        floor = [0.0] * n
-        for i in range(n - 1, -1, -1):
-            level[i] = max(level[i] + ops[i]["c"] + boost.get(ops[i]["t"], 0) + boost.get(ops[i]["u"], 0), floor[i])
-            for j, l in before[i]:
-                level[j] = max(level[j], level[i] + l - ops[j]["c"])
-                floor[j] = max(floor[j], level[i] + 0.01)
+    after = [[] for _ in ops]
+    for i in range(n):
+        for j, l in before[i]:
+            after[j].append((i, l + dur[i] - dur[j]))
+
+    def place(order, edges, first):
         busy = {}
         at = [0.0] * n
-        for i in sorted(range(n), key=lambda i: (-level[i], i)):
-            s = 0.0
-            for j, l in before[i]:
+        for i in order:
+            s = first[i]
+            for j, l in edges[i]:
                 if at[j] + l > s:
                     s = at[j] + l
             d = dur[i]
@@ -675,7 +798,23 @@ def plan(ops):
             at[i] = s
         return at
 
-    return run(BOOST), run
+    level = [0.0] * n
+    floor = [0.0] * n
+    for i in range(n - 1, -1, -1):
+        level[i] = max(level[i] + ops[i]["c"] + BOOST.get(ops[i]["e"] + ops[i]["b"], 0), floor[i])
+        for j, l in before[i]:
+            level[j] = max(level[j], level[i] + l - ops[j]["c"])
+            floor[j] = max(floor[j], level[i] + 0.01)
+    tail = [ops[i]["c"] - dur[i] for i in range(n)]
+    at = place(sorted(range(n), key=lambda i: (-level[i], i)), before, [0.0] * n)
+    best, end = at, max(at[i] + ops[i]["c"] for i in range(n))
+    for _ in range(PASSES):
+        back = place(sorted(range(n), key=lambda i: (-at[i] - dur[i], -i)), after, tail)
+        at = place(sorted(range(n), key=lambda i: (-back[i] - dur[i], i)), before, [0.0] * n)
+        e = max(at[i] + ops[i]["c"] for i in range(n))
+        if e < end:
+            best, end = at, e
+    return best, end
 
 
 def emit(g, T, ops, start):

@@ -8,23 +8,24 @@ FW, FO, DF = 1296, 2552, 1032
 FB = F0 - FO
 MID = 1792.0
 WT = 2176.0
-SPLIT = [[(0, 3, 0), (16, 2, 1)], [(32, 0, 0), (16, 2, 0)]]
-SPLIT0 = [[(64, 1, 1), (32, 1, 0)], [(32, 0, 0), (0, 2, 1)]]
-CUTS = (64, 128)
-OPT = {"brow": 1, "q": 32, "xc": 0, "e0": 0}
-BOOST = {'Vseat': -3500, 'PB01': 2000, 'Sgt00': 2500, 'Vmp00': 500, 'Vt0': 1200, 'Vkin00': -1000, 'VE3': 500, 'Pneg01': 4000, 'SC00': 200, 'Vmb11': 300, 'PAout': 8000, 'GAout': 6000, 'Gdec11': 2500, 'Gdec10': 3000, 'SA01': -2000, 'Pdec11': 500, 'Vturn': -500, 'YKN': 700, 'Vt1': -500, 'Pvl': -500, 'Vgv11': -500, 'Vparts01': -2000, 'Sfar': 4000, 'SXC': 1000, 'Vparts11': 500, 'PE1': -500}
+SPLIT = [[(0, 2, 0), (16, 2, 0)], [(32, 0, 0), (16, 2, 0)]]
+SPLIT0 = [[(48, 1, 0), (32, 1, 0)], [(32, 0, 0), (16, 2, 0)]]
+CUTS = (128,)
+OPT = {"brow": 1, "xc": 1, "e0": 0, "es": 0, "cm": 0, "ft": 0, "zs": 0}
+SCALAR = "v0 v1 t0 t1 hit brow1"
+BOOST = {}
 PASSES = 1
 
 SB, F32, BF, F16, I32, U16 = "sbuf", "float32", "bfloat16", "float16", "int32", "uint16"
 SCRATCH = {}
-for _d, _l in ((I32, "kst 3856 fst 1280 trs 224 trt 224 ci 8"),
+for _d, _l in ((I32, "kst 3856 fst 1280 trs 224 trt 224 ci 8 R 544 Di 32"),
                (F32, "KN 5152 ID 3584 TT 3856 trf 224 onef 128 tmpc 256 cf 32 cw 96 c17 16 d0 272 "
-                     "ain 40 aout 40 acc 8 b0 256 bF 16 R 544 Aq 32 colY 256 urow 256 nrow 1024 colM 256 KS 256 "
-                     "FWn 768 KWn 768 bb 256 w 512 q0 128 q1 128 q2 128 o0 64 o1 64 o2 64"),
+                     "ain 40 aout 40 acc 8 b0 256 colY 256 urow 256 nrow 1024 colM 256 KS 256 "
+                     "FWn 768 KWn 768 bb 256 Pf 256 w 512 q0 128 q1 128 q2 128 o0 64 o1 64 o2 64"),
                (BF, "X 3584 XC 3584 ones 272 Ib 128 Ih 128 In 128 I8 128 Pm 128 Qb 144 Qa 144 TM 2048 BD 48 CK 544 PH 272 "
                     "PH0 272 SH 16 RE 64 cq 256 tmpb 272 zin 1280 zp 256 b0h 256 chi 256 x0b 2048 x1b 2048 m0b 2048 m1b 2048 "
-                    "xb 256 mb 256 xs 256 D 32 Z 1152 HC 512 E 4352 XS 256 XWn 3840 phi 256 xp 256 mp 256 lv 16 c64 16 ZR 1904"),
-               (F16, "Qh 144 If 128 SF 8 PF 136 PF0 136 g16 512 e16 512 v16 256 t16 256 p16 256 c16 256 nW 128 brow 256"),
+                    "xb 256 mb 256 xs 256 D 32 Z 1152 HC 512 E 4352 XS 256 XWn 3840 phi 256 xp 256 mp 256 lv 16 c64 24 ZR 1904 zr 2048"),
+               (F16, "Qh 144 If 128 SF 8 PF 136 PF0 136 g16 512 e16 512 v16 256 t16 256 p16 256 c16 256 nW 144 brow 256"),
                (U16, "cu 32 bin 80 oin 80 bU 32 bO 80 cU 256 u 256 sl 320")):
     _l = _l.split()
     for _n, _c in zip(_l[::2], _l[1::2]):
@@ -36,6 +37,10 @@ for _n in ("pk0", "pk1", "pz0", "pz1", "pd", "pw", "pc", "pn"):
 SEMAPHORES = ["eV", "eS", "eP", "eG", "sent"] + ["d%d" % i for i in range(80)] + ["r%d" % i for i in range(36)]
 
 GA, SC, PE, HOP, XW, SW, FIX, DL = 1.56, 3.8, 0.55, 4000, 130, 80, 25, 2600
+CASES = [(1.56, 3.8, 0.55, 20, 3000, 2600, 140, 80, 80), (2.0, 5.5, 0.5, 10, 2600, 2000, 110, 60, 60),
+         (1.3, 3.0, 0.65, 35, 7000, 4000, 200, 100, 200), (1.1, 1.8, 0.5, 20, 3500, 2600, 320, 160, 80)]
+ROUNDS, SLACK, SEED, PLAN = 60000, 1000, 3, []
+MEAN, ANY, NEAR = 1.0, 30, 1000
 
 
 def build(T, topo, core, rank):
@@ -55,7 +60,9 @@ def build(T, topo, core, rank):
         return (win[0].indirect(off[0]), win[1] + off[1], off[2] * 16, win[3], "ind", off[1])
 
     def add(eng, fn, r, w, cost, kind="c", extra=None):
-        ops.append({"e": eng, "f": [fn], "r": r, "w": w, "c": float(cost), "k": kind, "x": extra,
+        cv = list(cost) + [0] * (7 - len(cost))
+        cost = sum(a * b for a, b in zip(cv, (1, GA, SC, PE, FIX, HOP, DL)))
+        ops.append({"e": eng, "f": [fn], "r": r, "w": w, "c": float(cost), "cv": cv, "k": kind, "x": extra,
                     "t": eng + (w[0][0] if w else "") + "." + tag[0], "b": tag[0], "v": tag[1]})
         return len(ops) - 1
 
@@ -70,7 +77,9 @@ def build(T, topo, core, rank):
             o["f"] = o["f"] + p["f"]
             o["r"] = o["r"] + [x for x in p["r"] if x not in o["r"]]
             o["w"] = o["w"] + [x for x in p["w"] if x not in o["w"]]
-            o["c"] += p["c"]
+            more = [100] + [0] * 6 if o["k"] == "d" else p["cv"]
+            o["c"] += 100 if o["k"] == "d" else p["c"]
+            o["cv"] = [a + b for a, b in zip(o["cv"], more)]
         del ops[len(ops) - n + 1:]
 
     chains = {}
@@ -91,15 +100,15 @@ def build(T, topo, core, rank):
 
     def vcost(out, in0, in1=None):
         if out[4] == "ind":
-            return 60 + SC * out[2]
+            return (60, 0, out[2])
         if in0[4] == "ind":
-            return 60 + GA * out[2]
+            return (60, out[2])
         n = out[2]
         if in1 is not None:
             n = n * (2 if in0[4] == SB and in1[4] == SB else 1)
         elif out[3] not in (F32, I32) and in0[3] not in (F32, I32):
             n = n / 2
-        return max(64, n) + FIX
+        return (max(64, n), 0, 0, 0, 1)
 
     def sv(s):
         return s[0] if isinstance(s, tuple) else s
@@ -121,11 +130,11 @@ def build(T, topo, core, rank):
         add("V", f, r, w, vcost(out, in0))
 
     def ms(out, val):
-        add("V", lambda q: q.memset(out[0], val), [], out[1], max(64, out[2] * (1 if out[3] in (F32, I32) else 0.5)))
+        add("V", lambda q: q.memset(out[0], val), [], out[1], (max(64, out[2] * (1 if out[3] in (F32, I32) else 0.5)),))
 
     def scan(out, a, b, op0, op1):
         r, w = rw(out, [a, b])
-        add("V", lambda q: q.tensor_tensor_scan(out[0], a[0], b[0], 0.0, op0, op1), r, w, max(64, out[2]) + FIX)
+        add("V", lambda q: q.tensor_tensor_scan(out[0], a[0], b[0], 0.0, op0, op1), r, w, (max(64, out[2]), 0, 0, 0, 1))
 
     def act(out, in_, bias=0.0, scale=1.0, func=None, accum=None):
         r, w = rw(out, [in_, bias, scale])
@@ -135,10 +144,10 @@ def build(T, topo, core, rank):
         else:
             w = w + accum[1]
             f = lambda q: q.activation(out[0], in_[0], fu, bias=sv(bias), scale=sv(scale), accum_out=accum[0])
-        add("S", f, r, w, 80 + GA * out[2] if in_[4] == "ind" else max(64, out[2]) + 30 + FIX)
+        add("S", f, r, w, (80, out[2]) if in_[4] == "ind" else (max(64, out[2]) + 30, 0, 0, 0, 1))
 
     def mm(out, lhsT, rhs, start, stop):
-        c = max(min(64, lhsT[2]), rhs[2]) * (4 if lhsT[3] == F32 else 1) * PE
+        c = (0, 0, 0, max(min(64, lhsT[2]), rhs[2]) * (4 if lhsT[3] == F32 else 1))
         add("P", lambda q: q.matmul(out[0], lhsT[0], rhs[0], start, stop), lhsT[1] + rhs[1], out[1], c)
 
     def iota(out, pat, base, cm):
@@ -146,13 +155,13 @@ def build(T, topo, core, rank):
             f = lambda q: q.iota(out[0], pat, base, cm)
         else:
             f = lambda q: q.iota(out[0], pat, base, cm, allow_small_or_imprecise_dtypes=True)
-        add("G", f, [], out[1], 160 + 2 * out[2])
+        add("G", f, [], out[1], (160 + 2 * out[2],))
 
     def asel(out, in_, pat, base, cm):
-        add("G", lambda q: q.affine_select(out[0], in_[0], pat, ALU.is_equal, 0.0, base, cm), in_[1], out[1], 200 + 2 * out[2])
+        add("G", lambda q: q.affine_select(out[0], in_[0], pat, ALU.is_equal, 0.0, base, cm), in_[1], out[1], (200 + 2 * out[2],))
 
-    def dma(eng, out, in_, cost=DL):
-        add(eng, lambda q: q.dma_start(out[0], in_[0]), in_[1], out[1], cost, "d")
+    def dma(eng, out, in_, cost=2600):
+        add(eng, lambda q: q.dma_start(out[0], in_[0]), in_[1], out[1], (cost - 2600, 0, 0, 0, 0, 0, 1), "d")
 
     def ext(name, a=None, b=None, rows=slice(None)):
         if a is None:
@@ -182,9 +191,9 @@ def build(T, topo, core, rank):
                     tr.append(RemoteDMATransfer(dst_ids=[DstId(rid=rid, pnc=pid)], dma_engine_mask=m,
                                                 remote_sem=T.sem[sems[j]], src=i[0], dst=o[0]))
                 return q.remote_dma_fused(tr, local_sem=T.sem.sent)
-        s = add("G", f, r, [], 150, "s", k * len(pairs))
+        s = add("G", f, r, [], (0, 0, 0, 0, 0, 0.12), "s", k * len(pairs))
         for j, (o, i) in enumerate(pairs):
-            add("R", None, [], o[1], cost, "r", (sems[j], k, s))
+            add("R", None, [], o[1], (cost - HOP, 0, 0, 0, 0, 1), "r", (sems[j], k, s))
 
     EQ, LT, GT, MUL, ADD, SUB, MAX, MIN = (ALU.is_equal, ALU.is_lt, ALU.is_gt, ALU.mult, ALU.add, ALU.subtract, ALU.max, ALU.min)
     row0 = (0, 128, 16)
@@ -210,7 +219,7 @@ def build(T, topo, core, rank):
     chain("load")
     dma("Y", A("X"), ext("x0"), 17000)
     chain("load")
-    send(nxt, [(ext("tin"), A("trs"))], 6000)
+    send(nxt, [(ext("tin"), A("trs"))], HOP + 4000)
     ms(A("KN", W_, F0 + 8), -1.0)
     fill(A("KN", FB + W_, F0 + FW), -1.0)
     dma("Y", A("kst", 0, W_, 1, row0), ext("tin"), 4000)
@@ -245,6 +254,8 @@ def build(T, topo, core, rank):
     ts(A("cf", 14, 15), cR, 8.0, MUL, cG, ADD)
     iota(A("tmpc", 0, 128), [[1, 128]], 0, 0)
     ts(A("Pm"), A("tmpc", 0, 128), A("cf", 14, 15), EQ)
+    act(A("Pf", 0, 128), A("Pm"), scale=WT)
+    act(A("Pf", 128, 256), A("Pm"), scale=-1.0)
     iota(A("tmpc", 160, 192), [[0, 2], [16, 16]], 0, 0)
     iW, spK, spM = A("cw", 0, 16), A("cw", 32, 48), A("cw", 64, 96)
     ts(A("cw", 0, 32), A("tmpc", 160, 192), cR, ADD)
@@ -253,6 +264,7 @@ def build(T, topo, core, rank):
     act(A("cw", 80, 96), iW, bias=DF + FO - MID)
     for j in range(N):
         ts(A("nW", 32 * j, 32 * j + 32), A("cw", 0, 32), -1.0, MUL, MID - B_ - L_ * j, ADD)
+    merge(N)
     for name in ("o0", "q0"):
         fill(A(name), 0.0)
     act(A("o1", 1, 32, 2), iW, bias=float(DK))
@@ -261,7 +273,8 @@ def build(T, topo, core, rank):
     act(A("q1", 33, 96, 2), A("cw", 0, 32), bias=float(DK))
     act(A("q1", 97, 128, 2), iW, bias=float(DF))
     fill(A("c17"), WT)
-    fill(A("c64"), 64.0)
+    fill(A("c64", 0, 16), 64.0)
+    fill(A("c64", 16, 24), -(MID + 32) / 128)
     iota(A("tmpc", 192, 208), [[0, 2], [1, 8]], 0, 0)
     two, neg, one = A("BD", 0, 16), A("BD", 16, 32), A("BD", 32, 48)
     for o, v in ((two, 2 * WT), (neg, -WT), (one, WT)):
@@ -277,11 +290,12 @@ def build(T, topo, core, rank):
     act(A("SH", 0, 8), A("cq", 0, 8), scale=1.0 / 32)
     act(A("SH", 8, 16), A("cq", 0, 8), scale=-1.0)
     cp(A("SF"), A("cq", 0, 8))
-    iota(A("CK"), [[0, 32], [4, 17]], 0, 0)
-    ms(A("CK", 0, 544, 1, (0, 32)), -1179648.0 / 32)
+    iota(A("CK"), [[0, 32], [4, 17]], -32, 0)
+    ms(A("CK", 0, 544, 1, (0, 32)), -16 * WT)
+    ms(A("CK", 272, 544, 17, (0, 32)), 0.0)
     for s in range(2):
-        ms(A("CK", 272 * s, 272 * s + 136, 1, (64, 128)), -184.0 / 64)
-        ms(A("CK", 272 * s + 136, 272 * s + 272, 1, (64, 128)), (4096.0 + MID) / 64)
+        ms(A("CK", 272 * s, 272 * s + 136, 1, (64, 128)), -128.0 / 64)
+        ms(A("CK", 272 * s + 136, 272 * s + 272, 1, (64, 128)), (4096.0 + MID + 32) / 64)
     ms(A("CK", 272, 544, 17, (64, 128)), 0.0)
     fill(A("d0"), 0.0)
     fill(A("d0", 0, 272, 17), 67108864.0)
@@ -305,14 +319,17 @@ def build(T, topo, core, rank):
     fill(A("FWn", 256, 512), float(W_))
     fill(A("aout"), 0.0)
     fill(A("urow"), 0.0)
-    act(A("nrow"), A("ID", B_, W_), scale=m1)
+    if not OPT["cm"]:
+        act(A("nrow"), A("ID", B_, W_), scale=m1)
     for a in range(0, B_, 640):
         iota(A("ID", a, a + 640), [[1, 640]], a, 0)
 
     zr = {}
-    for split in SPLIT0 + SPLIT:
+    for s, split in enumerate(SPLIT0 + SPLIT):
         for nv, ks, own in split:
-            if (ks, own) not in zr and 1 < ks + own < 5:
+            own *= 1 - s % 2
+            ks = 4 if nv == 128 else ks
+            if (ks, own) not in zr and 1 < ks + own:
                 a = 272 * len(zr)
                 zr[ks, own] = A("ZR", a, a + 272)
                 mm(A("pd", 0, 272), A("TM", 0, 128), A("ones"), True, False)
@@ -322,24 +339,35 @@ def build(T, topo, core, rank):
                 merge(1 + len(cols))
                 act(zr[ks, own], A("pd", 0, 272))
 
-    def conv(bank, c0, Q, name, n, start=True, a=0):
+    def conv(bank, c0, Q, name, n, start=True, a=0, stop=True):
         for r in range(16):
-            mm(A(bank, c0, c0 + n // 16), A(Q, 16 - r, 144 - r), A(name, a + r, a + n, 16), start and r == 0, r == 15)
+            mm(A(bank, c0, c0 + n // 16), A(Q, 16 - r, 144 - r), A(name, a + r, a + n, 16), start and r == 0, stop and r == 15)
         merge(16)
 
-    def kin(h, bu):
-        cp(A("cU", 128 * h, 128 * h + 128), I(KIN, bu))
+    def less(name, out, in_, by=MID):
+        if name in SCALAR.split():
+            act(out, in_, bias=-by)
+        else:
+            ts(out, in_, by, SUB)
 
-    def parts(a, b):
-        ts(A("c16", a, b), A("cU", a, b), MID, SUB)
-        ts(A("chi", a, b), A("cU", a, b), 4096.0, ADD)
-        merge(2)
+    def kin(s, h):
+        a, b, bu = 128 * h, 128 * h + 128, A("bU", 16 * s + 8 * h, 16 * s + 8 * h + 8)
+        at("kin%d%d" % (s, h))
+        if "kin%d%d" % (s, h) in SCALAR.split():
+            act(A("c16", a, b), I(KIN, bu), bias=-MID)
+            ts(A("cU", a, b), A("c16", a, b), MID, ADD)
+            at("parts%d%d" % (s, h))
+        else:
+            cp(A("cU", a, b), I(KIN, bu))
+            at("parts%d%d" % (s, h))
+            ts(A("c16", a, b), A("cU", a, b), MID, SUB)
+        less("chi%d%d" % (s, h), A("chi", a, b), A("c16", a, b), -MID - 4096.0)
 
     def starts(h):
         pz = "pk%d" % h
         conv(pz, 0, "Qh", "t16", 128, a=128 * h)
         ts(A("bU", 8 * h, 8 * h + 8), A(pz, 0, 8), MID, ADD)
-        ts(A("b0h", 128 * h, 128 * h + 128), A("t16", 128 * h, 128 * h + 128), MID + 4096.0, ADD)
+        less("b0h", A("b0h", 128 * h, 128 * h + 128), A("t16", 128 * h, 128 * h + 128), -MID - 4096.0)
 
     def early_kin(t):
         lo = B_ + L_ * ((rank - t) % N)
@@ -353,10 +381,7 @@ def build(T, topo, core, rank):
             first_kin(1)
 
     def first_kin(h):
-        at("kin0%d" % h)
-        kin(h, A("bU", 8 * h, 8 * h + 8))
-        at("parts0%d" % h)
-        parts(128 * h, 128 * h + 128)
+        kin(0, h)
 
     ts(A("t16"), A("b0"), MID, SUB)
     for h in (1, 0):
@@ -375,6 +400,7 @@ def build(T, topo, core, rank):
         nG = A("ID", lo, lo + 256)
         z = lambda a=0, b=256: A("zin", 256 * t + a, 256 * t + b)
         xw = 768 * t
+        others = [(r_ + d) % N for d in range(1, N)]
         at("yu", t)
         early = t > 0 or OPT["e0"]
         if early:
@@ -386,13 +412,13 @@ def build(T, topo, core, rank):
         else:
             act(A("urow"), A("KN", lo, lo + 256), scale=m1)
             act(A("FWn", 0, 256), A("KN", fl, fl + 256))
-        ts(A("g16", 256, 512), A("KN", lo, lo + 256), MID, SUB)
-        ts(A("g16", 0, 256), A("KN", fl, fl + 256), MID, SUB)
+        less("gu", A("g16", 256, 512), A("KN", lo, lo + 256))
+        less("gy", A("g16", 0, 256), A("KN", fl, fl + 256))
         conv("pc", 0, "Qh", "g16", 512)
         ts(uv(0), A("pc", 0, 16), MID, ADD)
         ts(uv(1), A("pc", 16, 32), MID + FB, ADD, float(F0), MAX)
+        merge(2)
         tt(A("o1", 0, 64, 2), A("pc", 0, 32), spM, SUB)
-        merge(3)
         at("own")
         act(wv(0, 32), A("pc", 0, 32), bias=MID - lo - 127.5, func=ACT.Abs)
         at("live")
@@ -400,27 +426,41 @@ def build(T, topo, core, rank):
         live = A("lv")
         ts(live, wv(4), 128.0, GT)
         at("e16")
-        ts(A("e16"), I(A("KN"), uv(0, 32)), MID, SUB)
+        ne = 16 if OPT["es"] == 1 else 32
+        if OPT["es"]:
+            less("py", A("e16", 0, 256), I(KINS, uv(0)))
+            at("fu")
+            less("fu", A("e16", 256, 512), I(A("KN"), uv(1)))
+        else:
+            less("py", A("e16"), I(A("KN"), uv(0, 32)))
         at("colY")
         act(A("colY"), I(KINS, uv(0)), scale=m0)
         for j in range(2):
             dma("Y", A("XWn", xw + 256 * j, xw + 256 * j + 256), A("X", lo, lo + 256))
         at("held")
-        mm(A("pc", 0, 32), A("If"), A("nW", 32 * r_, 32 * r_ + 32), True, False)
-        mm(A("pc", 0, 16), A("ones", 0, 128), A("c64"), False, False)
-        mm(A("pc", 0, 16), A("I8"), live, False, False)
+        conv("pc", 0, "Qh", "e16", 16 * ne, stop=False)
+        mm(A("pc", 0, ne), A("If"), A("nW", 32 * r_, 32 * r_ + ne), False, False)
+        mm(A("pc", 0, 16), A("ones", 0, 128), A("c64", 0, 16), False, False)
+        mm(A("pc", 0, 16), A("I8"), live, False, True)
         merge(3)
-        conv("pc", 0, "Qh", "e16", 512, start=False)
-        ts(A("o0", 1, 64, 2), A("pc", 0, 32), 0.0, EQ)
-        tt(A("o0", 33, 64, 2), A("o0", 33, 64, 2), A("o0", 1, 32, 2), MUL)
-        scan(A("o2"), A("o0"), A("o1"), MUL, ADD)
-        cp(uv(2, 32), A("o2", 1, 64, 2))
+        ts(A("o0", 1, 2 * ne, 2), A("pc", 0, ne), 0.0, EQ)
+        scan(A("o2", 0, 32), A("o0", 0, 32), A("o1", 0, 32), MUL, ADD)
+        cp(uv(2), A("o2", 1, 32, 2))
         tt(I(KINS, uv(2)), A("colY"), A("urow"), ADD)
+        at("turn0")
+        if OPT["es"] == 1:
+            conv("pc", 0, "Qh", "e16", 256, a=256, stop=False)
+            mm(A("pc", 0, 16), A("If"), A("nW", 32 * r_, 32 * r_ + 16), False, True)
+            merge(2)
+            ts(A("o0", 33, 64, 2), A("pc", 0, 16), 0.0, EQ)
+        tt(A("o0", 33, 64, 2), A("o0", 33, 64, 2), A("o0", 1, 32, 2), MUL)
+        scan(A("o2", 32, 64), A("o0", 32, 64), A("o1", 32, 64), MUL, ADD)
+        cp(uv(3), A("o2", 33, 64, 2))
         if early:
             at("p16")
-            ts(A("p16"), I(KIN, A("bU", 0, 16)), MID, SUB)
+            less("p16", A("p16"), I(KIN, A("bU", 0, 16)))
             at("phi")
-            ts(A("phi"), A("p16"), MID + 4096.0, ADD)
+            less("phi", A("phi"), A("p16"), -MID - 4096.0)
         else:
             first_kin(1)
             first_kin(0)
@@ -428,23 +468,23 @@ def build(T, topo, core, rank):
         for j in range(2):
             dma("Y", A("KWn", 256 * j, 256 * j + 256), A("KN", lo, lo + 256))
         at("turn")
-        cp(I(FEET, uv(3)), A("FWn", 0, 256))
+        for h in range(2):
+            cp(I(FEET, A("u", 48 + 8 * h, 56 + 8 * h)), A("FWn", 128 * h, 128 * h + 128))
         at("wts")
         act(wv(14), live, scale=256.0)
         tt(A("q1", 1, 32, 2), wv(14), iW, ADD)
         act(wv(16), live, scale=255.0, bias=1.0)
         if last:
-            for j in range(N):
-                if j != r_:
-                    a = B_ + 256 * j
-                    dma("Y", ext("yk", 256 * j, 256 * j + 256), A("KN", a, a + 256), 3000)
-                    dma("Y", ext("yx", 256 * j, 256 * j + 256), A("X", a, a + 256), 3000)
+            for j in others:
+                a = B_ + 256 * j
+                dma("Y", ext("yk", 256 * j, 256 * j + 256), A("KN", a, a + 256), 3000)
+                dma("Y", ext("yx", 256 * j, 256 * j + 256), A("X", a, a + 256), 3000)
         at("Ain")
         if t > 0:
             a0 = A("ain", 8 * t, 8 * t + 1)
             ts(A("acc", 2, 3), a0, 402653184.0, ADD, 402653184.0, SUB)
-            ts(A("acc", 3, 4), a0, A("acc", 2, 3), SUB, 15.5, ADD)
-            act(A("d0", 1, 272, 17), A("c17"), scale=A("acc", 3, 4))
+            act(A("acc", 3, 4), A("acc", 2, 3), scale=-1.0, bias=a0)
+            act(A("d0", 1, 272, 17), A("c17"), scale=A("acc", 3, 4), bias=15.5 * WT)
         for h in (1, 0):
             at("zp%d" % h)
             for c in range(8):
@@ -455,9 +495,8 @@ def build(T, topo, core, rank):
             at("p16")
             conv("pw", 48, "Qh", "p16", 256)
             ts(uv(10), A("pw", 48, 64), MID, ADD)
-            for h in (1, 0):
-                at("xp%d" % h)
-                act(A("xp", 128 * h, 128 * h + 128), I(A("XC"), A("u", 160 + 8 * h, 168 + 8 * h)))
+            at("xp")
+            act(A("xp"), I(A("XC"), uv(10)))
         at("xb0")
         if t:
             act(A("xb"), I(A("X"), A("bU", 0, 16)))
@@ -472,21 +511,35 @@ def build(T, topo, core, rank):
                 zP = A(pz, 0, 512, 4)
                 bu = A("bU", 16 * s + 8 * h, 16 * s + 8 * h + 8)
                 nv, ks, own = (SPLIT if t else SPLIT0)[s][1 - h]
+                fused = nv == 128
+                if fused:
+                    on("zr")
+                    for k in range(16):
+                        asel(A("zr", k, 2048, 16), zz, [[0, 128]], 0, 0)
+                        if k % 2:
+                            merge(2)
                 if s == 1:
-                    on("kin")
-                    kin(h, bu)
-                    on("parts")
-                    parts(hs, hs + 128)
-                    on("xb")
-                    act(H("xb"), I(A("X"), bu))
+                    kin(1, h)
+                    own = 0
+                if s == 1 and h == 1:
+                    at("stay")
+                    cp(A("D"), A("Di"))
+                    ts(wv(30, 32), A("R", 16, 544, 17), 56.0, SUB, 1.0 / WT, MUL)
+                    act(wv(22, 32), wv(30, 32), bias=12582912.0)
+                    act(wv(24, 32), wv(22, 32), bias=-12582912.0)
+                    tt(wv(26, 32), A("R", 16, 544, 17), A("R", 0, 544, 17), SUB)
+                    ts(wv(28, 32), wv(26, 32), A("d0", 1, 2), ALU.is_ge, A("d0", 1, 2), MUL)
                 on("z")
-                nz = 4 if ks < 4 else 1 - own
+                nz = 4 if ks < 4 and not fused else 1 - own if s == 0 else 0
                 for j in range(nz):
                     mm(A(pz, j, 512, 4), A("Ib"), zz, True, True)
                 if nz:
                     merge(nz)
                 on("gv")
-                if nv:
+                if fused:
+                    for a in (0, 64):
+                        tt(A(xn, 16 * a, 16 * a + 1024), I(A("XC"), A("cU", hs + a, hs + a + 64)), A("zr", 16 * a, 16 * a + 1024), SUB)
+                elif nv:
                     cp(A(xn, 0, 16 * nv), I(A("XC"), A("cU", hs, hs + nv)))
                 on("gs")
                 l0 = nv
@@ -514,14 +567,20 @@ def build(T, topo, core, rank):
                 on("mb")
                 if own:
                     diff(H("xb"), H("mb"), 1)
-                else:
+                elif s == 0:
                     tt(H("mb"), H("xb"), zP, MAX)
                 for j in sv_:
                     on("ABCD"[j])
-                    tt(mj(j), xs_(j), A(pz), MAX)
+                    if fused:
+                        ts(mj(j), xs_(j), 0.0, MAX)
+                    else:
+                        tt(mj(j), xs_(j), A(pz), MAX)
                 for j in ss_:
                     on("ABCD"[j])
-                    diff(xs_(j), mj(j), 4)
+                    if fused:
+                        act(mj(j), xs_(j), func=ACT.Abs)
+                    else:
+                        diff(xs_(j), mj(j), 4)
                 on("mp")
                 if apart:
                     if own:
@@ -533,23 +592,20 @@ def build(T, topo, core, rank):
                 col = lambda j: A(pk, j, 272, 17)
                 mm(key, A("ones", 0, 128), A("CK", 272 * s, 272 * s + 272), True, False)
                 zc = [1 + k for j in ss_ for k in ks_(j)] + ([0, 1][:1 + apart] if own else [])
-                if ks + own == 5:
-                    zc = []
-                elif (ks, own) in zr:
-                    zc = [1] if apart and own != (ks == 4) else []
-                    mm(key, zz, zr[ks, own], False, False)
+                kz = 4 if fused else ks
+                if (kz, own) in zr:
+                    zc = [1] if apart and own != (kz == 4) else []
+                    mm(key, zz, zr[kz, own], False, False)
                     merge(2)
                 for c in zc:
-                    mm(col(c), zz, neg if ks == 4 else one, False, False)
+                    mm(col(c), zz, neg if kz == 4 else one, False, False)
                 merge(1 + len(zc))
                 mm(key, H("chi"), A("PH0" if apart else "PH"), False, False)
                 mm(A(pk, 136, 272), H("c16"), A("PF0" if apart else "PF"), False, False)
                 if s == 0:
                     mm(col(0), H("b0h"), A("SH"), False, False)
                     mm(col(136), H("t16"), A("SF"), False, False)
-                else:
-                    mm(col(0), A("Pm"), A("D", 16 * h, 16 * h + 16), False, False)
-                merge(4 - s)
+                merge(4 - 2 * s)
                 on("neg")
                 kv = [k for j in sv_ for k in ks_(j)]
                 for k in kv:
@@ -559,7 +615,12 @@ def build(T, topo, core, rank):
                 turn = sorted(range(4), key=lambda j: (sv_.index(j) if j in sv_ else ss_.index(j), j))
                 for j in turn:
                     on("ABCD"[j])
-                    if j == turn[-1]:
+                    if j == turn[-1] and s == 1:
+                        mm(col(0), A("Pf", 0, 128), wv(24 + h), False, False)
+                        mm(col(0), A("Pf", 128, 256), wv(28 + h), False, False)
+                        mm(col(0), A("Pm"), A("D", 16 * h, 16 * h + 16), False, False)
+                        merge(3)
+                    elif j == turn[-1]:
                         if not own:
                             mm(col(0), H("xb"), neg, False, False)
                         mm(col(0), H("mb"), one if own else two, False, False)
@@ -577,17 +638,20 @@ def build(T, topo, core, rank):
                     merge(3 if own else 4)
                 scan(A("R", 272 * h, 272 * h + 272), A("d0"), key, ADD, MIN)
                 ends = A("R", 272 * h + 16, 272 * h + 272, 17)
-                aq, dd = A("Aq", 16 * h, 16 * h + 16), A("D", 16 * h, 16 * h + 16)
-                ts(aq, ends, 1610612736.0, ADD, 1610612736.0, SUB)
-                tt(dd, ends, aq, SUB)
+                dd = A("Di", 16 * h, 16 * h + 16)
+                ts(dd, ends, 127, ALU.bitwise_and)
                 cp(I(A("Z", zo, zo + 288), zl[s]), dd)
+
+                def winners(out):
+                    mm(out, A("ones", 0, 128), A("c64", 16, 24), True, False)
+                    for v in range(2):
+                        for e in range(2):
+                            a, c = zo + 144 * v + (1 - e) * (1 if s else 8), 32 * s + 16 * v + 8 * e
+                            mm(out, A("Z", a, a + 128), A("RE", c, c + 8), False, v + e == 2)
+                    merge(5)
+
                 bP = A(pk, 288, 296)
-                for v in range(2):
-                    for e in range(2):
-                        a = zo + 144 * v + (1 - e) * (1 if s else 8)
-                        c = 32 * s + 16 * v + 8 * e
-                        mm(bP, A("Z", a, a + 128), A("RE", c, c + 8), v + e == 0, v + e == 2)
-                merge(4)
+                winners(bP)
                 if s == 0:
                     ts(A("bU", 16 + 8 * h, 24 + 8 * h), bP, MID, ADD)
                     continue
@@ -601,31 +665,35 @@ def build(T, topo, core, rank):
                 merge(2)
                 mm(A(pz, 0, 128), A("Ih"), H("xs"), False, True)
                 zn = A("XWn", xw + 512 + hs, xw + 640 + hs)
-                ts(zn, A(pz, 0, 128), 12582912.0, ADD, 12582912.0, SUB)
+                if OPT["zs"] > h:
+                    act(H("bb"), A(pz, 0, 128), bias=12582912.0)
+                    act(zn, H("bb"), bias=-12582912.0)
+                else:
+                    ts(zn, A(pz, 0, 128), 12582912.0, ADD, 12582912.0, SUB)
                 if not last:
                     send(nxt, [(A("zin", 256 * t + 256 + hs, 256 * t + 384 + hs), zn)], HOP + 300)
                 at("bG%d" % h)
                 act(A("FWn", 512 + hs, 640 + hs), I(A("ID"), boh))
                 at("brow%d" % h)
-                ts(H("brow"), A("FWn", 512 + hs, 640 + hs) if h or not OPT["brow"] else I(A("ID"), boh), MID, SUB)
+                less("brow%d" % h, H("brow"), A("FWn", 512 + hs, 640 + hs) if h or not OPT["brow"] else I(A("ID"), boh))
                 at("v%d" % h)
                 act(A("KWn", 512 + hs, 640 + hs), I(KIN, boh))
-                ts(H("v16"), A("KWn", 512 + hs, 640 + hs), MID, SUB)
+                less("v%d" % h, H("v16"), A("KWn", 512 + hs, 640 + hs))
                 at("E2")
                 if h == 1:
                     mm(A("pn", 16, 256), A("TM", 0, 128), A("ones", 0, 240), True, False)
-                for c0 in range(8 * h, 8 * h + 8, 4):
-                    at("E%d" % (c0 // 4))
-                    for c in range(c0, c0 + 4):
+                for c0, c1 in ((8, 12), (12, 16)) if h else ((0, 3), (3, 6), (6, 8)):
+                    at("E%d" % c0)
+                    for c in range(c0, c1):
                         ts(A("E", 272 * c, 256 * c + 256), A("brow", 16 * c, 256), A(pk, 288 + c % 8, 289 + c % 8),
                            EQ, A("w", 256 + c, 257 + c), MUL)
-                    merge(4)
-                    cs = [c for c in range(c0, c0 + 4) if c < 15]
+                    merge(c1 - c0)
+                    cs = [c for c in range(c0, c1) if c < 15]
                     for c in cs:
                         mm(A("pn", 16 * c + 16, 256), A("Qa", 16, 144), A("E", 272 * c + 16, 256 * c + 256), False, c == 7)
                     merge(len(cs))
                 at("may")
-                act(A("bF", 8 * h, 8 * h + 8), bP, bias=MID)
+                winners(A("pw", 64 + 8 * h, 72 + 8 * h))
         at("zn0")
         bo = A("bO", 16 * t, 16 * t + 16)
         bi = lambda h: A("bin", 16 * t + 8 * h, 16 * t + 8 * h + 8)
@@ -640,7 +708,7 @@ def build(T, topo, core, rank):
         if not last:
             for h in (1, 0):
                 at("t%d" % h)
-                ts(A("t16", 128 * h, 128 * h + 128), I(A("kst", 0, W_), bi(h)), MID, SUB)
+                less("t%d" % h, A("t16", 128 * h, 128 * h + 128), I(A("kst", 0, W_), bi(h)))
                 starts(h)
         if t == VIS - 2:
             at("home")
@@ -649,14 +717,23 @@ def build(T, topo, core, rank):
             send(prv, [(ext("tback"), A("trf"))], HOP + 2000)
             dma("Y", A("TT", 0, W_, 1, row0), ext("tback"), 4000)
         at("may")
-        act(wv(18), A("bF"), bias=-lo - 127.5, func=ACT.Abs)
+        bW = A("pw", 64, 80)
+        act(wv(18), bW, bias=MID - lo - 127.5, func=ACT.Abs)
+        act(A("nW", 128, 144), bW, scale=-1.0)
+        merge(2)
+        tt(A("q1", 32, 64, 2), bW, A("cw", 64, 80), SUB)
         act(wv(19), wv(18), bias=-128.0, func=ACT.Sign)
         tt(wv(20), wv(19), wv(14), MUL)
-        tt(A("q1", 32, 64, 2), A("bF"), spK, SUB)
         if not last:
             act(A("q1", 64, 96, 2), A("q1", 32, 64, 2))
         at("colM")
-        act(A("colM"), kb, scale=m0)
+        if OPT["cm"]:
+            dma("Y", A("colM", 0, 256, 1, row0), A("ID", lo, lo + 256, 1, row0))
+            for j in range(8):
+                dma("Y", A("colM", 0, 256, 1, (16 * j + 1, 16 * j + 16)), A("KWn", 512, 768, 1, (16 * j + 1, 16 * j + 16)))
+            merge(9)
+        else:
+            act(A("colM"), kb, scale=m0)
         at("cnt")
         act(A("HC", 16, 256), A("pn", 16, 256))
         for r in range(16):
@@ -680,10 +757,18 @@ def build(T, topo, core, rank):
         merge(2)
         tt(A("q1", 96, 128, 2), wv(17), A("q0", 1, 32, 2), MUL)
         at("hit")
-        tt(A("HC", 256, 512), I(FEET, uv(5)), bG, EQ)
-        conv("pc", 0, "Qb", "HC", 256, a=256)
-        at("seat2")
-        cp(A("q0", 97, 128, 2), A("pc", 0, 16))
+        if "hit" in SCALAR.split():
+            act(A("e16", 0, 256), I(FEET, uv(5)), bias=-MID)
+            conv("pc", 0, "Qh", "e16", 256, stop=False)
+            mm(A("pc", 0, 16), A("If"), A("nW", 128, 144), False, True)
+            merge(2)
+            at("seat2")
+            ts(A("q0", 97, 128, 2), A("pc", 0, 16), 0.0, EQ)
+        else:
+            tt(A("HC", 256, 512), I(FEET, uv(5)), bG, EQ)
+            conv("pc", 0, "Qb", "HC", 256, a=256)
+            at("seat2")
+            cp(A("q0", 97, 128, 2), A("pc", 0, 16))
         scan(A("q2", 96, 128), A("q0", 96, 128), A("q1", 96, 128), MUL, ADD)
         cp(A("sl", 64 * t + 48, 64 * t + 64), A("q2", 97, 128, 2))
         sl = lambda j, t=t: A("sl", 64 * t + 16 * j, 64 * t + 16 * j + 16)
@@ -700,9 +785,12 @@ def build(T, topo, core, rank):
             dma("Y", A("X", lo, lo + 256), A("XC", lo, lo + 256))
             early_kin(t + 1)
         at("par")
-        tt(I(KINS, sl(1)), A("colM"), A("nrow", 256 * r_, 256 * r_ + 256), ADD)
+        if OPT["cm"]:
+            cp(I(KINS, sl(1)), A("colM"))
+        else:
+            tt(I(KINS, sl(1)), A("colM"), A("nrow", 256 * r_, 256 * r_ + 256), ADD)
         at("FT")
-        act(A("KN", fl, fl + 256), I(A("FWn"), sl(0)))
+        (cp if OPT["ft"] else act)(A("KN", fl, fl + 256), I(A("FWn"), sl(0)))
         at("foot")
         cp(I(FEET, sl(3)), nG)
         at("Aout")
@@ -721,10 +809,9 @@ def build(T, topo, core, rank):
                 cp(I(A("TT"), A("sl", a, a + 8)), bb)
             dma("Y", ext("yt"), A("TT", 0, W_, 1, row0), 3000)
             dma("S", ext("yp"), A("KN", 0, B_, 1, row0), 3000)
-            for j in range(N):
-                if j != r_:
-                    dma("S", ext("yk", 256 * j, 256 * j + 256, slice(*row0)),
-                        A("KN", B_ + 256 * j, B_ + 256 * j + 256, 1, row0))
+            for j in others:
+                dma("S", ext("yk", 256 * j, 256 * j + 256, slice(*row0)),
+                    A("KN", B_ + 256 * j, B_ + 256 * j + 256, 1, row0))
             dma("Y", ext("yf"), A("KN", FB + B_, FB + W_, 1, row0))
     return ops
 
@@ -817,6 +904,106 @@ def arrange(ops):
     return best, end
 
 
+def polish(ops, start, rounds):
+    n = len(ops)
+    above, deps = [], []
+    for i, o in enumerate(ops):
+        far = 0
+        for j in o["dep"]:
+            far |= above[j]
+        deps.append({j: w for j, w in o["dep"].items() if ops[j]["k"] != "c" or not far >> j & 1})
+        for j in o["dep"]:
+            far |= 1 << j
+        above.append(far)
+    cases = []
+    for fig in CASES:
+        c = [sum(a * b for a, b in zip(o["cv"], (1.0,) + fig[:6])) for o in ops]
+        du = [0.0 if o["k"] == "r" else fig[8] * len(o["f"]) if o["k"] == "d" else c[i] for i, o in enumerate(ops)]
+        lag = [[(j, c[j] + (fig[7] if ops[j]["e"] == o["e"] else fig[6]) if w else du[j]) for j, w in deps[i].items()]
+               for i, o in enumerate(ops)]
+        cases.append((c, du, lag))
+    name, seen = [], {}
+    for o in ops:
+        k = (o["e"], o["b"], o["v"])
+        seen[k] = seen.get(k, 0) + 1
+        name.append(k + (seen[k],))
+    index = {k: i for i, k in enumerate(name)}
+    needed = set(j for d in deps for j in d)
+    final = [i for i in range(n) if i not in needed]
+    queue = ["VSPGYR".index(o["e"]) for o in ops]
+
+    def timed(order, than=None, slack=0.0):
+        prev, last = [-1] * n, [-1] * 6
+        for i in order:
+            e = queue[i]
+            if e < 5:
+                prev[i] = last[e]
+                last[e] = i
+        total, runs = 0.0, []
+        for c, du, lag in cases:
+            at, why = [0.0] * n, [-1] * n
+            for i in order:
+                p = prev[i]
+                s = at[p] + du[p] if p >= 0 else 0.0
+                for j, l in lag[i]:
+                    if at[j] + l > s:
+                        s = at[j] + l
+                        p = j
+                at[i], why[i] = s, p
+            end, i = max((at[i] + c[i], i) for i in final)
+            worth = end + MEAN * sum(at) / n
+            total += worth
+            runs.append((at, why, i, end, worth))
+            if than and total > sum(x[4] for x in than[1][:len(runs)]) + slack + (SLACK if len(runs) < len(cases) else 0):
+                return None
+        return total, runs, prev
+
+    order = sorted(range(n), key=lambda i: (start[i], i))
+    now = best = timed(order)
+    seed = [SEED]
+
+    def draw(m):
+        seed[0] = (seed[0] * 1103515245 + 12345) % 2147483648
+        return (seed[0] >> 8) % m
+
+    for r in range(rounds):
+        at, why, i = now[1][draw(len(cases))][:3]
+        if draw(100) < ANY:
+            i = draw(n)
+        pairs = []
+        while i >= 0:
+            if why[i] >= 0 and why[i] == now[2][i] and not above[i] >> why[i] & 1:
+                pairs.append((why[i], i))
+            i = why[i]
+        if not pairs:
+            continue
+        u, v = pairs[draw(len(pairs) if pairs[0][1] in final or why[pairs[0][1]] < 0 else min(len(pairs), NEAR))]
+        q = [i for i in order if queue[i] == queue[u]]
+        far, ahead, a = (0, 0, 1, 2, 3, 5, 8, 13, 21, 34)[draw(10)], draw(2), (u, v)[draw(2)]
+        far += (a == v) != ahead
+        b = q[max(q.index(u) - far, 0)] if ahead else q[min(q.index(v) + far, len(q) - 1)]
+        alone = min(name[a][2], name[b][2]) < 1 or (name[a][2] == VIS - 1 and draw(2))
+        new = list(order)
+        for d in (0,) if alone else range(-VIS, VIS + 1):
+            x, y = (index.get(name[z][:2] + (name[z][2] + d, name[z][3])) for z in (a, b))
+            if x is None or y is None or (d and min(name[x][2], name[y][2]) < 1):
+                continue
+            i, j = new.index(x), new.index(y)
+            if ahead and j < i:
+                part = new[j:i + 1]
+                new[j:i + 1] = sorted(part, key=lambda k: k != x and not above[x] >> k & 1)
+            elif not ahead and i < j:
+                part = new[i:j + 1]
+                new[i:j + 1] = sorted(part, key=lambda k: k == x or above[k] >> x & 1)
+        trial = timed(new, now, SLACK * (1 - r / rounds))
+        if trial:
+            now = trial
+            order = sorted(new, key=lambda k: trial[1][0][0][k])
+            if now[0] < best[0]:
+                best = now
+    return best[1][0][0], [int(x[3]) for x in best[1]]
+
+
 def emit(g, T, ops, start):
     queue = {"V": g.vector, "S": g.scalar, "P": g.tensor, "G": g, "Y": g.sync}
     order = sorted(range(len(ops)), key=lambda i: (start[i], i))
@@ -864,7 +1051,7 @@ def emit(g, T, ops, start):
         if o["k"] == "r":
             target[i] = (o["x"][0], o["x"][1])
         elif o["k"] == "d":
-            target[i] = ("d%d" % nd, 16)
+            target[i] = ("d%d" % nd, 16 * len(o["f"]))
             nd += 1
         elif o["k"] == "c" and i in marked:
             count[o["e"]] = count.get(o["e"], 0) + 1
@@ -878,9 +1065,11 @@ def emit(g, T, ops, start):
             q.wait_ge(T.sem[target[j][0]], target[j][1])
         for f in o["f"]:
             ins = f(q)
+            if o["k"] == "d":
+                ins.then_inc(T.sem[target[i][0]], 16)
         if o["k"] == "d":
-            ins.then_inc(T.sem[target[i][0]], 16)
-        elif o["k"] == "s":
+            continue
+        if o["k"] == "s":
             sent += o["x"]
         elif i in marked:
             ins.then_inc(T.sem[target[i][0]], 1)
@@ -895,4 +1084,7 @@ def rank_program(g, core, T, topo):
     if rank is None:
         return
     ops = build(T, topo, core, rank)
-    emit(g, T, ops, plan(ops)[0])
+    start = plan(ops)[0]
+    if not PLAN:
+        PLAN.append(polish(ops, start, ROUNDS)[0])
+    emit(g, T, ops, polish(ops, PLAN[0], 0)[0])

@@ -6,26 +6,29 @@ W_, B_, L_, VIS = 3584, 2560, 256, 5
 F0, DK = 3856, 3600
 FW, FO, DF = 1296, 2552, 1032
 FB = F0 - FO
+UP = 1024
 MID = 1792.0
 WT = 2176.0
-SPLIT = [[(0, 2, 0), (16, 2, 0)], [(32, 0, 0), (16, 2, 0)]]
-SPLIT0 = [[(48, 1, 0), (32, 1, 0)], [(32, 0, 0), (16, 2, 0)]]
-CUTS = (128,)
-OPT = {"brow": 1, "xc": 1, "e0": 0, "es": 0, "cm": 0, "ft": 0, "zs": 0}
-SCALAR = "v0 v1 t0 t1 hit brow1"
+BIG = 12582912.0
+SPLIT = [[(0, 32, 2), (0, 32, 2)], [(0, 48, 1), (0, 48, 2)]]
+SPLIT0 = [[(0, 64, 2), (0, 32, 2)], [(0, 48, 1), (0, 48, 2)]]
+FCUT, VCUT, SCUT = 64, (32, 64), (64, 64)
+OPT = {"pf": 2, "xp": 1, "xx": "G", "tu": 16, "h0": 0, "tm": 1, "vd": 1, "t1": 0, "sc": 1}
+SCALAR = "v0 v1 kb0 kb1 t0 t1 hit brow1 brow0 kin01 colY xs0 xs1 lvN wt stay foot gy fu turn down"
 BOOST = {}
 PASSES = 1
 
 SB, F32, BF, F16, I32, U16 = "sbuf", "float32", "bfloat16", "float16", "int32", "uint16"
 SCRATCH = {}
-for _d, _l in ((I32, "kst 3856 fst 1280 trs 224 trt 224 ci 8 R 544 Di 32"),
-               (F32, "KN 5152 ID 3584 TT 3856 trf 224 onef 128 tmpc 256 cf 32 cw 96 c17 16 d0 272 "
-                     "ain 40 aout 40 acc 8 b0 256 colY 256 urow 256 nrow 1024 colM 256 KS 256 "
-                     "FWn 768 KWn 768 bb 256 Pf 256 w 512 q0 128 q1 128 q2 128 o0 64 o1 64 o2 64"),
-               (BF, "X 3584 XC 3584 ones 272 Ib 128 Ih 128 In 128 I8 128 Pm 128 Qb 144 Qa 144 TM 2048 BD 48 CK 544 PH 272 "
-                    "PH0 272 SH 16 RE 64 cq 256 tmpb 272 zin 1280 zp 256 b0h 256 chi 256 x0b 2048 x1b 2048 m0b 2048 m1b 2048 "
-                    "xb 256 mb 256 xs 256 D 32 Z 1152 HC 512 E 4352 XS 256 XWn 3840 phi 256 xp 256 mp 256 lv 16 c64 24 ZR 1904 zr 2048"),
-               (F16, "Qh 144 If 128 SF 8 PF 136 PF0 136 g16 512 e16 512 v16 256 t16 256 p16 256 c16 256 nW 144 brow 256"),
+for _d, _l in ((I32, "kst 3856 fsd 64 bsd 16 trs 224 trt 224 ci 8 R 544 Di 32"),
+               (F32, "KN 5152 ID 4608 TT 3856 trf 224 ftf 64 onef 128 tmpc 256 cf 40 cw 96 c17 16 d0 272 "
+                     "ain 40 aout 40 acc 8 colY 256 dq 256 I32 128 yrow 256 nrow 256 KS 256 "
+                     "KWn 512 bb 256 thr 48 Pf 256 w 512 q0 128 q1 128 q2 128 o0 64 o1 64 o2 64"),
+               (BF, "XX 7424 ones 272 BO 128 I15 128 Ib 128 Ih 128 In 128 I8 128 Pm 128 Qb 144 Qa 144 TM 2048 BD 48 CK 544 CB 272 "
+                    "RE 64 cq 256 tmpb 272 zin 1280 zp 256 x0b 2048 x1b 2048 m0b 2048 m1b 2048 "
+                    "xs 256 D 32 Z 1152 E 4352 XS 256 XWn 2560 xp 256 mp 256 lv 16 c64 24 ZR 2176 zr 4096"),
+               (F16, "Qh 144 Q16 144 HC 512 If 144 Im 128 I0 128 I1 128 SH 16 SF 8 PH 272 PH0 272 PF 136 PF0 136 g16 512 e16 512 v16 256 t16 256 "
+                     "p16 256 c16 256 nW 144 brow 256 b16 16 fw 16"),
                (U16, "cu 32 bin 80 oin 80 bU 32 bO 80 cU 256 u 256 sl 320")):
     _l = _l.split()
     for _n, _c in zip(_l[::2], _l[1::2]):
@@ -39,8 +42,9 @@ SEMAPHORES = ["eV", "eS", "eP", "eG", "sent"] + ["d%d" % i for i in range(80)] +
 GA, SC, PE, HOP, XW, SW, FIX, DL = 1.56, 3.8, 0.55, 4000, 130, 80, 25, 2600
 CASES = [(1.56, 3.8, 0.55, 20, 3000, 2600, 140, 80, 80), (2.0, 5.5, 0.5, 10, 2600, 2000, 110, 60, 60),
          (1.3, 3.0, 0.65, 35, 7000, 4000, 200, 100, 200), (1.1, 1.8, 0.5, 20, 3500, 2600, 320, 160, 80)]
-ROUNDS, SLACK, SEED, PLAN = 60000, 1000, 3, []
-MEAN, ANY, NEAR = 1.0, 30, 1000
+PLACE = (1.56, 3.8, 0.55, 20, 4500, 3200, 150, 80, 100)
+FIRST, ROUNDS, SLACK, SEED, PLAN = 42000, 70000, 200, 3, []
+MEAN, ANY, LOOK, EARLY, FREE = 1.0, 30, 300, 1e9, 10
 
 
 def build(T, topo, core, rank):
@@ -54,7 +58,8 @@ def build(T, topo, core, rank):
             b = SCRATCH[name][1][1]
         ps = slice(None) if p is None else slice(*p)
         ap = T[name][ps, a:b] if s == 1 else T[name][ps, a:b:s]
-        return (ap, [(name, a, b)], len(range(a, b, s)), SCRATCH[name][2], SCRATCH[name][0])
+        part = (name, 0, W_ + UP) if name == "ID" and tag[1] >= 0 else (name, a, b)
+        return (ap, [part], len(range(a, b, s)), SCRATCH[name][2], SCRATCH[name][0])
 
     def I(win, off):
         return (win[0].indirect(off[0]), win[1] + off[1], off[2] * 16, win[3], "ind", off[1])
@@ -63,7 +68,7 @@ def build(T, topo, core, rank):
         cv = list(cost) + [0] * (7 - len(cost))
         cost = sum(a * b for a, b in zip(cv, (1, GA, SC, PE, FIX, HOP, DL)))
         ops.append({"e": eng, "f": [fn], "r": r, "w": w, "c": float(cost), "cv": cv, "k": kind, "x": extra,
-                    "t": eng + (w[0][0] if w else "") + "." + tag[0], "b": tag[0], "v": tag[1]})
+                    "b": tag[0], "v": tag[1]})
         return len(ops) - 1
 
     def at(name, t=None):
@@ -139,6 +144,9 @@ def build(T, topo, core, rank):
     def act(out, in_, bias=0.0, scale=1.0, func=None, accum=None):
         r, w = rw(out, [in_, bias, scale])
         fu = ACT.Identity if func is None else func
+        if out[4] == "ind":
+            add("S", lambda q: q.activation(out[0], in_[0], fu), r, w, (80, 0, out[2]))
+            return
         if accum is None:
             f = lambda q: q.activation(out[0], in_[0], fu, bias=sv(bias), scale=sv(scale))
         else:
@@ -157,8 +165,8 @@ def build(T, topo, core, rank):
             f = lambda q: q.iota(out[0], pat, base, cm, allow_small_or_imprecise_dtypes=True)
         add("G", f, [], out[1], (160 + 2 * out[2],))
 
-    def asel(out, in_, pat, base, cm):
-        add("G", lambda q: q.affine_select(out[0], in_[0], pat, ALU.is_equal, 0.0, base, cm), in_[1], out[1], (200 + 2 * out[2],))
+    def asel(out, in_, pat, base, cm, op=ALU.is_equal, other=0.0):
+        add("G", lambda q: q.affine_select(out[0], in_[0], pat, op, other, base, cm), in_[1], out[1], (200 + 2 * out[2],))
 
     def dma(eng, out, in_, cost=2600):
         add(eng, lambda q: q.dma_start(out[0], in_[0]), in_[1], out[1], (cost - 2600, 0, 0, 0, 0, 0, 1), "d")
@@ -198,44 +206,66 @@ def build(T, topo, core, rank):
     EQ, LT, GT, MUL, ADD, SUB, MAX, MIN = (ALU.is_equal, ALU.is_lt, ALU.is_gt, ALU.mult, ALU.add, ALU.subtract, ALU.max, ALU.min)
     row0 = (0, 128, 16)
     KIN, KINS, FEET = A("KN", 0, W_), A("KN", 0, F0), A("KN", F0, F0 + FW)
+    X = lambda a=0, b=W_: A("XX", a, b)
+    XC = lambda a=0, b=W_: A("XX", W_ + a, W_ + b)
+    home = B_ + L_ * rank
+
+    def lin(name, out, in_, bias=0.0, scale=1.0):
+        if name in SCALAR.split():
+            act(out, in_, bias=bias, scale=scale)
+        elif scale != 1.0:
+            ts(out, in_, scale, MUL, bias, ADD)
+        elif bias != 0.0:
+            ts(out, in_, bias, ADD)
+        else:
+            cp(out, in_)
+
+    def scatter(name, out, in_):
+        if name in SCALAR.split():
+            act(out, in_, func=ACT.Silu)
+        else:
+            cp(out, in_)
 
     def fill(out, val, p=None):
         act(out, A("KN", W_, W_ + out[2], 1, p), bias=val, scale=0.0)
 
+    dma("S", A("bsd"), ext("bs"))
+    dma("S", A("fsd"), ext("ft"))
     for j, (a, b) in enumerate(((2560, 3584), (0, 896), (896, 1792), (1792, 2560))):
         dma("Y", A("kst", a, b), ext("kn", a, b), (3700, 4800, 6900, 8700)[j])
         chain("load")
         cp(A("KN", a, b), A("kst", a, b))
-        if j == 0:
-            ms(A("fst", 1024, 1280), 0)
-            dma("S", A("fst", 1024, 1280, 1, row0), ext("bs"), 3500)
-            ms(A("fst", 0, 1024), 0)
-            dma("Y", A("fst", 0, 1024, 1, row0), ext("ft"), 2700)
-            chain("load")
-            dma("S", A("zin", 0, 256), ext("z0"), 3900)
-    dma("Y", A("XC"), ext("x0"), 12700)
+    dma("S", A("zin", 0, 256), ext("z0"), 3900)
+    dma("Y", A("XX", 2 * W_, 2 * W_ + L_), ext("x0", home, home + L_), 9000)
+    chain("load")
+    for a, b in ((0, home), (home + L_, W_)):
+        if a < b:
+            dma("Y", XC(a, b), ext("x0", a, b), 12700)
+    merge(2 if home + L_ < W_ else 1)
     chain("load")
     dma("Y", A("trs"), ext("tr"), 13200)
     chain("load")
-    dma("Y", A("X"), ext("x0"), 17000)
-    chain("load")
+    ts(A("trs"), A("trs"), MID, SUB)
     send(nxt, [(ext("tin"), A("trs"))], HOP + 4000)
     ms(A("KN", W_, F0 + 8), -1.0)
-    fill(A("KN", FB + W_, F0 + FW), -1.0)
-    dma("Y", A("kst", 0, W_, 1, row0), ext("tin"), 4000)
-    cp(A("KN", FB + B_, FB + W_), A("fst", 0, 1024))
-    cp(A("b0"), A("fst", 1024, 1280))
+    for a in range(F0 + 8, F0 + FW, 280):
+        fill(A("KN", a, min(a + 280, F0 + FW)), -1.0)
+    ts(A("ftf"), A("fsd"), float(UP), ADD)
+    dma("S", A("KN", FB + B_, FB + W_, 1, row0), A("ftf"))
+    ms(A("t16"), 0.0)
+    ts(A("b16"), A("bsd"), MID, SUB)
+    dma("S", A("t16", 0, 256, 1, row0), A("b16"))
 
-    iota(A("ID", B_, W_), [[1, 1024]], B_, 0)
     ms(A("ones"), 1.0)
     fill(A("onef"), -1.0)
     asel(A("Qb"), A("ones", 0, 144), [[-16, 9], [-1000, 16]], 16, 1)
     cp(A("Qh"), A("Qb"))
-    asel(A("Ib"), A("ones", 0, 128), [[-1, 128]], 0, 1)
+    asel(A("tmpb", 0, 144), A("ones", 0, 144), [[-1, 144]], 0, 1)
+    cp(A("If"), A("tmpb", 0, 144))
+    cp(A("Ib"), A("tmpb", 0, 128))
     act(A("Ih"), A("Ib"), scale=0.5)
     act(A("In"), A("Ib"), scale=-1.0)
     act(A("I8"), A("Ib"), scale=-8192.0)
-    cp(A("If"), A("Ib"))
     iota(A("ci", 0, 1), [[0, 1]], 0, 1)
     ts(A("ci", 1, 2), A("ci", 0, 1), 15, ALU.bitwise_and)
     ts(A("ci", 2, 3), A("ci", 0, 1), 4, ALU.arith_shift_right)
@@ -243,9 +273,15 @@ def build(T, topo, core, rank):
     ts(A("ci", 4, 5), A("ci", 1, 2), 3, ALU.arith_shift_right)
     cp(A("cf", 0, 5), A("ci", 0, 5))
     cP, cR, cG, c7, cV = [A("cf", j, j + 1) for j in range(5)]
-    m0, m1 = A("cf", 8, 9), A("cf", 9, 10)
+    m0, m1, sgn, mid0, far0 = [A("cf", j, j + 1) for j in (8, 9, 32, 33, 34)]
     ts(m0, cR, 0.5, GT)
     ts(m1, cR, 0.5, LT)
+    act(sgn, m0, scale=2.0, bias=-1.0)
+    act(far0, m0, scale=float(W_), bias=MID)
+    act(mid0, m0, scale=-MID - 32768.0, bias=32768.0)
+    act(A("Im"), A("Ib"), scale=-1.0)
+    act(A("I0"), A("Ib"), scale=m0)
+    act(A("I1"), A("Ib"), scale=m1)
     ts(A("cf", 10, 11), cV, 144.0, MUL, 1.0, ADD)
     ts(A("cf", 11, 12), c7, 16.0, MUL, A("cf", 10, 11), ADD)
     zl = [A("cu", 0, 1), A("cu", 2, 3)]
@@ -257,9 +293,8 @@ def build(T, topo, core, rank):
     act(A("Pf", 0, 128), A("Pm"), scale=WT)
     act(A("Pf", 128, 256), A("Pm"), scale=-1.0)
     iota(A("tmpc", 160, 192), [[0, 2], [16, 16]], 0, 0)
-    iW, spK, spM = A("cw", 0, 16), A("cw", 32, 48), A("cw", 64, 96)
+    iW, spM = A("cw", 0, 16), A("cw", 64, 96)
     ts(A("cw", 0, 32), A("tmpc", 160, 192), cR, ADD)
-    act(spK, iW, bias=float(DK))
     act(A("cw", 64, 80), iW, bias=DK - MID)
     act(A("cw", 80, 96), iW, bias=DF + FO - MID)
     for j in range(N):
@@ -270,33 +305,43 @@ def build(T, topo, core, rank):
     act(A("o1", 1, 32, 2), iW, bias=float(DK))
     act(A("o1", 33, 64, 2), iW, bias=float(DF))
     fill(A("q1", 0, 32, 2), 256.0)
-    act(A("q1", 33, 96, 2), A("cw", 0, 32), bias=float(DK))
-    act(A("q1", 97, 128, 2), iW, bias=float(DF))
+    act(A("q1", 1, 32, 2), iW, bias=-MID)
+    act(A("q1", 33, 64, 2), iW, bias=DK - MID)
+    act(A("q1", 65, 96, 2), iW, bias=DF - MID)
+    act(A("q1", 97, 128, 2), iW, bias=DK - MID)
     fill(A("c17"), WT)
     fill(A("c64", 0, 16), 64.0)
-    fill(A("c64", 16, 24), -(MID + 32) / 128)
+    fill(A("c64", 16, 24), -33 * 64.0 / 128)
     iota(A("tmpc", 192, 208), [[0, 2], [1, 8]], 0, 0)
     two, neg, one = A("BD", 0, 16), A("BD", 16, 32), A("BD", 32, 48)
     for o, v in ((two, 2 * WT), (neg, -WT), (one, WT)):
         ts(o, A("tmpc", 192, 208), cG, EQ, v, MUL)
     asel(A("tmpb"), A("ones"), [[0, 2], [-16, 8], [-1, 17]], 1, 1)
     ms(A("tmpb", 0, 272, 17), 0.0)
-    act(A("PH", 0, 136), A("tmpb", 0, 136), scale=1.0 / 32)
-    act(A("PH", 136, 272), A("tmpb", 136, 272), scale=-1.0)
     cp(A("PF"), A("tmpb", 0, 136))
-    act(A("PH0"), A("PH"), scale=m0)
     ts(A("PF0"), A("PF"), m0, MUL)
+    ts(A("tmpb", 0, 136), A("tmpb", 0, 136), 1.0 / 32, MUL)
+    ts(A("tmpb", 136, 272), A("tmpb", 136, 272), -1.0, MUL)
+    cp(A("PH"), A("tmpb"))
+    for a in (0, 136):
+        asel(A("tmpb", a, a + 136), A("tmpb", a, a + 136), [[-16, 8], [0, 17]], 0, 1, ALU.not_equal, BIG / (1024 if a else 32768))
+    cp(A("PH0"), A("tmpb"))
     asel(A("cq", 0, 8), A("ones", 0, 8), [[-16, 8]], 0, 1)
     act(A("SH", 0, 8), A("cq", 0, 8), scale=1.0 / 32)
     act(A("SH", 8, 16), A("cq", 0, 8), scale=-1.0)
     cp(A("SF"), A("cq", 0, 8))
-    iota(A("CK"), [[0, 32], [4, 17]], -32, 0)
-    ms(A("CK", 0, 544, 1, (0, 32)), -16 * WT)
-    ms(A("CK", 272, 544, 17, (0, 32)), 0.0)
-    for s in range(2):
-        ms(A("CK", 272 * s, 272 * s + 136, 1, (64, 128)), -128.0 / 64)
-        ms(A("CK", 272 * s + 136, 272 * s + 272, 1, (64, 128)), (4096.0 + MID + 32) / 64)
-    ms(A("CK", 272, 544, 17, (64, 128)), 0.0)
+    ms(A("CK", 0, 544, 1, (32, 64)), -16 * WT)
+    ms(A("CK", 0, 544, 1, (0, 32)), 0.0)
+    iota(A("CK", 0, 544, 1, (0, 1)), [[0, 32], [128, 17]], -1088, 0)
+    for a in range(0, 544, 136):
+        big = BIG * (32 if a % 272 else 1)
+        if a < 272:
+            fill(A("CB", a, a + 136), big / 128)
+        ms(A("CK", a, a + 136, 1, (64, 128)), -big / 64)
+    ms(A("CK", 1, 272, 17), 0.0)
+    ms(A("CK", 272, 544, 17), 0.0)
+    ms(A("CK", 272, 544, 17, (0, 1)), -1152.0)
+    fill(A("CB", 0, 272, 17), 0.0)
     fill(A("d0"), 0.0)
     fill(A("d0", 0, 272, 17), 67108864.0)
     iota(A("tmpc", 208, 224), [[1, 2], [2, 8]], 0, 0)
@@ -309,85 +354,99 @@ def build(T, topo, core, rank):
     iota(A("tmpc", 240, 249), [[1, 9]], -1, 0)
     fill(A("Qa"), 0.0)
     ts(A("Qa", 0, 144, 16), A("tmpc", 240, 249), cG, EQ)
-    ts(A("cf", 16, 32), A("tmpc", 224, 240), cR, GT)
-    for r in range(16):
-        act(A("TM", 128 * r, 128 * r + 128), A("Qa", 16 - r, 144 - r), scale=A("cf", 16 + r, 17 + r))
-        if r % 4 == 3:
-            merge(4)
+    for a in (0, 1024):
+        dma("Y", A("TM", a, a + 1024), A("Z", 0, 1024), 15500)
+        chain("load")
+    dma("Y", X(), ext("x0"), 19500)
+    chain("load")
+    if OPT["sc"]:
+        iota(A("dq", 0, 128), [[1, 8], [0, 16]], 0, 0)
+        ts(A("BO"), A("dq", 0, 128), cG, EQ)
+        ts(A("D", 0, 16), A("tmpc", 224, 240), cR, EQ, 2.0 ** 23, MUL)
+        ts(A("cf", 16, 17), cR, 1.0, ADD)
+        ts(A("D", 16, 32), A("tmpc", 224, 240), A("cf", 16, 17), EQ, -2.0 ** 22, MUL)
+        for c in range(32):
+            mm(A("pn", 16 * (c // 2), 16 * (c // 2) + 16), A("Ib"), A("D", 16 * (c % 2), 16 * (c % 2) + 16), c == 0, c == 31)
+        merge(32)
+        act(A("dq"), A("pn", 0, 256))
+        ts(A("cf", 17, 18), cR, 14.5, LT, 2.0 ** 22, MUL)
+        act(A("I15"), A("Ib"), scale=A("cf", 17, 18))
+        act(A("I32"), A("Ib"))
+    for r in range(1, 16):
+        asel(A("TM", 129 * r, 128 * r + 128, 16), A("Qa", 16, 144, 16), [[16, 8]], r, -1, GT)
+        if r % 4 == 0 or r == 15:
+            merge(4 if r < 15 else 3)
+    act(A("Q16"), A("Qb"), scale=16.0)
     fill(A("cq"), -0.25 / 128)
     fill(A("HC", 0, 16), 0.0)
-    fill(A("FWn", 256, 512), float(W_))
     fill(A("aout"), 0.0)
-    fill(A("urow"), 0.0)
-    if not OPT["cm"]:
-        act(A("nrow"), A("ID", B_, W_), scale=m1)
-    for a in range(0, B_, 640):
-        iota(A("ID", a, a + 640), [[1, 640]], a, 0)
+    fill(A("nrow"), 0.0)
+    for a in range(0, W_ + UP, 512):
+        iota(A("ID", a, a + 512), [[1, 512]], a, 0)
+
+    kcol = lambda s, k: k + 1 if s or k else 0
+
+    def zcols(s, nf, ks):
+        plain = [kcol(s, k) for k in range(16) if k % 4 >= 4 - ks or nf == 128]
+        return plain, [kcol(s, k) for k in range(16) if kcol(s, k) not in plain and nf]
 
     zr = {}
     for s, split in enumerate(SPLIT0 + SPLIT):
-        for nv, ks, own in split:
-            own *= 1 - s % 2
-            ks = 4 if nv == 128 else ks
-            if (ks, own) not in zr and 1 < ks + own:
-                a = 272 * len(zr)
-                zr[ks, own] = A("ZR", a, a + 272)
-                mm(A("pd", 0, 272), A("TM", 0, 128), A("ones"), True, False)
-                cols = [1 + k for k in range(16) if k % 4 >= 4 - ks] + [0] * own
-                for c in cols:
-                    mm(A("pd", c, 272, 17), A("Ib"), one, False, c == cols[-1])
-                merge(1 + len(cols))
-                act(zr[ks, own], A("pd", 0, 272))
+        for nf, nv, ks in split:
+            for cols in zcols(s % 2, nf, ks):
+                if cols and tuple(cols) not in zr:
+                    a = 272 * len(zr)
+                    zr[tuple(cols)] = A("ZR", a, a + 272)
+                    mm(A("pd", 0, 272), A("Z", 0, 128), A("ones"), True, False)
+                    for c in cols:
+                        mm(A("pd", c, 272, 17), A("Ib"), one, False, c == cols[-1])
+                    merge(1 + len(cols))
+                    act(zr[tuple(cols)], A("pd", 0, 272))
 
     def conv(bank, c0, Q, name, n, start=True, a=0, stop=True):
         for r in range(16):
             mm(A(bank, c0, c0 + n // 16), A(Q, 16 - r, 144 - r), A(name, a + r, a + n, 16), start and r == 0, stop and r == 15)
         merge(16)
 
-    def less(name, out, in_, by=MID):
-        if name in SCALAR.split():
-            act(out, in_, bias=-by)
-        else:
-            ts(out, in_, by, SUB)
-
-    def kin(s, h):
+    def kin(s, h, t):
         a, b, bu = 128 * h, 128 * h + 128, A("bU", 16 * s + 8 * h, 16 * s + 8 * h + 8)
         at("kin%d%d" % (s, h))
-        if "kin%d%d" % (s, h) in SCALAR.split():
+        if s == 0:
+            lin("kin0%d" % h, A("c16", a, b), I(KIN, bu), mid0, m0)
+            pu = A("pk%d" % h, 288, 416)
+            mm(pu, A("I1"), A("t16", a, b), True, False)
+            if t == 0:
+                mm(pu, A("I1"), A("v16", a, b), False, False)
+                merge(2)
+            mm(pu, A("I0"), A("c16", a, b), False, True)
+            ts(A("cU", a, b), pu, far0 if t else MID, ADD)
+        elif "kin1%d" % h in SCALAR.split():
             act(A("c16", a, b), I(KIN, bu), bias=-MID)
             ts(A("cU", a, b), A("c16", a, b), MID, ADD)
-            at("parts%d%d" % (s, h))
         else:
             cp(A("cU", a, b), I(KIN, bu))
             at("parts%d%d" % (s, h))
             ts(A("c16", a, b), A("cU", a, b), MID, SUB)
-        less("chi%d%d" % (s, h), A("chi", a, b), A("c16", a, b), -MID - 4096.0)
 
     def starts(h):
         pz = "pk%d" % h
         conv(pz, 0, "Qh", "t16", 128, a=128 * h)
         ts(A("bU", 8 * h, 8 * h + 8), A(pz, 0, 8), MID, ADD)
-        less("b0h", A("b0h", 128 * h, 128 * h + 128), A("t16", 128 * h, 128 * h + 128), -MID - 4096.0)
 
     def early_kin(t):
         lo = B_ + L_ * ((rank - t) % N)
         at("far")
-        if t:
-            iota(A("XC", lo, lo + 256), [[0, 256]], 8192, 0)
-        else:
-            act(A("xb"), I(A("XC"), A("bU", 0, 16)))
-            ms(A("XC", lo, lo + 256), 8192.0)
-        if t or OPT["e0"]:
-            first_kin(1)
+        iota(XC(lo, lo + 256), [[0, 256]], 8192, 0)
+        kin(0, 1 - OPT["h0"], t)
 
-    def first_kin(h):
-        kin(0, h)
-
-    ts(A("t16"), A("b0"), MID, SUB)
+    act(A("e16", 0, 256), A("t16"), bias=MID - home - 127.5, func=ACT.Abs)
+    ts(A("v16"), A("e16", 0, 256), 128.0, LT, float(W_ - home), MUL)
     for h in (1, 0):
         at("t%d" % h)
         starts(h)
     early_kin(0)
+    at("init")
+    dma("Y", A("kst", 0, W_, 1, row0), ext("tin"), 4000)
     nd = [0]
     wv = lambda j, n=16: A("w", 16 * j, 16 * j + n)
     uv = lambda j, n=16: A("u", 16 * j, 16 * j + n)
@@ -397,88 +456,74 @@ def build(T, topo, core, rank):
         r_ = (rank - t) % N
         lo = B_ + L_ * r_
         fl = FB + lo
-        nG = A("ID", lo, lo + 256)
         z = lambda a=0, b=256: A("zin", 256 * t + a, 256 * t + b)
-        xw = 768 * t
+        xw = 512 * t
         others = [(r_ + d) % N for d in range(1, N)]
         at("yu", t)
-        early = t > 0 or OPT["e0"]
-        if early:
-            first_kin(0)
+        kin(0, OPT["h0"], t)
         at("yu")
         if t:
-            dma("Y", A("urow", 0, 256, 1, row0), A("KN", lo, lo + 256, 1, row0))
-            dma("Y", A("FWn", 0, 256), A("KN", fl, fl + 256))
+            dma("Y", A("yrow"), A("KN", fl, fl + 256))
         else:
-            act(A("urow"), A("KN", lo, lo + 256), scale=m1)
-            act(A("FWn", 0, 256), A("KN", fl, fl + 256))
-        less("gu", A("g16", 256, 512), A("KN", lo, lo + 256))
-        less("gy", A("g16", 0, 256), A("KN", fl, fl + 256))
-        conv("pc", 0, "Qh", "g16", 512)
-        ts(uv(0), A("pc", 0, 16), MID, ADD)
-        ts(uv(1), A("pc", 16, 32), MID + FB, ADD, float(F0), MAX)
-        merge(2)
-        tt(A("o1", 0, 64, 2), A("pc", 0, 32), spM, SUB)
+            dma("Y", A("yrow"), A("KN", fl, fl + 256), 6000)
+        lin("gu", A("g16", 256, 512), A("KN", lo, lo + 256), -MID)
+        lin("gy", A("g16", 0, 256), A("KN", fl, fl + 256), -MID - UP)
+        conv("pw", 96, "Qh", "g16", 512)
+        yu = lambda a, b: A("pw", 96 + a, 96 + b)
+        ts(uv(0, 32), yu(0, 32), MID, ADD)
+        tt(A("o1", 0, 64, 2), yu(0, 32), spM, SUB)
         at("own")
-        act(wv(0, 32), A("pc", 0, 32), bias=MID - lo - 127.5, func=ACT.Abs)
+        act(wv(0, 32), yu(0, 32), bias=MID - lo - 127.5, func=ACT.Abs)
         at("live")
         tt(wv(4), wv(0), wv(1), MIN)
         live = A("lv")
         ts(live, wv(4), 128.0, GT)
+        at("wts")
+        lin("lvN", wv(14), live, -MID, float(W_))
+        lin("wt", wv(16), live, 1.0, MID - 1)
+        tt(wv(15), yu(0, 16), wv(14), MAX)
         at("e16")
-        ne = 16 if OPT["es"] == 1 else 32
-        if OPT["es"]:
-            less("py", A("e16", 0, 256), I(KINS, uv(0)))
-            at("fu")
-            less("fu", A("e16", 256, 512), I(A("KN"), uv(1)))
-        else:
-            less("py", A("e16"), I(A("KN"), uv(0, 32)))
+        ne = 32
+        lin("py", A("e16", 0, 256), I(KINS, uv(0)), -MID)
+        at("fu")
+        lin("fu", A("e16", 256, 512), I(A("KN", FB), uv(1)), -MID - UP)
         at("colY")
-        act(A("colY"), I(KINS, uv(0)), scale=m0)
-        for j in range(2):
-            dma("Y", A("XWn", xw + 256 * j, xw + 256 * j + 256), A("X", lo, lo + 256))
+        mm(A("pz0", 0, 256), A("I1"), A("g16", 256, 512), True, False)
+        mm(A("pz0", 0, 256), A("I0"), A("e16", 0, 256), False, True)
+        lin("colY", A("colY"), A("pz0", 0, 256), MID)
+        dma("Y", A("XWn", xw, xw + 256), X(lo, lo + 256))
         at("held")
         conv("pc", 0, "Qh", "e16", 16 * ne, stop=False)
-        mm(A("pc", 0, ne), A("If"), A("nW", 32 * r_, 32 * r_ + ne), False, False)
+        mm(A("pc", 0, ne), A("If", 0, 128), A("nW", 32 * r_, 32 * r_ + ne), False, False)
         mm(A("pc", 0, 16), A("ones", 0, 128), A("c64", 0, 16), False, False)
         mm(A("pc", 0, 16), A("I8"), live, False, True)
         merge(3)
         ts(A("o0", 1, 2 * ne, 2), A("pc", 0, ne), 0.0, EQ)
-        scan(A("o2", 0, 32), A("o0", 0, 32), A("o1", 0, 32), MUL, ADD)
-        cp(uv(2), A("o2", 1, 32, 2))
-        tt(I(KINS, uv(2)), A("colY"), A("urow"), ADD)
-        at("turn0")
-        if OPT["es"] == 1:
-            conv("pc", 0, "Qh", "e16", 256, a=256, stop=False)
-            mm(A("pc", 0, 16), A("If"), A("nW", 32 * r_, 32 * r_ + 16), False, True)
-            merge(2)
-            ts(A("o0", 33, 64, 2), A("pc", 0, 16), 0.0, EQ)
-        tt(A("o0", 33, 64, 2), A("o0", 33, 64, 2), A("o0", 1, 32, 2), MUL)
-        scan(A("o2", 32, 64), A("o0", 32, 64), A("o1", 32, 64), MUL, ADD)
-        cp(uv(3), A("o2", 33, 64, 2))
-        if early:
-            at("p16")
-            less("p16", A("p16"), I(KIN, A("bU", 0, 16)))
-            at("phi")
-            less("phi", A("phi"), A("p16"), -MID - 4096.0)
+        if OPT["tm"]:
+            tt(A("o0", 33, 64, 2), A("o0", 33, 64, 2), A("o0", 1, 32, 2), MUL)
+            scan(A("o2"), A("o0"), A("o1"), MUL, ADD)
+            cp(uv(2, 32), A("o2", 1, 64, 2))
         else:
-            first_kin(1)
-            first_kin(0)
-        at("phi")
-        for j in range(2):
-            dma("Y", A("KWn", 256 * j, 256 * j + 256), A("KN", lo, lo + 256))
+            scan(A("o2", 0, 32), A("o0", 0, 32), A("o1", 0, 32), MUL, ADD)
+            cp(uv(2), A("o2", 1, 32, 2))
+        cp(I(KINS, uv(2)), A("colY"))
+        at("turn0")
+        if not OPT["tm"]:
+            tt(A("o0", 33, 64, 2), A("o0", 33, 64, 2), A("o0", 1, 32, 2), MUL)
+            scan(A("o2", 32, 64), A("o0", 32, 64), A("o1", 32, 64), MUL, ADD)
+            cp(uv(3), A("o2", 33, 64, 2))
+        at("p16")
+        lin("p16", A("p16"), I(KIN, A("bU", 0, 16)), -MID)
+        dma("Y", A("KWn", 0, 256), A("KN", lo, lo + 256))
+        dma("Y", A("nrow", 0, 256, 1, row0), A("ID", lo, lo + 256, 1, row0))
         at("turn")
-        for h in range(2):
-            cp(I(FEET, A("u", 48 + 8 * h, 56 + 8 * h)), A("FWn", 128 * h, 128 * h + 128))
-        at("wts")
-        act(wv(14), live, scale=256.0)
-        tt(A("q1", 1, 32, 2), wv(14), iW, ADD)
-        act(wv(16), live, scale=255.0, bias=1.0)
+        for a in range(0, 16, OPT["tu"]):
+            scatter("turn", I(FEET, A("u", 48 + a, 48 + a + OPT["tu"])), A("yrow", 16 * a, 16 * (a + OPT["tu"])))
         if last:
             for j in others:
                 a = B_ + 256 * j
                 dma("Y", ext("yk", 256 * j, 256 * j + 256), A("KN", a, a + 256), 3000)
-                dma("Y", ext("yx", 256 * j, 256 * j + 256), A("X", a, a + 256), 3000)
+                dma("Y", ext("yx", 256 * j, 256 * j + 256), X(a, a + 256), 3000)
         at("Ain")
         if t > 0:
             a0 = A("ain", 8 * t, 8 * t + 1)
@@ -491,151 +536,135 @@ def build(T, topo, core, rank):
                 asel(A("zp", 128 * h + c, 128 * h + 128, 8), z(128 * h + 16 * c, 128 * h + 16 * c + 16), [[0, 16]], 0, 0)
                 if c % 2:
                     merge(2)
-        if early:
-            at("p16")
-            conv("pw", 48, "Qh", "p16", 256)
-            ts(uv(10), A("pw", 48, 64), MID, ADD)
-            at("xp")
-            act(A("xp"), I(A("XC"), uv(10)))
-        at("xb0")
-        if t:
-            act(A("xb"), I(A("X"), A("bU", 0, 16)))
+        at("p16")
+        conv("pw", 48, "Qh", "p16", 256)
+        ts(uv(10), A("pw", 48, 64), MID, ADD)
+        at("xp")
+        if OPT["xp"]:
+            tt(A("xp"), I(XC(), uv(10)), z(), SUB)
+            ts(A("mp"), A("xp"), 0.0, MAX)
+        else:
+            act(A("xp"), I(XC(), uv(10)))
         for s in range(2):
-            for h in (1, 0):
+            for h in (0, 1) if s == 0 and OPT["h0"] else (1, 0):
                 on = lambda name: at("%s%d%d" % (name, s, h))
-                apart = early and s == 0
                 hs = 128 * h
                 H = lambda name: A(name, hs, hs + 128)
-                zz = z(hs, hs + 128) if s == 0 else H("zp")
+                zz = lambda a=0, b=128: z(hs + a, hs + b) if s == 0 else A("zp", hs + a, hs + b)
                 pz, pk, xn, mn, zo = "pz%d" % h, "pk%d" % h, "x%db" % h, "m%db" % h, 288 * (2 * s + h)
-                zP = A(pz, 0, 512, 4)
-                bu = A("bU", 16 * s + 8 * h, 16 * s + 8 * h + 8)
-                nv, ks, own = (SPLIT if t else SPLIT0)[s][1 - h]
-                fused = nv == 128
-                if fused:
+                win = XC() if s else A("XX", 0, 2 * W_) if t else A("XX", W_)
+                nf, nv, ks = (SPLIT if t else SPLIT0)[s][1 - h]
+                zo_ = 2048 * h
+                if nf:
                     on("zr")
                     for k in range(16):
-                        asel(A("zr", k, 2048, 16), zz, [[0, 128]], 0, 0)
-                        if k % 2:
+                        asel(A("zr", zo_ + k, zo_ + 16 * nf, 16), zz(0, nf), [[0, nf]], 0, 0)
+                        if k % 2 and nf < 128:
                             merge(2)
                 if s == 1:
-                    kin(1, h)
-                    own = 0
+                    kin(1, h, t)
                 if s == 1 and h == 1:
                     at("stay")
                     cp(A("D"), A("Di"))
-                    ts(wv(30, 32), A("R", 16, 544, 17), 56.0, SUB, 1.0 / WT, MUL)
-                    act(wv(22, 32), wv(30, 32), bias=12582912.0)
-                    act(wv(24, 32), wv(22, 32), bias=-12582912.0)
+                    ts(wv(22, 32), A("R", 16, 544, 17), 1.0 / WT, MUL, BIG, ADD)
+                    lin("stay", wv(24, 32), wv(22, 32), -BIG)
                     tt(wv(26, 32), A("R", 16, 544, 17), A("R", 0, 544, 17), SUB)
                     ts(wv(28, 32), wv(26, 32), A("d0", 1, 2), ALU.is_ge, A("d0", 1, 2), MUL)
                 on("z")
-                nz = 4 if ks < 4 and not fused else 1 - own if s == 0 else 0
+                nz = 4 if ks < 4 and nf < 128 else 1 if s == 0 and not OPT["xp"] else 0
+                z0_ = nf if s or OPT["xp"] else 0
                 for j in range(nz):
-                    mm(A(pz, j, 512, 4), A("Ib"), zz, True, True)
+                    mm(A(pz, 4 * z0_ + j, 512, 4), A("Ib"), zz(z0_), True, True)
                 if nz:
                     merge(nz)
+                on("gf")
+                for a in range(0, nf, FCUT):
+                    b = min(nf, a + FCUT)
+                    tt(A(xn, 16 * a, 16 * b), I(win, A("cU", hs + a, hs + b)), A("zr", zo_ + 16 * a, zo_ + 16 * b), SUB)
                 on("gv")
-                if fused:
-                    for a in (0, 64):
-                        tt(A(xn, 16 * a, 16 * a + 1024), I(A("XC"), A("cU", hs + a, hs + a + 64)), A("zr", 16 * a, 16 * a + 1024), SUB)
-                elif nv:
-                    cp(A(xn, 0, 16 * nv), I(A("XC"), A("cU", hs, hs + nv)))
+                for a in range(nf, nf + nv, VCUT[s]):
+                    b = min(nf + nv, a + VCUT[s])
+                    cp(A(xn, 16 * a, 16 * b), I(win, A("cU", hs + a, hs + b)))
                 on("gs")
-                l0 = nv
-                for l1 in CUTS:
-                    if l1 > l0:
-                        act(A(xn, 16 * l0, 16 * l1), I(A("XC"), A("cU", hs + l0, hs + l1)))
-                        l0 = l1
-                    on("gt")
-                xs_ = lambda j: A(xn, j, 2048, 4)
-                mj = lambda j: A(mn, 512 * j, 512 * j + 512)
-                ks_ = lambda j: [k for k in range(j, 16, 4) if k or not apart]
+                for a in range(nf + nv, 128, SCUT[s]):
+                    b = min(128, a + SCUT[s])
+                    act(A(xn, 16 * a, 16 * b), I(win, A("cU", hs + a, hs + b)))
+                xs_ = lambda j, a, b: A(xn, 16 * a + j, 16 * b, 4)
+                mj = lambda j, a, b: A(mn, 512 * j + 4 * a, 512 * j + 4 * b)
                 mk = lambda k: A(mn, 512 * (k % 4) + k // 4, 512 * (k % 4) + 512, 4)
                 sv_, ss_ = list(range(4 - ks)), list(range(4 - ks, 4))
                 banks = ("pd", "pc" if s else "pn")
-
-                def diff(x, m, n):
-                    pd = banks[nd[0] % 2]
-                    nd[0] += 1
-                    for j in range(n):
-                        mm(A(pd, j, 128 * n, n), A("In"), zz, j == 0, False)
-                    merge(n)
-                    mm(A(pd, 0, 128 * n), A("Ib"), x, False, True)
-                    act(m, A(pd, 0, 128 * n), func=ACT.Abs)
-
-                on("mb")
-                if own:
-                    diff(H("xb"), H("mb"), 1)
-                elif s == 0:
-                    tt(H("mb"), H("xb"), zP, MAX)
                 for j in sv_:
                     on("ABCD"[j])
-                    if fused:
-                        ts(mj(j), xs_(j), 0.0, MAX)
-                    else:
-                        tt(mj(j), xs_(j), A(pz), MAX)
+                    if nf:
+                        ts(mj(j, 0, nf), xs_(j, 0, nf), 0.0, MAX)
+                    if nf < 128:
+                        tt(mj(j, nf, 128), xs_(j, nf, 128), A(pz, 4 * nf, 512), MAX)
                 for j in ss_:
                     on("ABCD"[j])
-                    if fused:
-                        act(mj(j), xs_(j), func=ACT.Abs)
-                    else:
-                        diff(xs_(j), mj(j), 4)
+                    if nf:
+                        act(mj(j, 0, nf), xs_(j, 0, nf), func=ACT.Abs)
+                    if nf < 128:
+                        pd = banks[nd[0] % 2]
+                        nd[0] += 1
+                        for i in range(4):
+                            mm(A(pd, 4 * nf + i, 512, 4), A("In"), zz(nf), i == 0, False)
+                        merge(4)
+                        mm(A(pd, 4 * nf, 512), A("Ib"), xs_(j, nf, 128), False, True)
+                        act(mj(j, nf, 128), A(pd, 4 * nf, 512), func=ACT.Abs)
                 on("mp")
-                if apart:
-                    if own:
-                        diff(H("xp"), H("mp"), 1)
-                    else:
-                        tt(H("mp"), H("xp"), zP, MAX)
+                if s == 0 and not OPT["xp"]:
+                    tt(H("mp"), H("xp"), A(pz, 0, 512, 4), MAX)
                 on("key")
                 key = A(pk, 0, 272)
                 col = lambda j: A(pk, j, 272, 17)
-                mm(key, A("ones", 0, 128), A("CK", 272 * s, 272 * s + 272), True, False)
-                zc = [1 + k for j in ss_ for k in ks_(j)] + ([0, 1][:1 + apart] if own else [])
-                kz = 4 if fused else ks
-                if (kz, own) in zr:
-                    zc = [1] if apart and own != (kz == 4) else []
-                    mm(key, zz, zr[kz, own], False, False)
-                    merge(2)
-                for c in zc:
-                    mm(col(c), zz, neg if kz == 4 else one, False, False)
-                merge(1 + len(zc))
-                mm(key, H("chi"), A("PH0" if apart else "PH"), False, False)
-                mm(A(pk, 136, 272), H("c16"), A("PF0" if apart else "PF"), False, False)
+                if s:
+                    mm(key, A("ones", 0, 128), A("CB"), True, False)
+                mm(key, H("c16"), A("PH" if s else "PH0"), s == 0, False)
                 if s == 0:
-                    mm(col(0), H("b0h"), A("SH"), False, False)
+                    mm(col(0), H("t16"), A("SH"), False, False)
+                mm(key, A("ones", 0, 128), A("CK", 272 * s, 272 * s + 272), False, False)
+                mm(A(pk, 136, 272), H("c16"), A("PF" if s else "PF0"), False, False)
+                if s == 0:
                     mm(col(136), H("t16"), A("SF"), False, False)
-                merge(4 - 2 * s)
+                merge(5 - 2 * s)
+                if s:
+                    mm(col(0), A("Pf", 0, 128), wv(24 + h), False, False)
+                    mm(col(0), A("Pf", 128, 256), wv(28 + h), False, False)
+                    mm(col(0), A("Pm"), A("D", 16 * h, 16 * h + 16), False, False)
+                    merge(3)
+                n = 0
+                for cols, m in zip(zcols(s, nf, ks), (128, nf)):
+                    if cols:
+                        mm(A(pk, 0, 272, 1, (0, m)), zz(0, m), zr[tuple(cols)], False, False)
+                        n += 1
+                if n:
+                    merge(n)
                 on("neg")
-                kv = [k for j in sv_ for k in ks_(j)]
+                kv = [k for j in sv_ for k in range(j, 16, 4)]
                 for k in kv:
-                    mm(col(1 + k), A(xn, k, 2048, 16), neg, False, False)
+                    mm(col(kcol(s, k)), A(xn, k, 2048, 16), neg, False, False)
                 if kv:
                     merge(len(kv))
                 turn = sorted(range(4), key=lambda j: (sv_.index(j) if j in sv_ else ss_.index(j), j))
                 for j in turn:
                     on("ABCD"[j])
-                    if j == turn[-1] and s == 1:
-                        mm(col(0), A("Pf", 0, 128), wv(24 + h), False, False)
-                        mm(col(0), A("Pf", 128, 256), wv(28 + h), False, False)
-                        mm(col(0), A("Pm"), A("D", 16 * h, 16 * h + 16), False, False)
-                        merge(3)
-                    elif j == turn[-1]:
-                        if not own:
-                            mm(col(0), H("xb"), neg, False, False)
-                        mm(col(0), H("mb"), one if own else two, False, False)
-                        merge(1 if own else 2)
-                    for k in ks_(j):
-                        mm(col(1 + k), mk(k), two if j in sv_ else one, False, not apart and j == turn[-1] and k == j + 12)
-                    merge(len(ks_(j)))
-                on("dec")
-                if apart:
-                    mm(col(1), H("phi"), A("SH"), False, False)
+                    for k in range(j, 16, 4):
+                        mm(col(kcol(s, k)), mk(k), two if j in sv_ else one, False, s == 1 and j == turn[-1] and k == j + 12)
+                    merge(4)
+                if s == 0:
+                    on("par")
+                    mm(col(1), H("p16"), A("SH"), False, False)
+                    mm(col(1), A("ones", 0, 128), A("CK", 273, 544, 17), False, False)
                     mm(col(137), H("p16"), A("SF"), False, False)
-                    if not own:
-                        mm(col(1), H("xp"), neg, False, False)
-                    mm(col(1), H("mp"), one if own else two, False, True)
-                    merge(3 if own else 4)
+                    if OPT["xp"]:
+                        mm(col(1), zz(), one, False, False)
+                    merge(3 + OPT["xp"])
+                    on("dec")
+                    mm(col(1), H("xp"), neg, False, False)
+                    mm(col(1), H("mp"), two, False, True)
+                    merge(2)
+                on("dec")
                 scan(A("R", 272 * h, 272 * h + 272), A("d0"), key, ADD, MIN)
                 ends = A("R", 272 * h + 16, 272 * h + 272, 17)
                 dd = A("Di", 16 * h, 16 * h + 16)
@@ -659,29 +688,26 @@ def build(T, topo, core, rank):
                 ts(boh, bP, MID, ADD)
                 send(prv if last else nxt, [(A("bin", 16 * t + 8 * h, 16 * t + 8 * h + 8), boh)], HOP)
                 at("zn%d" % h)
-                act(H("xs"), I(A("X"), boh))
+                lin("xs%d" % h, H("xs"), I(X(), boh))
                 mm(A(pz, 0, 128), A("ones", 0, 128), A("cq", 0, 128), True, False)
                 mm(A(pz, 0, 128), A("Ih"), z(hs, hs + 128), False, False)
                 merge(2)
+                zn = A("XWn", xw + 256 + hs, xw + 384 + hs)
                 mm(A(pz, 0, 128), A("Ih"), H("xs"), False, True)
-                zn = A("XWn", xw + 512 + hs, xw + 640 + hs)
-                if OPT["zs"] > h:
-                    act(H("bb"), A(pz, 0, 128), bias=12582912.0)
-                    act(zn, H("bb"), bias=-12582912.0)
-                else:
-                    ts(zn, A(pz, 0, 128), 12582912.0, ADD, 12582912.0, SUB)
+                ts(zn, A(pz, 0, 128), BIG, ADD, BIG, SUB)
                 if not last:
                     send(nxt, [(A("zin", 256 * t + 256 + hs, 256 * t + 384 + hs), zn)], HOP + 300)
-                at("bG%d" % h)
-                act(A("FWn", 512 + hs, 640 + hs), I(A("ID"), boh))
                 at("brow%d" % h)
-                less("brow%d" % h, H("brow"), A("FWn", 512 + hs, 640 + hs) if h or not OPT["brow"] else I(A("ID"), boh))
+                lin("brow%d" % h, H("brow"), I(A("ID"), boh), -MID)
                 at("v%d" % h)
-                act(A("KWn", 512 + hs, 640 + hs), I(KIN, boh))
-                less("v%d" % h, H("v16"), A("KWn", 512 + hs, 640 + hs))
+                if OPT["vd"] > h:
+                    lin("v%d" % h, H("v16"), I(KIN, boh), -MID)
+                lin("kb%d" % h, A("KWn", 256 + hs, 384 + hs), I(KIN, boh), 0.0, sgn)
+                if OPT["vd"] <= h:
+                    lin("v%d" % h, H("v16"), A("KWn", 256 + hs, 384 + hs), -MID, -1.0)
                 at("E2")
                 if h == 1:
-                    mm(A("pn", 16, 256), A("TM", 0, 128), A("ones", 0, 240), True, False)
+                    mm(A("pn", 0, 256), A("TM", 0, 128), A("ones", 0, 256), True, False)
                 for c0, c1 in ((8, 12), (12, 16)) if h else ((0, 3), (3, 6), (6, 8)):
                     at("E%d" % c0)
                     for c in range(c0, c1):
@@ -690,30 +716,32 @@ def build(T, topo, core, rank):
                     merge(c1 - c0)
                     cs = [c for c in range(c0, c1) if c < 15]
                     for c in cs:
-                        mm(A("pn", 16 * c + 16, 256), A("Qa", 16, 144), A("E", 272 * c + 16, 256 * c + 256), False, c == 7)
+                        mm(A("pn", 16 * c + 16, 256), A("BO") if OPT["sc"] else A("Qa", 16, 144), A("E", 272 * c + 16, 256 * c + 256), False, c == 7)
                     merge(len(cs))
                 at("may")
                 winners(A("pw", 64 + 8 * h, 72 + 8 * h))
         at("zn0")
-        bo = A("bO", 16 * t, 16 * t + 16)
         bi = lambda h: A("bin", 16 * t + 8 * h, 16 * t + 8 * h + 8)
-        bG = A("FWn", 512, 768)
-        kb = A("KWn", 512, 768)
         if last:
-            dma("Y", ext("yz"), A("XWn", xw + 512, xw + 768))
+            dma("Y", ext("yz"), A("XWn", xw + 256, xw + 512))
         if 0 < t < VIS - 1:
             for h in (1, 0):
                 at("T%d" % h)
-                cp(I(A("kst"), A("oin", 16 * t + 8 * h, 16 * t + 8 * h + 8)), A("FWn", 512 + 128 * h, 640 + 128 * h))
-        if not last:
+                cp(I(A("kst"), A("oin", 16 * t + 8 * h, 16 * t + 8 * h + 8)), A("brow", 128 * h, 128 * h + 128))
+        if not last and OPT["t1"]:
+            at("t1")
+            lin("t1", A("t16"), I(A("kst", 0, W_), A("bin", 16 * t, 16 * t + 16)))
+            conv("pk1", 0, "Qh", "t16", 256)
+            ts(A("bU", 0, 16), A("pk1", 0, 16), MID, ADD)
+        elif not last:
             for h in (1, 0):
                 at("t%d" % h)
-                less("t%d" % h, A("t16", 128 * h, 128 * h + 128), I(A("kst", 0, W_), bi(h)))
+                lin("t%d" % h, A("t16", 128 * h, 128 * h + 128), I(A("kst", 0, W_), bi(h)))
                 starts(h)
         if t == VIS - 2:
             at("home")
             dma("Y", A("trt"), A("kst", 0, W_, 1, row0), 4000)
-            cp(A("trf"), A("trt"))
+            ts(A("trf"), A("trt"), MID, ADD)
             send(prv, [(ext("tback"), A("trf"))], HOP + 2000)
             dma("Y", A("TT", 0, W_, 1, row0), ext("tback"), 4000)
         at("may")
@@ -722,89 +750,109 @@ def build(T, topo, core, rank):
         act(A("nW", 128, 144), bW, scale=-1.0)
         merge(2)
         tt(A("q1", 32, 64, 2), bW, A("cw", 64, 80), SUB)
-        act(wv(19), wv(18), bias=-128.0, func=ACT.Sign)
-        tt(wv(20), wv(19), wv(14), MUL)
+        act(wv(19), wv(18), bias=-131072.0, scale=1024.0)
+        tt(A("thr", 0, 16), wv(19), wv(14), MIN)
         if not last:
-            act(A("q1", 64, 96, 2), A("q1", 32, 64, 2))
-        at("colM")
-        if OPT["cm"]:
-            dma("Y", A("colM", 0, 256, 1, row0), A("ID", lo, lo + 256, 1, row0))
-            for j in range(8):
-                dma("Y", A("colM", 0, 256, 1, (16 * j + 1, 16 * j + 16)), A("KWn", 512, 768, 1, (16 * j + 1, 16 * j + 16)))
-            merge(9)
-        else:
-            act(A("colM"), kb, scale=m0)
-        at("cnt")
-        act(A("HC", 16, 256), A("pn", 16, 256))
-        for r in range(16):
-            mm(A("pc", 0, 16), A("TM", 128 * r, 128 * r + 128), A("E", r, 16 * 272, 272), r == 0, False)
-        merge(16)
-        conv("pc", 0, "Qb", "HC", 256, start=False)
-        cnt = A("pc", 0, 16)
-        at("seat")
-        n = 64 if last else 96
-        tt(A("q0", 1, 32, 2), cnt, wv(20), LT)
-        tt(A("q0", 33, 64, 2), cnt, wv(20), LT)
-        if not last:
-            ts(A("q0", 65, 96, 2), cnt, 0.5, LT)
-        merge(n // 32)
-        scan(A("q2", 0, n), A("q0", 0, n), A("q1", 0, n), MUL, ADD)
-        cp(A("sl", 64 * t, 64 * t + n // 2), A("q2", 1, n, 2))
+            act(A("q1", 96, 128, 2), A("q1", 32, 64, 2))
         at("vl")
-        conv("pw", 0, "Qh", "v16", 256)
-        ts(uv(5), A("pw", 0, 16), MID - FO, ADD, 0.0, MAX)
-        tt(wv(17), A("pw", 0, 16), A("cw", 80, 96), SUB)
-        merge(2)
-        tt(A("q1", 96, 128, 2), wv(17), A("q0", 1, 32, 2), MUL)
+        conv("pd", 0, "Qh", "v16", 256)
+        ts(uv(5), A("pd", 0, 16), MID - FO, ADD)
+        tt(A("q1", 64, 96, 2), A("pd", 0, 16), A("cw", 80, 96), SUB)
         at("hit")
-        if "hit" in SCALAR.split():
-            act(A("e16", 0, 256), I(FEET, uv(5)), bias=-MID)
-            conv("pc", 0, "Qh", "e16", 256, stop=False)
-            mm(A("pc", 0, 16), A("If"), A("nW", 128, 144), False, True)
+        lin("hit", A("HC", 256, 512), I(FEET, uv(5)), (-MID - UP) / 16, 1.0 / 16)
+        if last:
+            lin("down", A("KN", FB + B_, FB + W_), A("KN", FB + B_, FB + W_), -float(UP))
+        cnt = A("pc", 0, 16)
+        n = 96 if last else 128
+        if OPT["sc"]:
+            mm(A("pd", 16, 32), A("If", 0, 128), A("nW", 128, 144), True, False)
+            conv("pd", 16, "Q16", "HC", 256, start=False, a=256)
+            ts(wv(17), A("pd", 16, 32), 0.0, EQ)
+            at("cnt")
+            scan(A("tmpc"), A("dq"), A("pn", 0, 256), ADD, MIN)
+            for r in range(16):
+                mm(cnt, A("TM", 128 * r, 128 * r + 128), A("E", r, 16 * 272, 272), r == 0, False)
+            mm(cnt, A("I15"), A("ones", 0, 16), False, False)
+            merge(17)
+            mm(cnt, A("I32"), A("tmpc", 15, 256, 16), False, True)
+            at("seat")
+            tt(A("q0", 1, 32, 2), cnt, A("thr", 0, 16), LT)
+            tt(A("q0", 33, 64, 2), cnt, A("thr", 0, 16), LT)
             merge(2)
-            at("seat2")
-            ts(A("q0", 97, 128, 2), A("pc", 0, 16), 0.0, EQ)
+            if OPT["sc"] == 2:
+                scan(A("q2", 0, 64), A("q0", 0, 64), A("q1", 0, 64), MUL, ADD)
+                ts(A("sl", 64 * t, 64 * t + 32), A("q2", 1, 64, 2), MID, ADD)
+                at("seat2")
         else:
-            tt(A("HC", 256, 512), I(FEET, uv(5)), bG, EQ)
-            conv("pc", 0, "Qb", "HC", 256, a=256)
-            at("seat2")
-            cp(A("q0", 97, 128, 2), A("pc", 0, 16))
-        scan(A("q2", 96, 128), A("q0", 96, 128), A("q1", 96, 128), MUL, ADD)
-        cp(A("sl", 64 * t + 48, 64 * t + 64), A("q2", 97, 128, 2))
+            at("cnt")
+            act(A("HC", 16, 256), A("pn", 16, 256), scale=1.0 / 16)
+            for r in range(16):
+                mm(cnt, A("TM", 128 * r, 128 * r + 128), A("E", r, 16 * 272, 272), r == 0, False)
+            merge(16)
+            mm(A("pc", 16, 32), A("If", 0, 128), A("nW", 128, 144), False, False)
+            conv("pc", 0, "Q16", "HC", 512, start=False)
+            at("seat")
+            tt(A("q0", 1, 32, 2), cnt, A("thr", 0, 16), LT)
+            ts(wv(17), A("pc", 16, 32), 0.0, EQ)
+            tt(A("q0", 33, 64, 2), cnt, A("thr", 0, 16), LT)
+            merge(3)
+        if not last:
+            ts(A("q0", 97, 128, 2), cnt, 0.5, LT)
+        tt(A("q0", 65, 96, 2), wv(17), A("q0", 1, 32, 2), MUL)
+        a = 64 if OPT["sc"] == 2 else 0
+        scan(A("q2", a, n), A("q0", a, n), A("q1", a, n), MUL, ADD)
+        ts(A("sl", 64 * t + a // 2, 64 * t + n // 2), A("q2", a + 1, n, 2), MID, ADD)
         sl = lambda j, t=t: A("sl", 64 * t + 16 * j, 64 * t + 16 * j + 16)
+
+        def parents():
+            at("par")
+            tt(I(KINS, sl(1)), A("KWn", 256, 512), A("nrow"), MAX)
+
+        if OPT["pf"] == 2 or last:
+            parents()
         at("KN")
         if last:
-            act(A("KS"), I(A("KWn"), sl(0)))
-            act(A("XS"), I(A("XWn", xw, xw + 768), sl(0)))
+            act(A("KS"), I(A("KWn"), sl(0)), func=ACT.Abs)
+            at("XC")
+            lin("XS", A("XS"), I(A("XWn", xw, xw + 512), sl(0)))
             dma("Y", ext("yk", 256 * r_, 256 * r_ + 256), A("KS"), 3000)
             dma("Y", ext("yx", 256 * r_, 256 * r_ + 256), A("XS"), 3000)
         else:
-            act(A("KN", lo, lo + 256), I(A("KWn"), sl(0)))
+            act(A("KN", lo, lo + 256), I(A("KWn"), sl(0)), func=ACT.Abs)
             at("XC")
-            (cp if OPT["xc"] else act)(A("XC", lo, lo + 256), I(A("XWn", xw, xw + 768), sl(0)))
-            dma("Y", A("X", lo, lo + 256), A("XC", lo, lo + 256))
+            lin("XC", XC(lo, lo + 256), I(A("XWn", xw, xw + 512), sl(0)))
+            if OPT["xx"] == "G":
+                asel(X(lo, lo + 256), XC(lo, lo + 256), [[0, 256]], 0, 0)
+            else:
+                cp(X(lo, lo + 256), XC(lo, lo + 256))
+            if OPT["pf"] == 1:
+                parents()
             early_kin(t + 1)
-        at("par")
-        if OPT["cm"]:
-            cp(I(KINS, sl(1)), A("colM"))
-        else:
-            tt(I(KINS, sl(1)), A("colM"), A("nrow", 256 * r_, 256 * r_ + 256), ADD)
+            if OPT["pf"] == 0:
+                parents()
         at("FT")
-        (cp if OPT["ft"] else act)(A("KN", fl, fl + 256), I(A("FWn"), sl(0)))
+        tt(A("fw"), wv(15), A("q2", 33, 64, 2), MIN)
+        mm(A("pn", 0, 256), A("Im"), A("g16", 0, 256), True, False)
+        for r in range(16):
+            mm(A("pn", r, 256, 16), A("If", r, r + 128), A("fw"), False, r == 15)
+        merge(16)
         at("foot")
-        cp(I(FEET, sl(3)), nG)
+        up = lo if last else lo + UP
+        scatter("foot", I(FEET, sl(2)), A("ID", up, up + 256))
+        at("FT")
+        tt(A("KN", fl, fl + 256), A("KN", fl, fl + 256), A("pn", 0, 256), ADD)
         at("Aout")
         if not last:
-            mm(A("pw", 32, 48), A("ones", 0, 128), live, True, False)
-            mm(A("pw", 32, 48), A("onef"), A("q0", 1, 32, 2), False, True)
+            mm(A("pc", 32, 48), A("ones", 0, 128), live, True, False)
+            mm(A("pc", 32, 48), A("onef"), A("q0", 1, 32, 2), False, True)
             merge(2)
-            act(wv(21), A("pw", 32, 48), bias=-15.5 / 16, accum=A("aout", 8 * t, 8 * t + 1))
+            act(wv(21), A("pc", 32, 48), bias=-15.5 / 16, accum=A("aout", 8 * t, 8 * t + 1))
             pa = (A("ain", 8 * t + 8, 8 * t + 16), A("aout", 8 * t, 8 * t + 8))
-            send(nxt, [pa] if t == VIS - 2 else [pa, (A("oin", 16 * t + 16, 16 * t + 32), sl(2))], HOP)
+            send(nxt, [pa] if t == VIS - 2 else [pa, (A("oin", 16 * t + 16, 16 * t + 32), sl(3))], HOP)
         else:
             for h in (1, 0):
                 at("t%d" % h)
-                bb, a = A("bb", 128 * h, 128 * h + 128), 64 * t - 32 + 8 * h
+                bb, a = A("bb", 128 * h, 128 * h + 128), 64 * t - 16 + 8 * h
                 act(bb, I(A("ID"), bi(h)))
                 cp(I(A("TT"), A("sl", a, a + 8)), bb)
             dma("Y", ext("yt"), A("TT", 0, W_, 1, row0), 3000)
@@ -921,7 +969,7 @@ def polish(ops, start, rounds):
         du = [0.0 if o["k"] == "r" else fig[8] * len(o["f"]) if o["k"] == "d" else c[i] for i, o in enumerate(ops)]
         lag = [[(j, c[j] + (fig[7] if ops[j]["e"] == o["e"] else fig[6]) if w else du[j]) for j, w in deps[i].items()]
                for i, o in enumerate(ops)]
-        cases.append((c, du, lag))
+        cases.append((c, du + [0.0], lag))
     name, seen = [], {}
     for o in ops:
         k = (o["e"], o["b"], o["v"])
@@ -932,34 +980,45 @@ def polish(ops, start, rounds):
     final = [i for i in range(n) if i not in needed]
     queue = ["VSPGYR".index(o["e"]) for o in ops]
 
-    def timed(order, than=None, slack=0.0):
-        prev, last = [-1] * n, [-1] * 6
+    def timed(order, first=0, than=None, slack=0.0, grow=1.0):
+        prev, last = [n] * n, [n] * 6
         for i in order:
             e = queue[i]
             if e < 5:
                 prev[i] = last[e]
                 last[e] = i
         total, runs = 0.0, []
-        for c, du, lag in cases:
-            at, why = [0.0] * n, [-1] * n
-            for i in order:
-                p = prev[i]
-                s = at[p] + du[p] if p >= 0 else 0.0
-                for j, l in lag[i]:
-                    if at[j] + l > s:
-                        s = at[j] + l
-                        p = j
-                at[i], why[i] = s, p
+        parts = [order[first:first + LOOK], order[first + LOOK:]]
+        for m, (c, du, lag) in enumerate(cases):
+            at, why = (than[1][m][0][:], than[1][m][1][:]) if first else ([0.0] * (n + 1), [n] * n)
+            for rest in parts:
+                for i in rest:
+                    p = prev[i]
+                    s = at[p] + du[p]
+                    for j, l in lag[i]:
+                        l += at[j]
+                        if l > s:
+                            s = l
+                            p = j
+                    at[i] = s
+                    why[i] = p
+                if than and rest is parts[0] and parts[1]:
+                    old = than[1][m][0]
+                    late = min(at[i] - old[i] for i in rest[-12:])
+                    if total + late * grow > (than[1][m - 1][4] if m else 0) + slack + EARLY:
+                        return None
             end, i = max((at[i] + c[i], i) for i in final)
             worth = end + MEAN * sum(at) / n
             total += worth
-            runs.append((at, why, i, end, worth))
-            if than and total > sum(x[4] for x in than[1][:len(runs)]) + slack + (SLACK if len(runs) < len(cases) else 0):
+            runs.append((at, why, i, end, total))
+            if than and total > than[1][m][4] + slack + (SLACK if m + 1 < len(cases) else 0):
                 return None
         return total, runs, prev
 
     order = sorted(range(n), key=lambda i: (start[i], i))
     now = best = timed(order)
+    place = {i: k for k, i in enumerate(order)}
+    lines = [[i for i in order if queue[i] == e] for e in range(6)]
     seed = [SEED]
 
     def draw(m):
@@ -970,38 +1029,196 @@ def polish(ops, start, rounds):
         at, why, i = now[1][draw(len(cases))][:3]
         if draw(100) < ANY:
             i = draw(n)
-        pairs = []
-        while i >= 0:
-            if why[i] >= 0 and why[i] == now[2][i] and not above[i] >> why[i] & 1:
-                pairs.append((why[i], i))
-            i = why[i]
+        pairs, prev = [], now[2]
+        while i < n:
+            p = why[i]
+            if p < n and p == prev[i] and not above[i] >> p & 1:
+                pairs.append((p, i))
+            i = p
         if not pairs:
             continue
-        u, v = pairs[draw(len(pairs) if pairs[0][1] in final or why[pairs[0][1]] < 0 else min(len(pairs), NEAR))]
-        q = [i for i in order if queue[i] == queue[u]]
+        u, v = pairs[draw(len(pairs))]
+        q = lines[queue[u]]
         far, ahead, a = (0, 0, 1, 2, 3, 5, 8, 13, 21, 34)[draw(10)], draw(2), (u, v)[draw(2)]
         far += (a == v) != ahead
         b = q[max(q.index(u) - far, 0)] if ahead else q[min(q.index(v) + far, len(q) - 1)]
         alone = min(name[a][2], name[b][2]) < 1 or (name[a][2] == VIS - 1 and draw(2))
-        new = list(order)
+        new, first = list(order), n
         for d in (0,) if alone else range(-VIS, VIS + 1):
             x, y = (index.get(name[z][:2] + (name[z][2] + d, name[z][3])) for z in (a, b))
             if x is None or y is None or (d and min(name[x][2], name[y][2]) < 1):
                 continue
-            i, j = new.index(x), new.index(y)
+            i, j = (place[x], place[y]) if first == n else (new.index(x), new.index(y))
             if ahead and j < i:
+                up = above[x] | 1 << x
                 part = new[j:i + 1]
-                new[j:i + 1] = sorted(part, key=lambda k: k != x and not above[x] >> k & 1)
+                new[j:i + 1] = [k for k in part if up >> k & 1] + [k for k in part if not up >> k & 1]
             elif not ahead and i < j:
                 part = new[i:j + 1]
                 new[i:j + 1] = sorted(part, key=lambda k: k == x or above[k] >> x & 1)
-        trial = timed(new, now, SLACK * (1 - r / rounds))
+            first = min(first, i, j)
+        if new == order:
+            continue
+        trial = timed(new, first, now, SLACK * (1 - r / rounds), 1.5 if alone else 1.5 * (n - first) / LOOK)
         if trial:
             now = trial
-            order = sorted(new, key=lambda k: trial[1][0][0][k])
+            at = trial[1][0][0]
+            order = sorted(new, key=lambda k: at[k])
+            place = {i: k for k, i in enumerate(order)}
+            lines = [[i for i in order if queue[i] == e] for e in range(6)]
             if now[0] < best[0]:
                 best = now
-    return best[1][0][0], [int(x[3]) for x in best[1]]
+    return best[1][0][0][:n], [int(x[3]) for x in best[1]]
+
+
+def improve(ops, start, rounds, CASES, SLACK):
+    n = len(ops)
+    above, deps = [], []
+    for i, o in enumerate(ops):
+        far = 0
+        for j in o["dep"]:
+            far |= above[j]
+        deps.append({j: w for j, w in o["dep"].items() if ops[j]["k"] != "c" or not far >> j & 1})
+        for j in o["dep"]:
+            far |= 1 << j
+        above.append(far)
+    cases = []
+    for fig in CASES:
+        c = [sum(a * b for a, b in zip(o["cv"], (1.0,) + fig[:6])) for o in ops]
+        du = [0.0 if o["k"] == "r" else fig[8] * len(o["f"]) if o["k"] == "d" else c[i] for i, o in enumerate(ops)]
+        lag = [[(j, c[j] + (fig[7] if ops[j]["e"] == o["e"] else fig[6]) if w else du[j]) for j, w in deps[i].items()]
+               for i, o in enumerate(ops)]
+        cases.append((c, du + [0.0], lag))
+    name, seen = [], {}
+    for o in ops:
+        k = (o["e"], o["b"], o["v"])
+        seen[k] = seen.get(k, 0) + 1
+        name.append(k + (seen[k],))
+    index = {k: i for i, k in enumerate(name)}
+    needs = [list(d) for d in deps]
+    needed = set(j for d in deps for j in d)
+    final = [i for i in range(n) if i not in needed]
+    queue = ["VSPGYR".index(o["e"]) for o in ops]
+    seed = [SEED]
+
+    def draw(m):
+        seed[0] = (seed[0] * 1103515245 + 12345) % 2147483648
+        return (seed[0] >> 8) % m
+
+    def place(key, old, least):
+        c, du, lag = cases[0]
+        order = sorted(range(n), key=lambda i: key[i])
+        begin, end = [[] for _ in range(6)], [[] for _ in range(6)]
+        at = old[:]
+        for i in order:
+            d = du[i]
+            if key[i] < least:
+                if d:
+                    begin[queue[i]].append(at[i])
+                    end[queue[i]].append(at[i] + d)
+                continue
+            s = 0.0
+            for j, l in lag[i]:
+                l += at[j]
+                if l > s:
+                    s = l
+            if d:
+                a, b = begin[queue[i]], end[queue[i]]
+                p = m = len(b)
+                while p and b[p - 1] > s:
+                    p -= 1
+                while p < m and s + d > a[p]:
+                    if b[p] > s:
+                        s = b[p]
+                    p += 1
+                a.insert(p, s)
+                b.insert(p, s + d)
+            at[i] = s
+        return at
+
+    def timed(at0, than, slack):
+        total = max(at0[i] + cases[0][0][i] for i in final) + MEAN * sum(at0) / n
+        if than and total > than[1][0][4] + slack + SLACK:
+            return None
+        order = sorted(range(n), key=lambda i: at0[i])
+        prev, last = [n] * n, [n] * 6
+        for i in order:
+            e = queue[i]
+            if e < 5:
+                prev[i] = last[e]
+                last[e] = i
+        runs = [(0, 0, 0, 0, total)]
+        if than and len(cases) == 1 and total > than[0] + slack:
+            return None
+        for m in list(range(1, len(cases))) + [0]:
+            c, du, lag = cases[m]
+            at, why = [0.0] * (n + 1), [n] * n
+            for i in order:
+                p = prev[i]
+                s = at[p] + du[p]
+                for j, l in lag[i]:
+                    l += at[j]
+                    if l >= s:
+                        s = l
+                        p = j
+                at[i] = s
+                why[i] = p
+            end, i = max((at[i] + c[i], i) for i in final)
+            if m == 0:
+                runs[0] = (at, why, i, end, runs[0][4])
+                break
+            total += end + MEAN * sum(at) / n
+            runs.append((at, why, i, end, total))
+            if than and total > than[1][m][4] + slack + (SLACK if m + 1 < len(cases) else 0):
+                return None
+        return total, runs, prev
+
+    now = best = timed(place(start, [0.0] * (n + 1), -1.0), None, 0)
+    for r in range(rounds):
+        old = now[1][0][0]
+        key = old[:]
+        why, i = now[1][draw(len(cases))][1:3]
+        if draw(100) < ANY:
+            i = draw(n)
+        pairs, prev = [], now[2]
+        while i < n:
+            p = why[i]
+            if p < n and p == prev[i] and not above[i] >> p & 1:
+                pairs.append((p, i))
+            i = p
+        if draw(100) < FREE:
+            a, d = draw(n), (-1500, -800, -400, -200, -100, 100, 200, 400, 800, 1500)[draw(10)]
+        elif pairs:
+            u, v = pairs[draw(len(pairs))]
+            d = key[v] - key[u] + (1, 1, 200, 500, 1000)[draw(5)]
+            a, d = ((u, d), (v, -d))[draw(2)]
+        else:
+            continue
+        k = name[a]
+        alone = k[2] < 1 or (k[2] == VIS - 1 and draw(10) < 4)
+        least = 1e9
+        for x in [a] if alone else [index[z] for z in [k[:2] + (v, k[3]) for v in range(1, VIS)] if z in index]:
+            least = min(least, key[x], key[x] + d)
+            key[x] += d
+            todo = [x] if d < 0 else []
+            while todo:
+                y = todo.pop()
+                for j in needs[y]:
+                    if key[j] > key[y] - 1:
+                        key[j] = key[y] - 1
+                        least = min(least, key[j])
+                        todo.append(j)
+        if d > 0:
+            for i in range(a if alone else index.get(k[:2] + (1, k[3]), 0), n):
+                for j in needs[i]:
+                    if key[j] >= key[i]:
+                        key[i] = key[j] + 0.01
+        trial = timed(place(key, old, least), now, SLACK * (1 - r / rounds))
+        if trial:
+            now = trial
+            if now[0] < best[0]:
+                best = now
+    return best[1][0][0][:n], [int(x[3]) for x in best[1]]
 
 
 def emit(g, T, ops, start):
@@ -1086,5 +1303,8 @@ def rank_program(g, core, T, topo):
     ops = build(T, topo, core, rank)
     start = plan(ops)[0]
     if not PLAN:
-        PLAN.append(polish(ops, start, ROUNDS)[0])
-    emit(g, T, ops, polish(ops, PLAN[0], 0)[0])
+        PLAN.append(polish(ops, improve(ops, start, FIRST, [PLACE], 40)[0], ROUNDS)[0])
+    start = list(PLAN[0])
+    for i, o in enumerate(ops):
+        start[i] = max([start[i]] + [start[j] + 0.01 for j in o["dep"]])
+    emit(g, T, ops, polish(ops, start, 0)[0])

@@ -1,4 +1,3 @@
-import numpy as np
 from concourse.bass import DstId, RemoteDMATransfer
 from concourse.mybir import AluOpType as ALU, ActivationFunctionType as ACT
 
@@ -10,46 +9,82 @@ UP = 1024
 MID = 1792.0
 WT = 2176.0
 BIG = 12582912.0
-SPLIT = [[(0, 32, 2), (0, 32, 2)], [(0, 48, 1), (0, 48, 2)]]
-SPLIT0 = [[(0, 64, 2), (0, 32, 2)], [(0, 48, 1), (0, 48, 2)]]
-FCUT, VCUT, SCUT = 64, (32, 64), (64, 64)
-OPT = {"pf": 2, "xp": 1, "xx": "G", "tu": 16, "h0": 0, "tm": 1, "vd": 1, "t1": 0, "sc": 1}
-SCALAR = "v0 v1 kb0 kb1 t0 t1 hit brow1 brow0 kin01 colY xs0 xs1 lvN wt stay foot gy fu turn down"
-BOOST = {}
-PASSES = 1
+SPLIT = [[[(48, 2), (48, 2)], [(48, 1), (48, 2)]], [[(48, 2), (32, 2)], [(48, 1), (56, 2)]]]
+CUT = (64, 96)
+BANKS = [[("pn", "pd"), ("pc", "pw")], [("pd",), ("pw", "pc")]]
+GFILL = "KN nrow aout o0 q0 onef dq"
+KCUT = (2560, 3584, 0, 1024, 1024, 2048, 2048, 2560)
+SCALAR = "v0 v1 t0 t1 hit kin01 colY xs0 xs1 lvN wt stay foot gy fu turn down kn0 kn2560 bb0 bb1 T0 T1"
+ORDER = {
+    "V": ["""ones- Z- t16- ci- cf- Z-.4 cf-.6 cw- BD- cf- b16- cf-.5 CK- cf- Ib- ftf- yu cf- cu- Z- tmpb- PH- v16- Pm-
+          PF- PF0- RE- KN- KN- yu yu py t1- CK- live t0- live kin00 CK- held wts CK- held kin00 held kin01- held
+          gv01 p16 gv00 A01 p16 B01 xp A00 xp B00 trf- dec01 turn dec01 turn dec01 dec00 turn stay dec00 dec01 stay
+          kin11 dec00 kin11 gv11 dec00 stay kin10 BO- kin10 gv10 A11 B11 C11 A10 B10 dec11 dec11 Dq- dec11 dec10 Z-
+          dec10 dec11 dec10 brow1 E8 dec10 E12 brow0 zn1 E0 may E3 vl E6 vl zn0 may.3 cnt may seat seat hit seat seat
+          seat FT par""",
+          """yu XC- FT- t1- yu yu py t0- kin01- live kin00 live gv01 held wts held held kin00 held Ain p16 A01 gv00 p16
+          B01 xp A00 xp B00 dec01 turn dec01 turn dec01 dec00 dec01 dec00 stay kin11 dec00 stay kin11 gv11 dec00 stay
+          kin10 turn kin10 gv10 A11 B11 C11 A10 B10 dec11 dec11 dec11 dec10 dec10 dec11 dec10 brow1 E8 dec10 E12
+          brow0 may E0 zn1 E3 vl E6 vl may zn0 may cnt seat seat hit seat seat seat FT par""",
+          """yu XC- FT- t1- yu yu py t0- kin01- live kin00 live gv01 held wts held held kin00 held Ain p16 A01 gv00 p16
+          B01 xp A00 xp B00 dec01 turn dec01 turn dec01 home- dec00 dec01 dec00 stay kin11 dec00 stay kin11 gv11
+          dec00 stay kin10 turn kin10 gv10 A11 B11 C11 A10 B10 dec11 dec11 dec11 dec10 dec10 dec11 dec10 brow1 E8
+          dec10 E12 brow0 E0 may E3 vl vl E6 may zn0 zn1 may cnt seat hit seat seat seat FT par T1 XC T0 FT"""],
+    "S": ["""fsd- bsd- cq- d0- zin- CB- q1- o1- cw- c64- I1- t16- In- KN- KN-.3 cf- I8- e16- ZN- KN- yu I0- ZN- nW- CB-
+          fu live kin01- Pf-.2 wts colY ZN- SH- Pf- d0- wts gs01 gs00 C01 D01 C00 D00 c17- Ih- stay gs11 gs10 D11 C10
+          D10 turn zn1 v1 v0 Im- zn0 may may hit v0 Aout t1 foot""",
+          """yu t0- KN- kin01- live fu colY wts gs01 gs00 Ain C01 Ain D01 C00 D00 wts stay gs11 gs10 D11 C10 D10 turn
+          v1 zn1 v0 zn0 may T1 may T1 hit T0 v0 T0 Aout t1 foot""",
+          """yu t0- KN- kin01- live fu colY wts gs01 gs00 Ain C01 Ain D01 C00 D00 wts stay gs11 gs10 D11 C10 D10 turn
+          v1 down.2 v0 zn0 zn1 down may hit may v0 T1 foot T0 KN out out out out"""],
+    "P": ["""pd- pd- colY t0- yu t1- pd- colY held held kin00 kin00 kin01- kin01- D01 z01 key00 key01 C01 z00 C00 neg01
+          neg00 p16 C01 D01 neg01 A01 D00 C00 C01 D00 B01 D01 neg00 par01 dec01 A00 C00 B00 D00 par00 dec00 dec01 D11
+          dec01 dec00 D10 C10 key11 z11 dec00 z10 key11 key10 key11 neg11 key10 key10 D11 neg10 neg11 A11 C10 D10 D11
+          B11 C11 neg10 A10 C10 B10 D10 dec11 dec11 dec10 zn1 zn0 E8 dec10 zn1 E8 E12 vl zn0 E0 E3 E6 hit Aout FT FT
+          t1""",
+          """colY yu t0- kin01- kin01- C01 colY kin00 held held z01 kin00 key01 D01 z00 neg01 key00 C01 neg00 p16 D01
+          neg01 A01 D00 C00 C00 C01 D00 B01 D01 par01 dec01 neg00 A00 C00 B00 D00 par00 dec00 dec01 dec01 z10 D11 C10
+          dec00 z11 dec00 D10 key11 key11 key10 key11 neg11 neg11 D11 key10 key10 C10 D10 neg10 A11 D11 B11 C11 neg10
+          A10 C10 B10 D10 dec11 E8 dec11 zn0 zn1 dec10 dec10 E8 zn1 E12 vl E0 zn0 E3 E6 hit Aout FT FT t1""",
+          """colY yu t0- kin01- kin01- C01 colY kin00 held held z01 kin00 key01 D01 z00 neg01 key00 C01 neg00 p16 neg01
+          A01 D01 D00 C00 C00 D00 C01 B01 D01 par01 dec01 neg00 A00 C00 B00 D00 par00 dec00 dec01 dec01 z10 D11 C10
+          dec00 z11 dec00 key11 key11 D10 key10 key11 neg11 neg11 D11 key10 key10 C10 D10 neg10 A11 D11 B11 C11 neg10
+          A10 C10 B10 D10 dec11 E8 dec11 zn0 dec10 zn1 dec10 E8 E12 vl E0 zn0 E3 zn1 E6 hit FT FT"""],
+    "G": ["""ci- tmpc-.3 tmpc-.4 If- KN-.4 KN-.3 KN-.2 KN-.5 tmpb- tmpc- tmpc- Qh- KN-.6 KN- CK- far- o0- SF- zp1 ID-.6
+          PH0-.2 PH0- zp1.3 onef- zp1.4 zp0.4 aout- dq- zp0 zp0 zp1 q0- ID-.2 zp0 ID-.5 nup trf- ID-.3 stay ID-.4
+          ID-.7 dq- ID- BL- dq- dec11 dq- nrow- dec10 zn1 zn0 may Aout far XC""",
+          "zp0 zp1.2 zp0.4 zp1 zp1 zp0.3 zp1 zp0 stay dec11 dec10 nup zn1 may zn0 Aout far XC",
+          "zp1.2 zp0 zp0.4 zp1 zp1 zp0.3 zp1 zp0 stay home- dec11 dec10"],
+    "Y": ["kst- kst- kst- kst- XX- XX- trs- XX- TT yu p16 colY TT p16",
+          "colY p16.2 yu p16",
+          "down.6 colY down.4 home- down.2 down down.5 p16.2 yu down p16 home- XC.2 XC out out zn0"],
+}
 
 SB, F32, BF, F16, I32, U16 = "sbuf", "float32", "bfloat16", "float16", "int32", "uint16"
 SCRATCH = {}
-for _d, _l in ((I32, "kst 3856 fsd 64 bsd 16 trs 224 trt 224 ci 8 R 544 Di 32"),
-               (F32, "KN 5152 ID 4608 TT 3856 trf 224 ftf 64 onef 128 tmpc 256 cf 40 cw 96 c17 16 d0 272 "
-                     "ain 40 aout 40 acc 8 colY 256 dq 256 I32 128 yrow 256 nrow 256 KS 256 "
-                     "KWn 512 bb 256 thr 48 Pf 256 w 512 q0 128 q1 128 q2 128 o0 64 o1 64 o2 64"),
-               (BF, "XX 7424 ones 272 BO 128 I15 128 Ib 128 Ih 128 In 128 I8 128 Pm 128 Qb 144 Qa 144 TM 2048 BD 48 CK 544 CB 272 "
-                    "RE 64 cq 256 tmpb 272 zin 1280 zp 256 x0b 2048 x1b 2048 m0b 2048 m1b 2048 "
-                    "xs 256 D 32 Z 1152 E 4352 XS 256 XWn 2560 xp 256 mp 256 lv 16 c64 24 ZR 2176 zr 4096"),
-               (F16, "Qh 144 Q16 144 HC 512 If 144 Im 128 I0 128 I1 128 SH 16 SF 8 PH 272 PH0 272 PF 136 PF0 136 g16 512 e16 512 v16 256 t16 256 "
-                     "p16 256 c16 256 nW 144 brow 256 b16 16 fw 16"),
-               (U16, "cu 32 bin 80 oin 80 bU 32 bO 80 cU 256 u 256 sl 320")):
+for _d, _l in ((I32, "kst 3584 fsd 64 bsd 16 trs 224 ci 8 R 544 Di 32"),
+               (F32, "KN 5152 ID 3584 nup 256 TT 3856 trf 224 trt 224 trh 224 ftf 64 onef 128 tmpc 256 cf 40 cw 96 c17 16 d0 272 "
+                     "ain 40 aout 40 acc 8 colY 256 dq 256 yrow 256 nrow 256 KS 256 "
+                     "KWn 512 bb 256 thr 16 Pf 256 w 512 q0 128 q1 128 q2 128 o0 64 o1 64 o2 64"),
+               (BF, "XX 7424 ones 272 BO 128 BL 128 Dq 256 Ib 128 Ih 128 In 128 I8 128 BD 48 CK 544 CB 272 "
+                    "RE 64 Pm 128 zp 256 cq 128 tmpb 272 zin 1280 x0b 2048 x1b 2048 m0b 2048 m1b 2048 "
+                    "xs 256 D 32 Z 1152 E 4352 XS 256 XWn 2560 xp 256 mp 256 lv 16 c64 24 ZN 1088"),
+               (F16, "Qh 144 HC 256 If 144 Im 128 I0 128 I1 128 SH 16 SF 8 PH 272 PH0 272 PF 136 PF0 136 "
+                     "g16 512 e16 512 v16 256 t16 256 p16 256 c16 256 nW 64 brow 256 b16 16 fw 16"),
+               (U16, "cu 4 bin 80 oin 80 bU 32 bO 80 cU 256 u 256 sl 320")):
     _l = _l.split()
     for _n, _c in zip(_l[::2], _l[1::2]):
         SCRATCH[_n] = (SB, [128, int(_c)], _d)
-for _n, _d in (("tin", I32), ("tback", F32)):
-    SCRATCH[_n] = ("dram", [128, 224], _d)
+for _n in ("tin", "tback"):
+    SCRATCH[_n] = ("dram", [128, 224], F32)
 for _n in ("pk0", "pk1", "pz0", "pz1", "pd", "pw", "pc", "pn"):
     SCRATCH[_n] = ("psum", [128, 512], F32)
 SEMAPHORES = ["eV", "eS", "eP", "eG", "sent"] + ["d%d" % i for i in range(80)] + ["r%d" % i for i in range(36)]
 
-GA, SC, PE, HOP, XW, SW, FIX, DL = 1.56, 3.8, 0.55, 4000, 130, 80, 25, 2600
-CASES = [(1.56, 3.8, 0.55, 20, 3000, 2600, 140, 80, 80), (2.0, 5.5, 0.5, 10, 2600, 2000, 110, 60, 60),
-         (1.3, 3.0, 0.65, 35, 7000, 4000, 200, 100, 200), (1.1, 1.8, 0.5, 20, 3500, 2600, 320, 160, 80)]
-PLACE = (1.56, 3.8, 0.55, 20, 4500, 3200, 150, 80, 100)
-FIRST, ROUNDS, SLACK, SEED, PLAN = 42000, 70000, 200, 3, []
-MEAN, ANY, LOOK, EARLY, FREE = 1.0, 30, 300, 1e9, 10
-
 
 def build(T, topo, core, rank):
     ops = []
-    tag = ["init", -1]
+    tag = [None, -1]
     N = len(T.cores)
     nxt, prv = T.cores[(rank + 1) % N], T.cores[(rank - 1) % N]
 
@@ -58,17 +93,17 @@ def build(T, topo, core, rank):
             b = SCRATCH[name][1][1]
         ps = slice(None) if p is None else slice(*p)
         ap = T[name][ps, a:b] if s == 1 else T[name][ps, a:b:s]
-        part = (name, 0, W_ + UP) if name == "ID" and tag[1] >= 0 else (name, a, b)
-        return (ap, [part], len(range(a, b, s)), SCRATCH[name][2], SCRATCH[name][0])
+        return (ap, [(name, a, b)], len(range(a, b, s)), SCRATCH[name][2], False)
 
     def I(win, off):
-        return (win[0].indirect(off[0]), win[1] + off[1], off[2] * 16, win[3], "ind", off[1])
+        return (win[0].indirect(off[0]), win[1] + off[1], off[2] * 16, win[3], True, off[1])
 
-    def add(eng, fn, r, w, cost, kind="c", extra=None):
-        cv = list(cost) + [0] * (7 - len(cost))
-        cost = sum(a * b for a, b in zip(cv, (1, GA, SC, PE, FIX, HOP, DL)))
-        ops.append({"e": eng, "f": [fn], "r": r, "w": w, "c": float(cost), "cv": cv, "k": kind, "x": extra,
-                    "b": tag[0], "v": tag[1]})
+    def parts(ap, names, a, b):
+        return (ap[0], [(n, a, b) for n in names]) + ap[2:]
+
+    def add(eng, fn, r, w, kind="c", extra=None):
+        ops.append({"e": eng, "f": [fn], "r": r, "w": w, "k": kind, "x": extra,
+                    "b": tag[0] or (w or r)[0][0], "v": tag[1]})
         return len(ops) - 1
 
     def at(name, t=None):
@@ -82,103 +117,72 @@ def build(T, topo, core, rank):
             o["f"] = o["f"] + p["f"]
             o["r"] = o["r"] + [x for x in p["r"] if x not in o["r"]]
             o["w"] = o["w"] + [x for x in p["w"] if x not in o["w"]]
-            more = [100] + [0] * 6 if o["k"] == "d" else p["cv"]
-            o["c"] += 100 if o["k"] == "d" else p["c"]
-            o["cv"] = [a + b for a, b in zip(o["cv"], more)]
         del ops[len(ops) - n + 1:]
-
-    chains = {}
-
-    def chain(key):
-        if key in chains:
-            ops[-1]["after"] = chains[key]
-        chains[key] = len(ops) - 1
 
     def rw(out, ins):
         r = []
         for i in ins:
             if isinstance(i, tuple):
                 r = r + i[1]
-        if out[4] == "ind":
-            return r + out[5], out[1][:1]
-        return r, out[1]
-
-    def vcost(out, in0, in1=None):
-        if out[4] == "ind":
-            return (60, 0, out[2])
-        if in0[4] == "ind":
-            return (60, out[2])
-        n = out[2]
-        if in1 is not None:
-            n = n * (2 if in0[4] == SB and in1[4] == SB else 1)
-        elif out[3] not in (F32, I32) and in0[3] not in (F32, I32):
-            n = n / 2
-        return (max(64, n), 0, 0, 0, 1)
+        return (r + out[5], out[1][:1]) if out[4] else (r, out[1])
 
     def sv(s):
         return s[0] if isinstance(s, tuple) else s
 
     def cp(out, in_):
-        r, w = rw(out, [in_])
-        add("V", lambda q: q.tensor_copy(out[0], in_[0]), r, w, vcost(out, in_))
+        add("V", lambda q: q.tensor_copy(out[0], in_[0]), *rw(out, [in_]))
 
     def tt(out, in0, in1, op):
-        r, w = rw(out, [in0, in1])
-        add("V", lambda q: q.tensor_tensor(out[0], in0[0], in1[0], op), r, w, vcost(out, in0, in1))
+        add("V", lambda q: q.tensor_tensor(out[0], in0[0], in1[0], op), *rw(out, [in0, in1]))
 
     def ts(out, in0, s1, op0, s2=None, op1=None):
-        r, w = rw(out, [in0, s1, s2])
         if op1 is None:
             f = lambda q: q.tensor_scalar(out[0], in0[0], sv(s1), None, op0)
         else:
             f = lambda q: q.tensor_scalar(out[0], in0[0], sv(s1), sv(s2), op0, op1)
-        add("V", f, r, w, vcost(out, in0))
+        add("V", f, *rw(out, [in0, s1, s2]))
 
     def ms(out, val):
-        add("V", lambda q: q.memset(out[0], val), [], out[1], (max(64, out[2] * (1 if out[3] in (F32, I32) else 0.5)),))
+        add("V", lambda q: q.memset(out[0], val), [], out[1])
 
     def scan(out, a, b, op0, op1):
-        r, w = rw(out, [a, b])
-        add("V", lambda q: q.tensor_tensor_scan(out[0], a[0], b[0], 0.0, op0, op1), r, w, (max(64, out[2]), 0, 0, 0, 1))
+        add("V", lambda q: q.tensor_tensor_scan(out[0], a[0], b[0], 0.0, op0, op1), *rw(out, [a, b]))
 
-    def act(out, in_, bias=0.0, scale=1.0, func=None, accum=None):
+    def act(out, in_, bias=0.0, scale=1.0, func=ACT.Identity, accum=None):
         r, w = rw(out, [in_, bias, scale])
-        fu = ACT.Identity if func is None else func
-        if out[4] == "ind":
-            add("S", lambda q: q.activation(out[0], in_[0], fu), r, w, (80, 0, out[2]))
-            return
-        if accum is None:
-            f = lambda q: q.activation(out[0], in_[0], fu, bias=sv(bias), scale=sv(scale))
+        if out[4]:
+            f = lambda q: q.activation(out[0], in_[0], func)
+        elif accum is None:
+            f = lambda q: q.activation(out[0], in_[0], func, bias=sv(bias), scale=sv(scale))
         else:
             w = w + accum[1]
-            f = lambda q: q.activation(out[0], in_[0], fu, bias=sv(bias), scale=sv(scale), accum_out=accum[0])
-        add("S", f, r, w, (80, out[2]) if in_[4] == "ind" else (max(64, out[2]) + 30, 0, 0, 0, 1))
+            f = lambda q: q.activation(out[0], in_[0], func, bias=sv(bias), scale=sv(scale), accum_out=accum[0])
+        add("S", f, r, w)
 
     def mm(out, lhsT, rhs, start, stop):
-        c = (0, 0, 0, max(min(64, lhsT[2]), rhs[2]) * (4 if lhsT[3] == F32 else 1))
-        add("P", lambda q: q.matmul(out[0], lhsT[0], rhs[0], start, stop), lhsT[1] + rhs[1], out[1], c)
+        add("P", lambda q: q.matmul(out[0], lhsT[0], rhs[0], start, stop), lhsT[1] + rhs[1], out[1])
 
     def iota(out, pat, base, cm):
         if out[3] == I32:
             f = lambda q: q.iota(out[0], pat, base, cm)
         else:
             f = lambda q: q.iota(out[0], pat, base, cm, allow_small_or_imprecise_dtypes=True)
-        add("G", f, [], out[1], (160 + 2 * out[2],))
+        add("G", f, [], out[1])
 
     def asel(out, in_, pat, base, cm, op=ALU.is_equal, other=0.0):
-        add("G", lambda q: q.affine_select(out[0], in_[0], pat, op, other, base, cm), in_[1], out[1], (200 + 2 * out[2],))
+        add("G", lambda q: q.affine_select(out[0], in_[0], pat, op, other, base, cm), in_[1], out[1])
 
-    def dma(eng, out, in_, cost=2600):
-        add(eng, lambda q: q.dma_start(out[0], in_[0]), in_[1], out[1], (cost - 2600, 0, 0, 0, 0, 0, 1), "d")
+    def dma(eng, out, in_):
+        add(eng, lambda q: q.dma_start(out[0], in_[0]), in_[1], out[1], "d")
 
     def ext(name, a=None, b=None, rows=slice(None)):
         if a is None:
-            return (T[name][:], [(name, 0, 1)], 0, "", "hbm")
-        return (T[name][rows, a:b], [(name, a, b)], 0, "", "hbm")
+            return (T[name][:], [(name, 0, 1)])
+        return (T[name][rows, a:b], [(name, a, b)])
 
     nr = [0]
 
-    def send(dst, pairs, cost):
+    def send(dst, pairs):
         rid, pid, _ = topo.addr(dst)
         eng = topo.engines(core, dst)
         k = len(eng) // len(pairs)
@@ -199,9 +203,9 @@ def build(T, topo, core, rank):
                     tr.append(RemoteDMATransfer(dst_ids=[DstId(rid=rid, pnc=pid)], dma_engine_mask=m,
                                                 remote_sem=T.sem[sems[j]], src=i[0], dst=o[0]))
                 return q.remote_dma_fused(tr, local_sem=T.sem.sent)
-        s = add("G", f, r, [], (0, 0, 0, 0, 0, 0.12), "s", k * len(pairs))
+        s = add("G", f, r, [], "s", k * len(pairs))
         for j, (o, i) in enumerate(pairs):
-            add("R", None, [], o[1], (cost - HOP, 0, 0, 0, 0, 1), "r", (sems[j], k, s))
+            add("R", None, [], o[1], "r", (sems[j], k, s))
 
     EQ, LT, GT, MUL, ADD, SUB, MAX, MIN = (ALU.is_equal, ALU.is_lt, ALU.is_gt, ALU.mult, ALU.add, ALU.subtract, ALU.max, ALU.min)
     row0 = (0, 128, 16)
@@ -226,186 +230,165 @@ def build(T, topo, core, rank):
         else:
             cp(out, in_)
 
-    def fill(out, val, p=None):
-        act(out, A("KN", W_, W_ + out[2], 1, p), bias=val, scale=0.0)
+    def fill(out, val, func=ACT.Identity):
+        if out[1][0][0] in GFILL.split():
+            iota(out, [[0, out[2]]], int(val), 0)
+        else:
+            act(out, A("ones", 0, out[2]), scale=val, func=func)
 
+    ms(A("ones"), 1.0)
     dma("S", A("bsd"), ext("bs"))
     dma("S", A("fsd"), ext("ft"))
-    for j, (a, b) in enumerate(((2560, 3584), (0, 896), (896, 1792), (1792, 2560))):
-        dma("Y", A("kst", a, b), ext("kn", a, b), (3700, 4800, 6900, 8700)[j])
-        chain("load")
-        cp(A("KN", a, b), A("kst", a, b))
-    dma("S", A("zin", 0, 256), ext("z0"), 3900)
-    dma("Y", A("XX", 2 * W_, 2 * W_ + L_), ext("x0", home, home + L_), 9000)
-    chain("load")
+    for a, b in zip(KCUT[::2], KCUT[1::2]):
+        dma("Y", A("kst", a, b), ext("kn", a, b))
+        lin("kn%d" % a, A("KN", a, b), A("kst", a, b))
+    dma("S", A("zin", 0, 256), ext("z0"))
+    dma("Y", A("XX", 2 * W_, 2 * W_ + L_), ext("x0", home, home + L_))
     for a, b in ((0, home), (home + L_, W_)):
         if a < b:
-            dma("Y", XC(a, b), ext("x0", a, b), 12700)
+            dma("Y", XC(a, b), ext("x0", a, b))
     merge(2 if home + L_ < W_ else 1)
-    chain("load")
-    dma("Y", A("trs"), ext("tr"), 13200)
-    chain("load")
-    ts(A("trs"), A("trs"), MID, SUB)
-    send(nxt, [(ext("tin"), A("trs"))], HOP + 4000)
-    ms(A("KN", W_, F0 + 8), -1.0)
-    for a in range(F0 + 8, F0 + FW, 280):
-        fill(A("KN", a, min(a + 280, F0 + FW)), -1.0)
+    dma("Y", A("trs"), ext("tr"))
+    dma("Y", X(), ext("x0"))
+    lin("trf", A("trf"), A("trs"), float(UP))
+    send(nxt, [(ext("tin"), A("trf"))])
+    for a in range(W_, F0 + FW, 272):
+        fill(A("KN", a, min(a + 272, F0 + FW)), -1.0)
     ts(A("ftf"), A("fsd"), float(UP), ADD)
     dma("S", A("KN", FB + B_, FB + W_, 1, row0), A("ftf"))
     ms(A("t16"), 0.0)
     ts(A("b16"), A("bsd"), MID, SUB)
     dma("S", A("t16", 0, 256, 1, row0), A("b16"))
 
-    ms(A("ones"), 1.0)
     fill(A("onef"), -1.0)
-    asel(A("Qb"), A("ones", 0, 144), [[-16, 9], [-1000, 16]], 16, 1)
-    cp(A("Qh"), A("Qb"))
-    asel(A("tmpb", 0, 144), A("ones", 0, 144), [[-1, 144]], 0, 1)
-    cp(A("If"), A("tmpb", 0, 144))
-    cp(A("Ib"), A("tmpb", 0, 128))
-    act(A("Ih"), A("Ib"), scale=0.5)
-    act(A("In"), A("Ib"), scale=-1.0)
-    act(A("I8"), A("Ib"), scale=-8192.0)
+    asel(A("Qh"), A("ones", 0, 144), [[-16, 9], [-1000, 16]], 16, 1)
+    asel(A("If"), A("ones", 0, 144), [[-1, 144]], 0, 1)
+    If = A("If", 0, 128)
+    cp(A("Ib"), If)
+    act(A("Ih"), If, scale=0.5)
+    act(A("In"), If, scale=-1.0)
+    act(A("I8"), If, scale=-8192.0)
     iota(A("ci", 0, 1), [[0, 1]], 0, 1)
     ts(A("ci", 1, 2), A("ci", 0, 1), 15, ALU.bitwise_and)
     ts(A("ci", 2, 3), A("ci", 0, 1), 4, ALU.arith_shift_right)
-    ts(A("ci", 3, 4), A("ci", 0, 1), 7, ALU.bitwise_and)
-    ts(A("ci", 4, 5), A("ci", 1, 2), 3, ALU.arith_shift_right)
-    cp(A("cf", 0, 5), A("ci", 0, 5))
-    cP, cR, cG, c7, cV = [A("cf", j, j + 1) for j in range(5)]
-    m0, m1, sgn, mid0, far0 = [A("cf", j, j + 1) for j in (8, 9, 32, 33, 34)]
+    merge(2)
+    cp(A("cf", 0, 2), A("ci", 1, 3))
+    cR, cG, m0, m1, sgn, sgm, mid0, far0 = [A("cf", j, j + 1) for j in (0, 1, 8, 9, 32, 33, 34, 35)]
     ts(m0, cR, 0.5, GT)
     ts(m1, cR, 0.5, LT)
+    merge(2)
     act(sgn, m0, scale=2.0, bias=-1.0)
+    act(sgm, m0, scale=2 * MID, bias=-MID)
     act(far0, m0, scale=float(W_), bias=MID)
     act(mid0, m0, scale=-MID - 32768.0, bias=32768.0)
-    act(A("Im"), A("Ib"), scale=-1.0)
-    act(A("I0"), A("Ib"), scale=m0)
-    act(A("I1"), A("Ib"), scale=m1)
-    ts(A("cf", 10, 11), cV, 144.0, MUL, 1.0, ADD)
-    ts(A("cf", 11, 12), c7, 16.0, MUL, A("cf", 10, 11), ADD)
+    merge(4)
+    act(A("Im"), If, scale=-1.0)
+    act(A("I0"), If, scale=m0)
+    act(A("I1"), If, scale=m1)
+    ts(A("cf", 10, 11), cR, 7.5, GT, 16.0, MUL)
+    ts(A("cf", 11, 12), cR, 16.0, MUL, A("cf", 10, 11), ADD)
+    ts(A("cf", 12, 13), cG, 2.0, MUL, 1.0, ADD)
     zl = [A("cu", 0, 1), A("cu", 2, 3)]
-    ts(zl[0], cG, 7.0, ADD, A("cf", 11, 12), ADD)
-    ts(zl[1], cG, 2.0, MUL, A("cf", 11, 12), ADD)
+    ts(zl[0], cG, 8.0, ADD, A("cf", 11, 12), ADD)
+    ts(zl[1], A("cf", 12, 13), A("cf", 11, 12), ADD)
+    merge(2)
     ts(A("cf", 14, 15), cR, 8.0, MUL, cG, ADD)
     iota(A("tmpc", 0, 128), [[1, 128]], 0, 0)
     ts(A("Pm"), A("tmpc", 0, 128), A("cf", 14, 15), EQ)
     act(A("Pf", 0, 128), A("Pm"), scale=WT)
     act(A("Pf", 128, 256), A("Pm"), scale=-1.0)
-    iota(A("tmpc", 160, 192), [[0, 2], [16, 16]], 0, 0)
+    iota(A("tmpc", 208, 224), [[1, 2], [2, 8]], 0, 0)
+    for s, a in enumerate((208, 0)):
+        ts(A("RE", 32 * s, 32 * s + 16), A("tmpc", a, a + 16), cR, EQ, 32.0, MUL)
+        ts(A("RE", 32 * s + 16, 32 * s + 32), A("tmpc", a, a + 16), cR, EQ)
+    merge(4)
     iW, spM = A("cw", 0, 16), A("cw", 64, 96)
-    ts(A("cw", 0, 32), A("tmpc", 160, 192), cR, ADD)
+    iota(A("tmpc", 160, 176), [[16, 16]], 0, 0)
+    ts(iW, A("tmpc", 160, 176), cR, ADD)
     act(A("cw", 64, 80), iW, bias=DK - MID)
     act(A("cw", 80, 96), iW, bias=DF + FO - MID)
+    merge(2)
     for j in range(N):
-        ts(A("nW", 32 * j, 32 * j + 32), A("cw", 0, 32), -1.0, MUL, MID - B_ - L_ * j, ADD)
+        act(A("nW", 16 * j, 16 * j + 16), iW, MID - B_ - L_ * j, -1.0)
     merge(N)
     for name in ("o0", "q0"):
         fill(A(name), 0.0)
     act(A("o1", 1, 32, 2), iW, bias=float(DK))
     act(A("o1", 33, 64, 2), iW, bias=float(DF))
+    merge(2)
     fill(A("q1", 0, 32, 2), 256.0)
-    act(A("q1", 1, 32, 2), iW, bias=-MID)
-    act(A("q1", 33, 64, 2), iW, bias=DK - MID)
-    act(A("q1", 65, 96, 2), iW, bias=DF - MID)
-    act(A("q1", 97, 128, 2), iW, bias=DK - MID)
-    fill(A("c17"), WT)
+    for a, v in ((1, -MID), (33, DK - MID), (65, DF - MID), (97, DK - MID)):
+        act(A("q1", a, a + 31, 2), iW, bias=v)
+    merge(5)
+    fill(A("c17"), WT, ACT.Silu)
     fill(A("c64", 0, 16), 64.0)
     fill(A("c64", 16, 24), -33 * 64.0 / 128)
+    merge(2)
     iota(A("tmpc", 192, 208), [[0, 2], [1, 8]], 0, 0)
     two, neg, one = A("BD", 0, 16), A("BD", 16, 32), A("BD", 32, 48)
     for o, v in ((two, 2 * WT), (neg, -WT), (one, WT)):
         ts(o, A("tmpc", 192, 208), cG, EQ, v, MUL)
+    merge(3)
     asel(A("tmpb"), A("ones"), [[0, 2], [-16, 8], [-1, 17]], 1, 1)
     ms(A("tmpb", 0, 272, 17), 0.0)
     cp(A("PF"), A("tmpb", 0, 136))
     ts(A("PF0"), A("PF"), m0, MUL)
-    ts(A("tmpb", 0, 136), A("tmpb", 0, 136), 1.0 / 32, MUL)
-    ts(A("tmpb", 136, 272), A("tmpb", 136, 272), -1.0, MUL)
-    cp(A("PH"), A("tmpb"))
-    for a in (0, 136):
-        asel(A("tmpb", a, a + 136), A("tmpb", a, a + 136), [[-16, 8], [0, 17]], 0, 1, ALU.not_equal, BIG / (1024 if a else 32768))
-    cp(A("PH0"), A("tmpb"))
-    asel(A("cq", 0, 8), A("ones", 0, 8), [[-16, 8]], 0, 1)
-    act(A("SH", 0, 8), A("cq", 0, 8), scale=1.0 / 32)
-    act(A("SH", 8, 16), A("cq", 0, 8), scale=-1.0)
-    cp(A("SF"), A("cq", 0, 8))
-    ms(A("CK", 0, 544, 1, (32, 64)), -16 * WT)
+    ts(A("PH", 0, 136), A("tmpb", 0, 136), 1.0 / 32, MUL)
+    ts(A("PH", 136, 272), A("tmpb", 136, 272), -1.0, MUL)
+    merge(2)
+    asel(A("PH0", 0, 136), A("PH", 0, 136), [[-16, 8], [0, 17]], 0, 1, ALU.not_equal, BIG / 32768)
+    asel(A("PH0", 136, 272), A("PH", 136, 272), [[-16, 8], [0, 17]], 0, 1, ALU.not_equal, BIG / 1024)
+    asel(A("SF"), A("ones", 0, 8), [[-16, 8]], 0, 1)
+    act(A("SH", 0, 8), A("SF"), scale=1.0 / 32)
+    act(A("SH", 8, 16), A("SF"), scale=-1.0)
+    merge(2)
     ms(A("CK", 0, 544, 1, (0, 32)), 0.0)
+    ms(A("CK", 0, 544, 1, (32, 64)), 16 * WT)
+    merge(2)
     iota(A("CK", 0, 544, 1, (0, 1)), [[0, 32], [128, 17]], -1088, 0)
     for a in range(0, 544, 136):
-        big = BIG * (32 if a % 272 else 1)
-        if a < 272:
-            fill(A("CB", a, a + 136), big / 128)
-        ms(A("CK", a, a + 136, 1, (64, 128)), -big / 64)
+        ms(A("CK", a, a + 136, 1, (64, 128)), -BIG * (32 if a % 272 else 1) / 64)
+    merge(4)
+    fill(A("CB", 0, 136), BIG / 128)
+    fill(A("CB", 136, 272), BIG / 4)
+    merge(2)
     ms(A("CK", 1, 272, 17), 0.0)
     ms(A("CK", 272, 544, 17), 0.0)
+    merge(2)
     ms(A("CK", 272, 544, 17, (0, 1)), -1152.0)
     fill(A("CB", 0, 272, 17), 0.0)
     fill(A("d0"), 0.0)
     fill(A("d0", 0, 272, 17), 67108864.0)
-    iota(A("tmpc", 208, 224), [[1, 2], [2, 8]], 0, 0)
-    iota(A("tmpc", 224, 240), [[1, 16]], 0, 0)
-    for s in range(2):
-        ts(A("RE", 32 * s, 32 * s + 16), A("tmpc", 208 + 16 * s, 224 + 16 * s), cR, EQ, 32.0, MUL)
-        ts(A("RE", 32 * s + 16, 32 * s + 32), A("tmpc", 208 + 16 * s, 224 + 16 * s), cR, EQ)
     for a in range(0, 1152, 288):
         ms(A("Z", a, a + 288), 0.0)
-    iota(A("tmpc", 240, 249), [[1, 9]], -1, 0)
-    fill(A("Qa"), 0.0)
-    ts(A("Qa", 0, 144, 16), A("tmpc", 240, 249), cG, EQ)
-    for a in (0, 1024):
-        dma("Y", A("TM", a, a + 1024), A("Z", 0, 1024), 15500)
-        chain("load")
-    dma("Y", X(), ext("x0"), 19500)
-    chain("load")
-    if OPT["sc"]:
-        iota(A("dq", 0, 128), [[1, 8], [0, 16]], 0, 0)
-        ts(A("BO"), A("dq", 0, 128), cG, EQ)
-        ts(A("D", 0, 16), A("tmpc", 224, 240), cR, EQ, 2.0 ** 23, MUL)
-        ts(A("cf", 16, 17), cR, 1.0, ADD)
-        ts(A("D", 16, 32), A("tmpc", 224, 240), A("cf", 16, 17), EQ, -2.0 ** 22, MUL)
-        for c in range(32):
-            mm(A("pn", 16 * (c // 2), 16 * (c // 2) + 16), A("Ib"), A("D", 16 * (c % 2), 16 * (c % 2) + 16), c == 0, c == 31)
-        merge(32)
-        act(A("dq"), A("pn", 0, 256))
-        ts(A("cf", 17, 18), cR, 14.5, LT, 2.0 ** 22, MUL)
-        act(A("I15"), A("Ib"), scale=A("cf", 17, 18))
-        act(A("I32"), A("Ib"))
-    for r in range(1, 16):
-        asel(A("TM", 129 * r, 128 * r + 128, 16), A("Qa", 16, 144, 16), [[16, 8]], r, -1, GT)
-        if r % 4 == 0 or r == 15:
-            merge(4 if r < 15 else 3)
-    act(A("Q16"), A("Qb"), scale=16.0)
-    fill(A("cq"), -0.25 / 128)
-    fill(A("HC", 0, 16), 0.0)
+    iota(A("dq", 0, 128), [[1, 8], [0, 16]], 0, 0)
+    ts(A("BO"), A("dq", 0, 128), cG, EQ)
+    asel(A("BL"), A("BO"), [[1, 128]], 0, -1, GT)
+    iota(A("dq"), [[0, 16], [1, 16]], 0, 0)
+    ts(A("Dq"), A("dq"), cR, ALU.not_equal, 2.0 ** 22, MUL)
+    fill(A("dq"), 0.0)
+    fill(A("dq", 0, 256, 16), 2.0 ** 23)
+    fill(A("cq", 0, 128), -0.25 / 128)
     fill(A("aout"), 0.0)
     fill(A("nrow"), 0.0)
-    for a in range(0, W_ + UP, 512):
+    for a in range(0, W_, 512):
         iota(A("ID", a, a + 512), [[1, 512]], a, 0)
+    ID = lambda a, b, p=None: parts(A("ID", a, b, 1, p), ["ID"], 0, W_)
 
     kcol = lambda s, k: k + 1 if s or k else 0
+    zneg = {}
+    for s, ks in sorted(set((s, ks) for split in SPLIT for s in range(2) for nv, ks in split[s])):
+        zneg[s, ks] = A("ZN", 272 * len(zneg), 272 * len(zneg) + 272)
+        cols = [kcol(s, k) for k in range(16) if k % 4 < 4 - ks]
+        mm(A("pd", 0, 272), A("Z", 0, 128), A("ones"), True, False)
+        for c in cols:
+            mm(A("pd", c, 272, 17), A("Ib"), neg, False, c == cols[-1])
+        merge(1 + len(cols))
+        act(zneg[s, ks], A("pd", 0, 272))
 
-    def zcols(s, nf, ks):
-        plain = [kcol(s, k) for k in range(16) if k % 4 >= 4 - ks or nf == 128]
-        return plain, [kcol(s, k) for k in range(16) if kcol(s, k) not in plain and nf]
-
-    zr = {}
-    for s, split in enumerate(SPLIT0 + SPLIT):
-        for nf, nv, ks in split:
-            for cols in zcols(s % 2, nf, ks):
-                if cols and tuple(cols) not in zr:
-                    a = 272 * len(zr)
-                    zr[tuple(cols)] = A("ZR", a, a + 272)
-                    mm(A("pd", 0, 272), A("Z", 0, 128), A("ones"), True, False)
-                    for c in cols:
-                        mm(A("pd", c, 272, 17), A("Ib"), one, False, c == cols[-1])
-                    merge(1 + len(cols))
-                    act(zr[tuple(cols)], A("pd", 0, 272))
-
-    def conv(bank, c0, Q, name, n, start=True, a=0, stop=True):
+    def conv(bank, c0, name, n, start=True, a=0, stop=True):
         for r in range(16):
-            mm(A(bank, c0, c0 + n // 16), A(Q, 16 - r, 144 - r), A(name, a + r, a + n, 16), start and r == 0, stop and r == 15)
+            mm(A(bank, c0, c0 + n // 16), A("Qh", 16 - r, 144 - r), A(name, a + r, a + n, 16), start and r == 0, stop and r == 15)
         merge(16)
 
     def kin(s, h, t):
@@ -420,24 +403,19 @@ def build(T, topo, core, rank):
                 merge(2)
             mm(pu, A("I0"), A("c16", a, b), False, True)
             ts(A("cU", a, b), pu, far0 if t else MID, ADD)
-        elif "kin1%d" % h in SCALAR.split():
-            act(A("c16", a, b), I(KIN, bu), bias=-MID)
-            ts(A("cU", a, b), A("c16", a, b), MID, ADD)
         else:
             cp(A("cU", a, b), I(KIN, bu))
-            at("parts%d%d" % (s, h))
             ts(A("c16", a, b), A("cU", a, b), MID, SUB)
 
     def starts(h):
-        pz = "pk%d" % h
-        conv(pz, 0, "Qh", "t16", 128, a=128 * h)
-        ts(A("bU", 8 * h, 8 * h + 8), A(pz, 0, 8), MID, ADD)
+        conv("pk%d" % h, 0, "t16", 128, a=128 * h)
+        ts(A("bU", 8 * h, 8 * h + 8), A("pk%d" % h, 0, 8), MID, ADD)
 
     def early_kin(t):
         lo = B_ + L_ * ((rank - t) % N)
         at("far")
         iota(XC(lo, lo + 256), [[0, 256]], 8192, 0)
-        kin(0, 1 - OPT["h0"], t)
+        kin(0, 1, t)
 
     act(A("e16", 0, 256), A("t16"), bias=MID - home - 127.5, func=ACT.Abs)
     ts(A("v16"), A("e16", 0, 256), 128.0, LT, float(W_ - home), MUL)
@@ -445,9 +423,6 @@ def build(T, topo, core, rank):
         at("t%d" % h)
         starts(h)
     early_kin(0)
-    at("init")
-    dma("Y", A("kst", 0, W_, 1, row0), ext("tin"), 4000)
-    nd = [0]
     wv = lambda j, n=16: A("w", 16 * j, 16 * j + n)
     uv = lambda j, n=16: A("u", 16 * j, 16 * j + n)
 
@@ -460,21 +435,17 @@ def build(T, topo, core, rank):
         xw = 512 * t
         others = [(r_ + d) % N for d in range(1, N)]
         at("yu", t)
-        kin(0, OPT["h0"], t)
+        kin(0, 0, t)
         at("yu")
-        if t:
-            dma("Y", A("yrow"), A("KN", fl, fl + 256))
-        else:
-            dma("Y", A("yrow"), A("KN", fl, fl + 256), 6000)
+        dma("Y", A("yrow"), A("KN", fl, fl + 256))
         lin("gu", A("g16", 256, 512), A("KN", lo, lo + 256), -MID)
         lin("gy", A("g16", 0, 256), A("KN", fl, fl + 256), -MID - UP)
-        conv("pw", 96, "Qh", "g16", 512)
+        conv("pw", 96, "g16", 512)
         yu = lambda a, b: A("pw", 96 + a, 96 + b)
         ts(uv(0, 32), yu(0, 32), MID, ADD)
         tt(A("o1", 0, 64, 2), yu(0, 32), spM, SUB)
-        at("own")
-        act(wv(0, 32), yu(0, 32), bias=MID - lo - 127.5, func=ACT.Abs)
         at("live")
+        act(wv(0, 32), yu(0, 32), bias=MID - lo - 127.5, func=ACT.Abs)
         tt(wv(4), wv(0), wv(1), MIN)
         live = A("lv")
         ts(live, wv(4), 128.0, GT)
@@ -482,8 +453,7 @@ def build(T, topo, core, rank):
         lin("lvN", wv(14), live, -MID, float(W_))
         lin("wt", wv(16), live, 1.0, MID - 1)
         tt(wv(15), yu(0, 16), wv(14), MAX)
-        at("e16")
-        ne = 32
+        at("py")
         lin("py", A("e16", 0, 256), I(KINS, uv(0)), -MID)
         at("fu")
         lin("fu", A("e16", 256, 512), I(A("KN", FB), uv(1)), -MID - UP)
@@ -493,37 +463,37 @@ def build(T, topo, core, rank):
         lin("colY", A("colY"), A("pz0", 0, 256), MID)
         dma("Y", A("XWn", xw, xw + 256), X(lo, lo + 256))
         at("held")
-        conv("pc", 0, "Qh", "e16", 16 * ne, stop=False)
-        mm(A("pc", 0, ne), A("If", 0, 128), A("nW", 32 * r_, 32 * r_ + ne), False, False)
+        conv("pc", 0, "e16", 512, stop=False)
+        for a in (0, 16):
+            mm(A("pc", a, a + 16), If, A("nW", 16 * r_, 16 * r_ + 16), False, False)
         mm(A("pc", 0, 16), A("ones", 0, 128), A("c64", 0, 16), False, False)
         mm(A("pc", 0, 16), A("I8"), live, False, True)
-        merge(3)
-        ts(A("o0", 1, 2 * ne, 2), A("pc", 0, ne), 0.0, EQ)
-        if OPT["tm"]:
-            tt(A("o0", 33, 64, 2), A("o0", 33, 64, 2), A("o0", 1, 32, 2), MUL)
-            scan(A("o2"), A("o0"), A("o1"), MUL, ADD)
-            cp(uv(2, 32), A("o2", 1, 64, 2))
-        else:
-            scan(A("o2", 0, 32), A("o0", 0, 32), A("o1", 0, 32), MUL, ADD)
-            cp(uv(2), A("o2", 1, 32, 2))
+        merge(4)
+        ts(A("o0", 1, 64, 2), A("pc", 0, 32), 0.0, EQ)
+        scan(A("o2", 0, 32), A("o0", 0, 32), A("o1", 0, 32), MUL, ADD)
+        cp(uv(2), A("o2", 1, 32, 2))
         cp(I(KINS, uv(2)), A("colY"))
-        at("turn0")
-        if not OPT["tm"]:
-            tt(A("o0", 33, 64, 2), A("o0", 33, 64, 2), A("o0", 1, 32, 2), MUL)
-            scan(A("o2", 32, 64), A("o0", 32, 64), A("o1", 32, 64), MUL, ADD)
-            cp(uv(3), A("o2", 33, 64, 2))
+        at("turn")
+        tt(A("o0", 33, 64, 2), A("o0", 33, 64, 2), A("o0", 1, 32, 2), MUL)
+        scan(A("o2", 32, 64), A("o0", 32, 64), A("o1", 32, 64), MUL, ADD)
+        cp(uv(3), A("o2", 33, 64, 2))
+        scatter("turn", I(FEET, uv(3)), A("yrow"))
         at("p16")
         lin("p16", A("p16"), I(KIN, A("bU", 0, 16)), -MID)
         dma("Y", A("KWn", 0, 256), A("KN", lo, lo + 256))
-        dma("Y", A("nrow", 0, 256, 1, row0), A("ID", lo, lo + 256, 1, row0))
-        at("turn")
-        for a in range(0, 16, OPT["tu"]):
-            scatter("turn", I(FEET, A("u", 48 + a, 48 + a + OPT["tu"])), A("yrow", 16 * a, 16 * (a + OPT["tu"])))
+        dma("Y", A("nrow", 0, 256, 1, row0), ID(lo, lo + 256, row0))
+        if t == 0:
+            at("TT")
+            dma("Y", A("TT"), KINS)
+            dma("Y", A("TT", 0, W_, 1, row0), ext("tin"))
         if last:
+            at("down")
+            for a in (B_, B_ + 512):
+                lin("down", A("KN", FB + a, FB + a + 512), A("KN", FB + a, FB + a + 512), -float(UP))
             for j in others:
                 a = B_ + 256 * j
-                dma("Y", ext("yk", 256 * j, 256 * j + 256), A("KN", a, a + 256), 3000)
-                dma("Y", ext("yx", 256 * j, 256 * j + 256), X(a, a + 256), 3000)
+                dma("Y", ext("yk", 256 * j, 256 * j + 256), A("KN", a, a + 256))
+                dma("Y", ext("yx", 256 * j, 256 * j + 256), X(a, a + 256))
         at("Ain")
         if t > 0:
             a0 = A("ain", 8 * t, 8 * t + 1)
@@ -533,88 +503,61 @@ def build(T, topo, core, rank):
         for h in (1, 0):
             at("zp%d" % h)
             for c in range(8):
-                asel(A("zp", 128 * h + c, 128 * h + 128, 8), z(128 * h + 16 * c, 128 * h + 16 * c + 16), [[0, 16]], 0, 0)
+                asel(parts(A("zp", 128 * h + c, 128 * h + 128, 8), ["zp"], 128 * h + 16 * c, 128 * h + 16 * c + 16),
+                     z(128 * h + 16 * c, 128 * h + 16 * c + 16), [[0, 16]], 0, 0)
                 if c % 2:
                     merge(2)
+        if not last:
+            at("nup")
+            iota(A("nup"), [[1, 256]], lo + UP, 0)
         at("p16")
-        conv("pw", 48, "Qh", "p16", 256)
-        ts(uv(10), A("pw", 48, 64), MID, ADD)
+        conv("pc", 48, "p16", 256)
+        ts(uv(10), A("pc", 48, 64), MID, ADD)
         at("xp")
-        if OPT["xp"]:
-            tt(A("xp"), I(XC(), uv(10)), z(), SUB)
-            ts(A("mp"), A("xp"), 0.0, MAX)
-        else:
-            act(A("xp"), I(XC(), uv(10)))
+        tt(A("xp"), I(XC(), uv(10)), z(), SUB)
+        ts(A("mp"), A("xp"), 0.0, MAX)
         for s in range(2):
-            for h in (0, 1) if s == 0 and OPT["h0"] else (1, 0):
+            for h in (1, 0):
                 on = lambda name: at("%s%d%d" % (name, s, h))
                 hs = 128 * h
                 H = lambda name: A(name, hs, hs + 128)
-                zz = lambda a=0, b=128: z(hs + a, hs + b) if s == 0 else A("zp", hs + a, hs + b)
+                zz = lambda: H("zp") if s else z(hs, hs + 128)
                 pz, pk, xn, mn, zo = "pz%d" % h, "pk%d" % h, "x%db" % h, "m%db" % h, 288 * (2 * s + h)
                 win = XC() if s else A("XX", 0, 2 * W_) if t else A("XX", W_)
-                nf, nv, ks = (SPLIT if t else SPLIT0)[s][1 - h]
-                zo_ = 2048 * h
-                if nf:
-                    on("zr")
-                    for k in range(16):
-                        asel(A("zr", zo_ + k, zo_ + 16 * nf, 16), zz(0, nf), [[0, nf]], 0, 0)
-                        if k % 2 and nf < 128:
-                            merge(2)
+                nv, ks = SPLIT[t > 0][s][1 - h]
                 if s == 1:
                     kin(1, h, t)
                 if s == 1 and h == 1:
                     at("stay")
-                    cp(A("D"), A("Di"))
+                    asel(A("D"), A("Di"), [[0, 32]], 0, 0)
                     ts(wv(22, 32), A("R", 16, 544, 17), 1.0 / WT, MUL, BIG, ADD)
                     lin("stay", wv(24, 32), wv(22, 32), -BIG)
                     tt(wv(26, 32), A("R", 16, 544, 17), A("R", 0, 544, 17), SUB)
                     ts(wv(28, 32), wv(26, 32), A("d0", 1, 2), ALU.is_ge, A("d0", 1, 2), MUL)
                 on("z")
-                nz = 4 if ks < 4 and nf < 128 else 1 if s == 0 and not OPT["xp"] else 0
-                z0_ = nf if s or OPT["xp"] else 0
-                for j in range(nz):
-                    mm(A(pz, 4 * z0_ + j, 512, 4), A("Ib"), zz(z0_), True, True)
-                if nz:
-                    merge(nz)
-                on("gf")
-                for a in range(0, nf, FCUT):
-                    b = min(nf, a + FCUT)
-                    tt(A(xn, 16 * a, 16 * b), I(win, A("cU", hs + a, hs + b)), A("zr", zo_ + 16 * a, zo_ + 16 * b), SUB)
+                for j in range(4):
+                    mm(A(pz, j, 512, 4), A("Ib"), zz(), True, True)
+                merge(4)
                 on("gv")
-                for a in range(nf, nf + nv, VCUT[s]):
-                    b = min(nf + nv, a + VCUT[s])
+                for a in range(0, nv, CUT[0]):
+                    b = min(nv, a + CUT[0])
                     cp(A(xn, 16 * a, 16 * b), I(win, A("cU", hs + a, hs + b)))
                 on("gs")
-                for a in range(nf + nv, 128, SCUT[s]):
-                    b = min(128, a + SCUT[s])
+                for a in range(nv, 128, CUT[1]):
+                    b = min(128, a + CUT[1])
                     act(A(xn, 16 * a, 16 * b), I(win, A("cU", hs + a, hs + b)))
-                xs_ = lambda j, a, b: A(xn, 16 * a + j, 16 * b, 4)
-                mj = lambda j, a, b: A(mn, 512 * j + 4 * a, 512 * j + 4 * b)
-                mk = lambda k: A(mn, 512 * (k % 4) + k // 4, 512 * (k % 4) + 512, 4)
-                sv_, ss_ = list(range(4 - ks)), list(range(4 - ks, 4))
-                banks = ("pd", "pc" if s else "pn")
-                for j in sv_:
+                for j in range(4):
                     on("ABCD"[j])
-                    if nf:
-                        ts(mj(j, 0, nf), xs_(j, 0, nf), 0.0, MAX)
-                    if nf < 128:
-                        tt(mj(j, nf, 128), xs_(j, nf, 128), A(pz, 4 * nf, 512), MAX)
-                for j in ss_:
-                    on("ABCD"[j])
-                    if nf:
-                        act(mj(j, 0, nf), xs_(j, 0, nf), func=ACT.Abs)
-                    if nf < 128:
-                        pd = banks[nd[0] % 2]
-                        nd[0] += 1
-                        for i in range(4):
-                            mm(A(pd, 4 * nf + i, 512, 4), A("In"), zz(nf), i == 0, False)
-                        merge(4)
-                        mm(A(pd, 4 * nf, 512), A("Ib"), xs_(j, nf, 128), False, True)
-                        act(mj(j, nf, 128), A(pd, 4 * nf, 512), func=ACT.Abs)
-                on("mp")
-                if s == 0 and not OPT["xp"]:
-                    tt(H("mp"), H("xp"), A(pz, 0, 512, 4), MAX)
+                    xj, mj = A(xn, j, 2048, 4), A(mn, 512 * j, 512 * j + 512)
+                    if j < 4 - ks:
+                        tt(mj, xj, A(pz), MAX)
+                        continue
+                    pd = BANKS[s][1 - h][3 - j]
+                    for i in range(4):
+                        mm(A(pd, i, 512, 4), A("In"), zz(), i == 0, False)
+                    merge(4)
+                    mm(A(pd), A("Ib"), xj, False, True)
+                    act(mj, A(pd), func=ACT.Abs)
                 on("key")
                 key = A(pk, 0, 272)
                 col = lambda j: A(pk, j, 272, 17)
@@ -633,60 +576,47 @@ def build(T, topo, core, rank):
                     mm(col(0), A("Pf", 128, 256), wv(28 + h), False, False)
                     mm(col(0), A("Pm"), A("D", 16 * h, 16 * h + 16), False, False)
                     merge(3)
-                n = 0
-                for cols, m in zip(zcols(s, nf, ks), (128, nf)):
-                    if cols:
-                        mm(A(pk, 0, 272, 1, (0, m)), zz(0, m), zr[tuple(cols)], False, False)
-                        n += 1
-                if n:
-                    merge(n)
                 on("neg")
-                kv = [k for j in sv_ for k in range(j, 16, 4)]
+                mm(key, zz(), zneg[s, ks], False, False)
+                kv = [k for k in range(16) if k % 4 < 4 - ks]
                 for k in kv:
                     mm(col(kcol(s, k)), A(xn, k, 2048, 16), neg, False, False)
-                if kv:
-                    merge(len(kv))
-                turn = sorted(range(4), key=lambda j: (sv_.index(j) if j in sv_ else ss_.index(j), j))
+                merge(len(kv))
+                turn = sorted(range(4), key=lambda j: (j if j < 4 - ks else j - 4 + ks, j))
                 for j in turn:
                     on("ABCD"[j])
-                    for k in range(j, 16, 4):
-                        mm(col(kcol(s, k)), mk(k), two if j in sv_ else one, False, s == 1 and j == turn[-1] and k == j + 12)
+                    for i in range(4):
+                        mm(col(kcol(s, 4 * i + j)), A(mn, 512 * j + i, 512 * j + 512, 4), two if j < 4 - ks else one,
+                           False, s == 1 and j == turn[-1] and i == 3)
                     merge(4)
                 if s == 0:
                     on("par")
                     mm(col(1), H("p16"), A("SH"), False, False)
                     mm(col(1), A("ones", 0, 128), A("CK", 273, 544, 17), False, False)
                     mm(col(137), H("p16"), A("SF"), False, False)
-                    if OPT["xp"]:
-                        mm(col(1), zz(), one, False, False)
-                    merge(3 + OPT["xp"])
+                    merge(3)
                     on("dec")
                     mm(col(1), H("xp"), neg, False, False)
                     mm(col(1), H("mp"), two, False, True)
                     merge(2)
                 on("dec")
                 scan(A("R", 272 * h, 272 * h + 272), A("d0"), key, ADD, MIN)
-                ends = A("R", 272 * h + 16, 272 * h + 272, 17)
                 dd = A("Di", 16 * h, 16 * h + 16)
-                ts(dd, ends, 127, ALU.bitwise_and)
+                ts(dd, A("R", 272 * h + 16, 272 * h + 272, 17), 127, ALU.bitwise_and)
                 cp(I(A("Z", zo, zo + 288), zl[s]), dd)
-
-                def winners(out):
-                    mm(out, A("ones", 0, 128), A("c64", 16, 24), True, False)
-                    for v in range(2):
-                        for e in range(2):
-                            a, c = zo + 144 * v + (1 - e) * (1 if s else 8), 32 * s + 16 * v + 8 * e
-                            mm(out, A("Z", a, a + 128), A("RE", c, c + 8), False, v + e == 2)
-                    merge(5)
-
                 bP = A(pk, 288, 296)
-                winners(bP)
+                mm(bP, A("ones", 0, 128), A("c64", 16, 24), True, False)
+                for v in range(2):
+                    for e in range(2):
+                        a, c = zo + 144 * v + (1 - e) * (1 if s else 8), 32 * s + 16 * v + 8 * e
+                        mm(bP, A("Z", a, a + 128), A("RE", c, c + 8), False, v + e == 2)
+                merge(4)
                 if s == 0:
                     ts(A("bU", 16 + 8 * h, 24 + 8 * h), bP, MID, ADD)
                     continue
                 boh = A("bO", 16 * t + 8 * h, 16 * t + 8 * h + 8)
                 ts(boh, bP, MID, ADD)
-                send(prv if last else nxt, [(A("bin", 16 * t + 8 * h, 16 * t + 8 * h + 8), boh)], HOP)
+                send(prv if last else nxt, [(A("bin", 16 * t + 8 * h, 16 * t + 8 * h + 8), boh)])
                 at("zn%d" % h)
                 lin("xs%d" % h, H("xs"), I(X(), boh))
                 mm(A(pz, 0, 128), A("ones", 0, 128), A("cq", 0, 128), True, False)
@@ -696,30 +626,27 @@ def build(T, topo, core, rank):
                 mm(A(pz, 0, 128), A("Ih"), H("xs"), False, True)
                 ts(zn, A(pz, 0, 128), BIG, ADD, BIG, SUB)
                 if not last:
-                    send(nxt, [(A("zin", 256 * t + 256 + hs, 256 * t + 384 + hs), zn)], HOP + 300)
+                    send(nxt, [(A("zin", 256 * t + 256 + hs, 256 * t + 384 + hs), zn)])
                 at("brow%d" % h)
-                lin("brow%d" % h, H("brow"), I(A("ID"), boh), -MID)
+                lin("brow%d" % h, H("brow"), I(ID(0, W_), boh), -MID)
                 at("v%d" % h)
-                if OPT["vd"] > h:
-                    lin("v%d" % h, H("v16"), I(KIN, boh), -MID)
-                lin("kb%d" % h, A("KWn", 256 + hs, 384 + hs), I(KIN, boh), 0.0, sgn)
-                if OPT["vd"] <= h:
-                    lin("v%d" % h, H("v16"), A("KWn", 256 + hs, 384 + hs), -MID, -1.0)
-                at("E2")
+                lin("v%d" % h, H("v16"), I(KIN, boh), -MID)
+                if h == 0:
+                    act(A("KWn", 256, 512), A("v16"), bias=sgm, scale=sgn)
+                at("E8")
                 if h == 1:
-                    mm(A("pn", 0, 256), A("TM", 0, 128), A("ones", 0, 256), True, False)
+                    mm(A("pn", 0, 256), A("Ib"), A("Dq"), True, False)
                 for c0, c1 in ((8, 12), (12, 16)) if h else ((0, 3), (3, 6), (6, 8)):
                     at("E%d" % c0)
                     for c in range(c0, c1):
                         ts(A("E", 272 * c, 256 * c + 256), A("brow", 16 * c, 256), A(pk, 288 + c % 8, 289 + c % 8),
                            EQ, A("w", 256 + c, 257 + c), MUL)
                     merge(c1 - c0)
-                    cs = [c for c in range(c0, c1) if c < 15]
-                    for c in cs:
-                        mm(A("pn", 16 * c + 16, 256), A("BO") if OPT["sc"] else A("Qa", 16, 144), A("E", 272 * c + 16, 256 * c + 256), False, c == 7)
-                    merge(len(cs))
-                at("may")
-                winners(A("pw", 64 + 8 * h, 72 + 8 * h))
+                    for c in range(c0, c1):
+                        mm(A("pn", 16 * c, 16 * c + 16), A("BL"), A("E", 272 * c, 272 * c + 16), False, False)
+                        if c < 15:
+                            mm(A("pn", 16 * c + 16, 256), A("BO"), A("E", 272 * c + 16, 256 * c + 256), False, c == 7)
+                    merge(2 * (c1 - c0) - (c1 == 16))
         at("zn0")
         bi = lambda h: A("bin", 16 * t + 8 * h, 16 * t + 8 * h + 8)
         if last:
@@ -727,109 +654,64 @@ def build(T, topo, core, rank):
         if 0 < t < VIS - 1:
             for h in (1, 0):
                 at("T%d" % h)
-                cp(I(A("kst"), A("oin", 16 * t + 8 * h, 16 * t + 8 * h + 8)), A("brow", 128 * h, 128 * h + 128))
-        if not last and OPT["t1"]:
-            at("t1")
-            lin("t1", A("t16"), I(A("kst", 0, W_), A("bin", 16 * t, 16 * t + 16)))
-            conv("pk1", 0, "Qh", "t16", 256)
-            ts(A("bU", 0, 16), A("pk1", 0, 16), MID, ADD)
-        elif not last:
+                bb = A("bb", 128 * h, 128 * h + 128)
+                lin("bb%d" % h, bb, A("brow", 128 * h, 128 * h + 128), MID + UP)
+                scatter("T%d" % h, I(A("TT"), A("oin", 16 * t + 8 * h, 16 * t + 8 * h + 8)), bb)
+        if not last:
             for h in (1, 0):
                 at("t%d" % h)
-                lin("t%d" % h, A("t16", 128 * h, 128 * h + 128), I(A("kst", 0, W_), bi(h)))
+                lin("t%d" % h, A("t16", 128 * h, 128 * h + 128), I(A("TT", 0, W_), bi(h)), -MID - UP)
                 starts(h)
         if t == VIS - 2:
             at("home")
-            dma("Y", A("trt"), A("kst", 0, W_, 1, row0), 4000)
-            ts(A("trf"), A("trt"), MID, ADD)
-            send(prv, [(ext("tback"), A("trf"))], HOP + 2000)
-            dma("Y", A("TT", 0, W_, 1, row0), ext("tback"), 4000)
+            dma("Y", A("trt"), A("TT", 0, W_, 1, row0))
+            lin("home", A("trh"), A("trt"), -float(UP))
+            send(prv, [(ext("tback"), A("trh"))])
+            dma("Y", A("TT", 0, W_, 1, row0), ext("tback"))
         at("may")
-        bW = A("pw", 64, 80)
+        bW = wv(30)
+        ts(bW, A("bO", 16 * t, 16 * t + 16), MID, SUB)
         act(wv(18), bW, bias=MID - lo - 127.5, func=ACT.Abs)
-        act(A("nW", 128, 144), bW, scale=-1.0)
-        merge(2)
         tt(A("q1", 32, 64, 2), bW, A("cw", 64, 80), SUB)
         act(wv(19), wv(18), bias=-131072.0, scale=1024.0)
-        tt(A("thr", 0, 16), wv(19), wv(14), MIN)
+        tt(A("thr"), wv(19), wv(14), MIN)
         if not last:
-            act(A("q1", 96, 128, 2), A("q1", 32, 64, 2))
+            asel(A("q1", 96, 128, 2), A("q1", 32, 64, 2), [[0, 16]], 0, 0)
         at("vl")
-        conv("pd", 0, "Qh", "v16", 256)
+        conv("pd", 0, "v16", 256)
         ts(uv(5), A("pd", 0, 16), MID - FO, ADD)
         tt(A("q1", 64, 96, 2), A("pd", 0, 16), A("cw", 80, 96), SUB)
         at("hit")
-        lin("hit", A("HC", 256, 512), I(FEET, uv(5)), (-MID - UP) / 16, 1.0 / 16)
-        if last:
-            lin("down", A("KN", FB + B_, FB + W_), A("KN", FB + B_, FB + W_), -float(UP))
-        cnt = A("pc", 0, 16)
+        lin("hit", A("HC"), I(FEET, uv(5)), -MID if last else -MID - UP)
+        conv("pd", 16, "HC", 256)
+        tt(wv(17), A("pd", 16, 32), bW, EQ)
+        at("cnt")
+        scan(A("tmpc"), A("dq"), A("pn", 0, 256), ADD, MIN)
+        cnt = A("tmpc", 15, 256, 16)
+        at("seat")
         n = 96 if last else 128
-        if OPT["sc"]:
-            mm(A("pd", 16, 32), A("If", 0, 128), A("nW", 128, 144), True, False)
-            conv("pd", 16, "Q16", "HC", 256, start=False, a=256)
-            ts(wv(17), A("pd", 16, 32), 0.0, EQ)
-            at("cnt")
-            scan(A("tmpc"), A("dq"), A("pn", 0, 256), ADD, MIN)
-            for r in range(16):
-                mm(cnt, A("TM", 128 * r, 128 * r + 128), A("E", r, 16 * 272, 272), r == 0, False)
-            mm(cnt, A("I15"), A("ones", 0, 16), False, False)
-            merge(17)
-            mm(cnt, A("I32"), A("tmpc", 15, 256, 16), False, True)
-            at("seat")
-            tt(A("q0", 1, 32, 2), cnt, A("thr", 0, 16), LT)
-            tt(A("q0", 33, 64, 2), cnt, A("thr", 0, 16), LT)
-            merge(2)
-            if OPT["sc"] == 2:
-                scan(A("q2", 0, 64), A("q0", 0, 64), A("q1", 0, 64), MUL, ADD)
-                ts(A("sl", 64 * t, 64 * t + 32), A("q2", 1, 64, 2), MID, ADD)
-                at("seat2")
-        else:
-            at("cnt")
-            act(A("HC", 16, 256), A("pn", 16, 256), scale=1.0 / 16)
-            for r in range(16):
-                mm(cnt, A("TM", 128 * r, 128 * r + 128), A("E", r, 16 * 272, 272), r == 0, False)
-            merge(16)
-            mm(A("pc", 16, 32), A("If", 0, 128), A("nW", 128, 144), False, False)
-            conv("pc", 0, "Q16", "HC", 512, start=False)
-            at("seat")
-            tt(A("q0", 1, 32, 2), cnt, A("thr", 0, 16), LT)
-            ts(wv(17), A("pc", 16, 32), 0.0, EQ)
-            tt(A("q0", 33, 64, 2), cnt, A("thr", 0, 16), LT)
-            merge(3)
+        tt(A("q0", 1, 32, 2), cnt, A("thr"), LT)
+        tt(A("q0", 33, 64, 2), cnt, A("thr"), LT)
+        merge(2)
         if not last:
             ts(A("q0", 97, 128, 2), cnt, 0.5, LT)
         tt(A("q0", 65, 96, 2), wv(17), A("q0", 1, 32, 2), MUL)
-        a = 64 if OPT["sc"] == 2 else 0
-        scan(A("q2", a, n), A("q0", a, n), A("q1", a, n), MUL, ADD)
-        ts(A("sl", 64 * t + a // 2, 64 * t + n // 2), A("q2", a + 1, n, 2), MID, ADD)
-        sl = lambda j, t=t: A("sl", 64 * t + 16 * j, 64 * t + 16 * j + 16)
-
-        def parents():
-            at("par")
-            tt(I(KINS, sl(1)), A("KWn", 256, 512), A("nrow"), MAX)
-
-        if OPT["pf"] == 2 or last:
-            parents()
+        scan(A("q2", 0, n), A("q0", 0, n), A("q1", 0, n), MUL, ADD)
+        ts(A("sl", 64 * t, 64 * t + n // 2), A("q2", 1, n, 2), MID, ADD)
+        sl = lambda j: A("sl", 64 * t + 16 * j, 64 * t + 16 * j + 16)
+        at("par")
+        tt(I(KINS, sl(1)), A("KWn", 256, 512), A("nrow"), MAX)
         at("KN")
+        act(A("KS") if last else A("KN", lo, lo + 256), I(A("KWn"), sl(0)), func=ACT.Abs)
+        at("XC")
         if last:
-            act(A("KS"), I(A("KWn"), sl(0)), func=ACT.Abs)
-            at("XC")
             lin("XS", A("XS"), I(A("XWn", xw, xw + 512), sl(0)))
-            dma("Y", ext("yk", 256 * r_, 256 * r_ + 256), A("KS"), 3000)
-            dma("Y", ext("yx", 256 * r_, 256 * r_ + 256), A("XS"), 3000)
+            dma("Y", ext("yk", 256 * r_, 256 * r_ + 256), A("KS"))
+            dma("Y", ext("yx", 256 * r_, 256 * r_ + 256), A("XS"))
         else:
-            act(A("KN", lo, lo + 256), I(A("KWn"), sl(0)), func=ACT.Abs)
-            at("XC")
             lin("XC", XC(lo, lo + 256), I(A("XWn", xw, xw + 512), sl(0)))
-            if OPT["xx"] == "G":
-                asel(X(lo, lo + 256), XC(lo, lo + 256), [[0, 256]], 0, 0)
-            else:
-                cp(X(lo, lo + 256), XC(lo, lo + 256))
-            if OPT["pf"] == 1:
-                parents()
+            asel(X(lo, lo + 256), XC(lo, lo + 256), [[0, 256]], 0, 0)
             early_kin(t + 1)
-            if OPT["pf"] == 0:
-                parents()
         at("FT")
         tt(A("fw"), wv(15), A("q2", 33, 64, 2), MIN)
         mm(A("pn", 0, 256), A("Im"), A("g16", 0, 256), True, False)
@@ -837,8 +719,7 @@ def build(T, topo, core, rank):
             mm(A("pn", r, 256, 16), A("If", r, r + 128), A("fw"), False, r == 15)
         merge(16)
         at("foot")
-        up = lo if last else lo + UP
-        scatter("foot", I(FEET, sl(2)), A("ID", up, up + 256))
+        scatter("foot", I(FEET, sl(2)), ID(lo, lo + 256) if last else A("nup"))
         at("FT")
         tt(A("KN", fl, fl + 256), A("KN", fl, fl + 256), A("pn", 0, 256), ADD)
         at("Aout")
@@ -848,15 +729,16 @@ def build(T, topo, core, rank):
             merge(2)
             act(wv(21), A("pc", 32, 48), bias=-15.5 / 16, accum=A("aout", 8 * t, 8 * t + 1))
             pa = (A("ain", 8 * t + 8, 8 * t + 16), A("aout", 8 * t, 8 * t + 8))
-            send(nxt, [pa] if t == VIS - 2 else [pa, (A("oin", 16 * t + 16, 16 * t + 32), sl(3))], HOP)
+            send(nxt, [pa] if t == VIS - 2 else [pa, (A("oin", 16 * t + 16, 16 * t + 32), sl(3))])
         else:
             for h in (1, 0):
-                at("t%d" % h)
+                at("T%d" % h)
                 bb, a = A("bb", 128 * h, 128 * h + 128), 64 * t - 16 + 8 * h
-                act(bb, I(A("ID"), bi(h)))
+                act(bb, I(ID(0, W_), bi(h)))
                 cp(I(A("TT"), A("sl", a, a + 8)), bb)
-            dma("Y", ext("yt"), A("TT", 0, W_, 1, row0), 3000)
-            dma("S", ext("yp"), A("KN", 0, B_, 1, row0), 3000)
+            at("out")
+            dma("Y", ext("yt"), A("TT", 0, W_, 1, row0))
+            dma("S", ext("yp"), A("KN", 0, B_, 1, row0))
             for j in others:
                 dma("S", ext("yk", 256 * j, 256 * j + 256, slice(*row0)),
                     A("KN", B_ + 256 * j, B_ + 256 * j + 256, 1, row0))
@@ -864,8 +746,7 @@ def build(T, topo, core, rank):
     return ops
 
 
-def plan(ops):
-    n = len(ops)
+def depend(ops):
     hist = {}
     bank = lambda name: name in SCRATCH and SCRATCH[name][0] == "psum"
     for i, o in enumerate(ops):
@@ -889,341 +770,38 @@ def plan(ops):
                     h[:] = [e for e in h if not (a <= e[2] and e[3] <= b)]
                 h.append((i, wr, a, b))
         dep.pop(i, None)
-        if "after" in o:
-            dep[o["after"]] = dep.get(o["after"], False)
         if o["k"] == "r":
             dep = {o["x"][2]: False}
         o["dep"] = dep
-    return arrange(ops)
 
 
 def arrange(ops):
-    n = len(ops)
-    dur = [0.0 if o["k"] == "r" else 60.0 if o["k"] == "d" else o["c"] for o in ops]
-    before = [[(j, ops[j]["c"] + (SW if ops[j]["e"] == o["e"] else XW) if w else dur[j]) for j, w in o["dep"].items()]
-              for o in ops]
-
-    after = [[] for _ in ops]
-    for i in range(n):
-        for j, l in before[i]:
-            after[j].append((i, l + dur[i] - dur[j]))
-
-    def place(order, edges, first):
-        busy = {}
-        at = [0.0] * n
-        for i in order:
-            s = first[i]
-            for j, l in edges[i]:
-                if at[j] + l > s:
-                    s = at[j] + l
-            d = dur[i]
-            if d:
-                lst = busy.setdefault(ops[i]["e"], [])
-                a, b = 0, len(lst)
-                while a < b:
-                    m = (a + b) // 2
-                    if lst[m][1] <= s:
-                        a = m + 1
-                    else:
-                        b = m
-                while a < len(lst) and s + d > lst[a][0]:
-                    s = max(s, lst[a][1])
-                    a += 1
-                lst.insert(a, (s, s + d))
-            at[i] = s
-        return at
-
-    level = [0.0] * n
-    floor = [0.0] * n
-    for i in range(n - 1, -1, -1):
-        level[i] = max(level[i] + ops[i]["c"] + BOOST.get(ops[i]["e"] + ops[i]["b"], 0), floor[i])
-        for j, l in before[i]:
-            level[j] = max(level[j], level[i] + l - ops[j]["c"])
-            floor[j] = max(floor[j], level[i] + 0.01)
-    tail = [ops[i]["c"] - dur[i] for i in range(n)]
-    at = place(sorted(range(n), key=lambda i: (-level[i], i)), before, [0.0] * n)
-    best, end = at, max(at[i] + ops[i]["c"] for i in range(n))
-    for _ in range(PASSES):
-        back = place(sorted(range(n), key=lambda i: (-at[i] - dur[i], -i)), after, tail)
-        at = place(sorted(range(n), key=lambda i: (-back[i] - dur[i], i)), before, [0.0] * n)
-        e = max(at[i] + ops[i]["c"] for i in range(n))
-        if e < end:
-            best, end = at, e
-    return best, end
-
-
-def polish(ops, start, rounds):
-    n = len(ops)
-    above, deps = [], []
+    named = {}
     for i, o in enumerate(ops):
-        far = 0
-        for j in o["dep"]:
-            far |= above[j]
-        deps.append({j: w for j, w in o["dep"].items() if ops[j]["k"] != "c" or not far >> j & 1})
-        for j in o["dep"]:
-            far |= 1 << j
-        above.append(far)
-    cases = []
-    for fig in CASES:
-        c = [sum(a * b for a, b in zip(o["cv"], (1.0,) + fig[:6])) for o in ops]
-        du = [0.0 if o["k"] == "r" else fig[8] * len(o["f"]) if o["k"] == "d" else c[i] for i, o in enumerate(ops)]
-        lag = [[(j, c[j] + (fig[7] if ops[j]["e"] == o["e"] else fig[6]) if w else du[j]) for j, w in deps[i].items()]
-               for i, o in enumerate(ops)]
-        cases.append((c, du + [0.0], lag))
-    name, seen = [], {}
-    for o in ops:
-        k = (o["e"], o["b"], o["v"])
-        seen[k] = seen.get(k, 0) + 1
-        name.append(k + (seen[k],))
-    index = {k: i for i, k in enumerate(name)}
-    needed = set(j for d in deps for j in d)
-    final = [i for i in range(n) if i not in needed]
-    queue = ["VSPGYR".index(o["e"]) for o in ops]
-
-    def timed(order, first=0, than=None, slack=0.0, grow=1.0):
-        prev, last = [n] * n, [n] * 6
-        for i in order:
-            e = queue[i]
-            if e < 5:
-                prev[i] = last[e]
-                last[e] = i
-        total, runs = 0.0, []
-        parts = [order[first:first + LOOK], order[first + LOOK:]]
-        for m, (c, du, lag) in enumerate(cases):
-            at, why = (than[1][m][0][:], than[1][m][1][:]) if first else ([0.0] * (n + 1), [n] * n)
-            for rest in parts:
-                for i in rest:
-                    p = prev[i]
-                    s = at[p] + du[p]
-                    for j, l in lag[i]:
-                        l += at[j]
-                        if l > s:
-                            s = l
-                            p = j
-                    at[i] = s
-                    why[i] = p
-                if than and rest is parts[0] and parts[1]:
-                    old = than[1][m][0]
-                    late = min(at[i] - old[i] for i in rest[-12:])
-                    if total + late * grow > (than[1][m - 1][4] if m else 0) + slack + EARLY:
-                        return None
-            end, i = max((at[i] + c[i], i) for i in final)
-            worth = end + MEAN * sum(at) / n
-            total += worth
-            runs.append((at, why, i, end, total))
-            if than and total > than[1][m][4] + slack + (SLACK if m + 1 < len(cases) else 0):
-                return None
-        return total, runs, prev
-
-    order = sorted(range(n), key=lambda i: (start[i], i))
-    now = best = timed(order)
-    place = {i: k for k, i in enumerate(order)}
-    lines = [[i for i in order if queue[i] == e] for e in range(6)]
-    seed = [SEED]
-
-    def draw(m):
-        seed[0] = (seed[0] * 1103515245 + 12345) % 2147483648
-        return (seed[0] >> 8) % m
-
-    for r in range(rounds):
-        at, why, i = now[1][draw(len(cases))][:3]
-        if draw(100) < ANY:
-            i = draw(n)
-        pairs, prev = [], now[2]
-        while i < n:
-            p = why[i]
-            if p < n and p == prev[i] and not above[i] >> p & 1:
-                pairs.append((p, i))
-            i = p
-        if not pairs:
-            continue
-        u, v = pairs[draw(len(pairs))]
-        q = lines[queue[u]]
-        far, ahead, a = (0, 0, 1, 2, 3, 5, 8, 13, 21, 34)[draw(10)], draw(2), (u, v)[draw(2)]
-        far += (a == v) != ahead
-        b = q[max(q.index(u) - far, 0)] if ahead else q[min(q.index(v) + far, len(q) - 1)]
-        alone = min(name[a][2], name[b][2]) < 1 or (name[a][2] == VIS - 1 and draw(2))
-        new, first = list(order), n
-        for d in (0,) if alone else range(-VIS, VIS + 1):
-            x, y = (index.get(name[z][:2] + (name[z][2] + d, name[z][3])) for z in (a, b))
-            if x is None or y is None or (d and min(name[x][2], name[y][2]) < 1):
-                continue
-            i, j = (place[x], place[y]) if first == n else (new.index(x), new.index(y))
-            if ahead and j < i:
-                up = above[x] | 1 << x
-                part = new[j:i + 1]
-                new[j:i + 1] = [k for k in part if up >> k & 1] + [k for k in part if not up >> k & 1]
-            elif not ahead and i < j:
-                part = new[i:j + 1]
-                new[i:j + 1] = sorted(part, key=lambda k: k == x or above[k] >> x & 1)
-            first = min(first, i, j)
-        if new == order:
-            continue
-        trial = timed(new, first, now, SLACK * (1 - r / rounds), 1.5 if alone else 1.5 * (n - first) / LOOK)
-        if trial:
-            now = trial
-            at = trial[1][0][0]
-            order = sorted(new, key=lambda k: at[k])
-            place = {i: k for k, i in enumerate(order)}
-            lines = [[i for i in order if queue[i] == e] for e in range(6)]
-            if now[0] < best[0]:
-                best = now
-    return best[1][0][0][:n], [int(x[3]) for x in best[1]]
+        named.setdefault((o["e"], o["b"], o["v"]), []).append(i)
+    need = [set(o["dep"]) for o in ops]
+    for e, lists in ORDER.items():
+        before, done = None, set()
+        for v in range(VIS):
+            for word in lists[(v > 0) + (v == VIS - 1)].split():
+                name, _, nth = word.partition(".")
+                calls = named.get((e, name.rstrip("-"), v - name.endswith("-")), [])
+                calls = calls[int(nth) - 1:int(nth)] if nth else [i for i in calls if i not in done]
+                if calls:
+                    done.add(calls[0])
+                    need[calls[0]].add(before)
+                    before = calls[0]
+    order, placed = [], {None}
+    while len(order) < len(ops):
+        ready = [i for i in range(len(ops)) if i not in placed and need[i] <= placed]
+        assert ready
+        order += ready
+        placed.update(ready)
+    return order
 
 
-def improve(ops, start, rounds, CASES, SLACK):
-    n = len(ops)
-    above, deps = [], []
-    for i, o in enumerate(ops):
-        far = 0
-        for j in o["dep"]:
-            far |= above[j]
-        deps.append({j: w for j, w in o["dep"].items() if ops[j]["k"] != "c" or not far >> j & 1})
-        for j in o["dep"]:
-            far |= 1 << j
-        above.append(far)
-    cases = []
-    for fig in CASES:
-        c = [sum(a * b for a, b in zip(o["cv"], (1.0,) + fig[:6])) for o in ops]
-        du = [0.0 if o["k"] == "r" else fig[8] * len(o["f"]) if o["k"] == "d" else c[i] for i, o in enumerate(ops)]
-        lag = [[(j, c[j] + (fig[7] if ops[j]["e"] == o["e"] else fig[6]) if w else du[j]) for j, w in deps[i].items()]
-               for i, o in enumerate(ops)]
-        cases.append((c, du + [0.0], lag))
-    name, seen = [], {}
-    for o in ops:
-        k = (o["e"], o["b"], o["v"])
-        seen[k] = seen.get(k, 0) + 1
-        name.append(k + (seen[k],))
-    index = {k: i for i, k in enumerate(name)}
-    needs = [list(d) for d in deps]
-    needed = set(j for d in deps for j in d)
-    final = [i for i in range(n) if i not in needed]
-    queue = ["VSPGYR".index(o["e"]) for o in ops]
-    seed = [SEED]
-
-    def draw(m):
-        seed[0] = (seed[0] * 1103515245 + 12345) % 2147483648
-        return (seed[0] >> 8) % m
-
-    def place(key, old, least):
-        c, du, lag = cases[0]
-        order = sorted(range(n), key=lambda i: key[i])
-        begin, end = [[] for _ in range(6)], [[] for _ in range(6)]
-        at = old[:]
-        for i in order:
-            d = du[i]
-            if key[i] < least:
-                if d:
-                    begin[queue[i]].append(at[i])
-                    end[queue[i]].append(at[i] + d)
-                continue
-            s = 0.0
-            for j, l in lag[i]:
-                l += at[j]
-                if l > s:
-                    s = l
-            if d:
-                a, b = begin[queue[i]], end[queue[i]]
-                p = m = len(b)
-                while p and b[p - 1] > s:
-                    p -= 1
-                while p < m and s + d > a[p]:
-                    if b[p] > s:
-                        s = b[p]
-                    p += 1
-                a.insert(p, s)
-                b.insert(p, s + d)
-            at[i] = s
-        return at
-
-    def timed(at0, than, slack):
-        total = max(at0[i] + cases[0][0][i] for i in final) + MEAN * sum(at0) / n
-        if than and total > than[1][0][4] + slack + SLACK:
-            return None
-        order = sorted(range(n), key=lambda i: at0[i])
-        prev, last = [n] * n, [n] * 6
-        for i in order:
-            e = queue[i]
-            if e < 5:
-                prev[i] = last[e]
-                last[e] = i
-        runs = [(0, 0, 0, 0, total)]
-        if than and len(cases) == 1 and total > than[0] + slack:
-            return None
-        for m in list(range(1, len(cases))) + [0]:
-            c, du, lag = cases[m]
-            at, why = [0.0] * (n + 1), [n] * n
-            for i in order:
-                p = prev[i]
-                s = at[p] + du[p]
-                for j, l in lag[i]:
-                    l += at[j]
-                    if l >= s:
-                        s = l
-                        p = j
-                at[i] = s
-                why[i] = p
-            end, i = max((at[i] + c[i], i) for i in final)
-            if m == 0:
-                runs[0] = (at, why, i, end, runs[0][4])
-                break
-            total += end + MEAN * sum(at) / n
-            runs.append((at, why, i, end, total))
-            if than and total > than[1][m][4] + slack + (SLACK if m + 1 < len(cases) else 0):
-                return None
-        return total, runs, prev
-
-    now = best = timed(place(start, [0.0] * (n + 1), -1.0), None, 0)
-    for r in range(rounds):
-        old = now[1][0][0]
-        key = old[:]
-        why, i = now[1][draw(len(cases))][1:3]
-        if draw(100) < ANY:
-            i = draw(n)
-        pairs, prev = [], now[2]
-        while i < n:
-            p = why[i]
-            if p < n and p == prev[i] and not above[i] >> p & 1:
-                pairs.append((p, i))
-            i = p
-        if draw(100) < FREE:
-            a, d = draw(n), (-1500, -800, -400, -200, -100, 100, 200, 400, 800, 1500)[draw(10)]
-        elif pairs:
-            u, v = pairs[draw(len(pairs))]
-            d = key[v] - key[u] + (1, 1, 200, 500, 1000)[draw(5)]
-            a, d = ((u, d), (v, -d))[draw(2)]
-        else:
-            continue
-        k = name[a]
-        alone = k[2] < 1 or (k[2] == VIS - 1 and draw(10) < 4)
-        least = 1e9
-        for x in [a] if alone else [index[z] for z in [k[:2] + (v, k[3]) for v in range(1, VIS)] if z in index]:
-            least = min(least, key[x], key[x] + d)
-            key[x] += d
-            todo = [x] if d < 0 else []
-            while todo:
-                y = todo.pop()
-                for j in needs[y]:
-                    if key[j] > key[y] - 1:
-                        key[j] = key[y] - 1
-                        least = min(least, key[j])
-                        todo.append(j)
-        if d > 0:
-            for i in range(a if alone else index.get(k[:2] + (1, k[3]), 0), n):
-                for j in needs[i]:
-                    if key[j] >= key[i]:
-                        key[i] = key[j] + 0.01
-        trial = timed(place(key, old, least), now, SLACK * (1 - r / rounds))
-        if trial:
-            now = trial
-            if now[0] < best[0]:
-                best = now
-    return best[1][0][0][:n], [int(x[3]) for x in best[1]]
-
-
-def emit(g, T, ops, start):
+def emit(g, T, ops, order):
     queue = {"V": g.vector, "S": g.scalar, "P": g.tensor, "G": g, "Y": g.sync}
-    order = sorted(range(len(ops)), key=lambda i: (start[i], i))
     place = {}
     seq = {}
     for i in order:
@@ -1240,14 +818,11 @@ def emit(g, T, ops, start):
             clock[i] = {("o", i): 1}
             continue
         kn = known[o["e"]]
-        wl = []
-        for j in sorted(o["dep"], key=lambda j: -start[j]):
-            if not o["dep"][j]:
-                continue
-            key, val = (ops[j]["e"], place[j]) if ops[j]["k"] == "c" else (("o", j), 1)
-            if kn.get(key, 0) >= val:
-                continue
-            wl.append(j)
+        sign = lambda j: (ops[j]["e"], place[j]) if ops[j]["k"] == "c" else (("o", j), 1)
+        covers = lambda seen, j: seen.get(sign(j)[0], 0) >= sign(j)[1]
+        wl = [j for j in o["dep"] if o["dep"][j] and not covers(kn, j)]
+        wl = [j for j in wl if not any(k != j and covers(clock[k], j) for k in wl)]
+        for j in wl:
             marked.add(j)
             for k2, v2 in clock[j].items():
                 if kn.get(k2, 0) < v2:
@@ -1301,10 +876,5 @@ def rank_program(g, core, T, topo):
     if rank is None:
         return
     ops = build(T, topo, core, rank)
-    start = plan(ops)[0]
-    if not PLAN:
-        PLAN.append(polish(ops, improve(ops, start, FIRST, [PLACE], 40)[0], ROUNDS)[0])
-    start = list(PLAN[0])
-    for i, o in enumerate(ops):
-        start[i] = max([start[i]] + [start[j] + 0.01 for j in o["dep"]])
-    emit(g, T, ops, polish(ops, start, 0)[0])
+    depend(ops)
+    emit(g, T, ops, arrange(ops))

from concourse.bass import DstId, RemoteDMATransfer
from concourse.mybir import AluOpType as ALU, ActivationFunctionType as ACT

W_, B_, L_, VIS = 3584, 2560, 256, 5
F0, DK = 3856, 3600
FW, FO, DF = 1296, 2552, 1032
FB = F0 - FO
UP = 1024
MID = 1792.0
WT = 2176.0
BIG = 12582912.0
SPLIT = [[[(48, 2), (48, 2)], [(48, 1), (48, 2)]], [[(48, 2), (32, 2)], [(48, 1), (56, 2)]]]
CUT = (64, 96)
BANKS = [[("pn", "pd"), ("pc", "pw")], [("pd",), ("pw", "pc")]]
GFILL = "KN nrow aout o0 q0 onef dq"
KCUT = (2560, 3584, 0, 1024, 1024, 2048, 2048, 2560)
SCALAR = "v0 v1 t0 t1 hit kin01 colY xs0 xs1 lvN wt stay foot gy fu turn down kn0 kn2560 bb0 bb1 T0 T1"
ORDER = {
    "V": ["""ones- Z- t16- ci- cf- Z-.4 cf-.6 cw- BD- cf- b16- cf-.5 CK- cf- Ib- ftf- yu cf- cu- Z- tmpb- PH- v16- Pm-
          PF- PF0- RE- KN- KN- yu yu py t1- CK- live t0- live kin00 CK- held wts CK- held kin00 held kin01- held
          gv01 p16 gv00 A01 p16 B01 xp A00 xp B00 trf- dec01 turn dec01 turn dec01 dec00 turn stay dec00 dec01 stay
          kin11 dec00 kin11 gv11 dec00 stay kin10 BO- kin10 gv10 A11 B11 C11 A10 B10 dec11 dec11 Dq- dec11 dec10 Z-
          dec10 dec11 dec10 brow1 E8 dec10 E12 brow0 zn1 E0 may E3 vl E6 vl zn0 may.3 cnt may seat seat hit seat seat
          seat FT par""",
          """yu XC- FT- t1- yu yu py t0- kin01- live kin00 live gv01 held wts held held kin00 held Ain p16 A01 gv00 p16
          B01 xp A00 xp B00 dec01 turn dec01 turn dec01 dec00 dec01 dec00 stay kin11 dec00 stay kin11 gv11 dec00 stay
          kin10 turn kin10 gv10 A11 B11 C11 A10 B10 dec11 dec11 dec11 dec10 dec10 dec11 dec10 brow1 E8 dec10 E12
          brow0 may E0 zn1 E3 vl E6 vl may zn0 may cnt seat seat hit seat seat seat FT par""",
          """yu XC- FT- t1- yu yu py t0- kin01- live kin00 live gv01 held wts held held kin00 held Ain p16 A01 gv00 p16
          B01 xp A00 xp B00 dec01 turn dec01 turn dec01 home- dec00 dec01 dec00 stay kin11 dec00 stay kin11 gv11
          dec00 stay kin10 turn kin10 gv10 A11 B11 C11 A10 B10 dec11 dec11 dec11 dec10 dec10 dec11 dec10 brow1 E8
          dec10 E12 brow0 E0 may E3 vl vl E6 may zn0 zn1 may cnt seat hit seat seat seat FT par T1 XC T0 FT"""],
    "S": ["""fsd- bsd- cq- d0- zin- CB- q1- o1- cw- c64- I1- t16- In- KN- KN-.3 cf- I8- e16- ZN- KN- yu I0- ZN- nW- CB-
          fu live kin01- Pf-.2 wts colY ZN- SH- Pf- d0- wts gs01 gs00 C01 D01 C00 D00 c17- Ih- stay gs11 gs10 D11 C10
          D10 turn zn1 v1 v0 Im- zn0 may may hit v0 Aout t1 foot""",
          """yu t0- KN- kin01- live fu colY wts gs01 gs00 Ain C01 Ain D01 C00 D00 wts stay gs11 gs10 D11 C10 D10 turn
          v1 zn1 v0 zn0 may T1 may T1 hit T0 v0 T0 Aout t1 foot""",
          """yu t0- KN- kin01- live fu colY wts gs01 gs00 Ain C01 Ain D01 C00 D00 wts stay gs11 gs10 D11 C10 D10 turn
          v1 down.2 v0 zn0 zn1 down may hit may v0 T1 foot T0 KN out out out out"""],
    "P": ["""pd- pd- colY t0- yu t1- pd- colY held held kin00 kin00 kin01- kin01- D01 z01 key00 key01 C01 z00 C00 neg01
          neg00 p16 C01 D01 neg01 A01 D00 C00 C01 D00 B01 D01 neg00 par01 dec01 A00 C00 B00 D00 par00 dec00 dec01 D11
          dec01 dec00 D10 C10 key11 z11 dec00 z10 key11 key10 key11 neg11 key10 key10 D11 neg10 neg11 A11 C10 D10 D11
          B11 C11 neg10 A10 C10 B10 D10 dec11 dec11 dec10 zn1 zn0 E8 dec10 zn1 E8 E12 vl zn0 E0 E3 E6 hit Aout FT FT
          t1""",
          """colY yu t0- kin01- kin01- C01 colY kin00 held held z01 kin00 key01 D01 z00 neg01 key00 C01 neg00 p16 D01
          neg01 A01 D00 C00 C00 C01 D00 B01 D01 par01 dec01 neg00 A00 C00 B00 D00 par00 dec00 dec01 dec01 z10 D11 C10
          dec00 z11 dec00 D10 key11 key11 key10 key11 neg11 neg11 D11 key10 key10 C10 D10 neg10 A11 D11 B11 C11 neg10
          A10 C10 B10 D10 dec11 E8 dec11 zn0 zn1 dec10 dec10 E8 zn1 E12 vl E0 zn0 E3 E6 hit Aout FT FT t1""",
          """colY yu t0- kin01- kin01- C01 colY kin00 held held z01 kin00 key01 D01 z00 neg01 key00 C01 neg00 p16 neg01
          A01 D01 D00 C00 C00 D00 C01 B01 D01 par01 dec01 neg00 A00 C00 B00 D00 par00 dec00 dec01 dec01 z10 D11 C10
          dec00 z11 dec00 key11 key11 D10 key10 key11 neg11 neg11 D11 key10 key10 C10 D10 neg10 A11 D11 B11 C11 neg10
          A10 C10 B10 D10 dec11 E8 dec11 zn0 dec10 zn1 dec10 E8 E12 vl E0 zn0 E3 zn1 E6 hit FT FT"""],
    "G": ["""ci- tmpc-.3 tmpc-.4 If- KN-.4 KN-.3 KN-.2 KN-.5 tmpb- tmpc- tmpc- Qh- KN-.6 KN- CK- far- o0- SF- zp1 ID-.6
          PH0-.2 PH0- zp1.3 onef- zp1.4 zp0.4 aout- dq- zp0 zp0 zp1 q0- ID-.2 zp0 ID-.5 nup trf- ID-.3 stay ID-.4
          ID-.7 dq- ID- BL- dq- dec11 dq- nrow- dec10 zn1 zn0 may Aout far XC""",
          "zp0 zp1.2 zp0.4 zp1 zp1 zp0.3 zp1 zp0 stay dec11 dec10 nup zn1 may zn0 Aout far XC",
          "zp1.2 zp0 zp0.4 zp1 zp1 zp0.3 zp1 zp0 stay home- dec11 dec10"],
    "Y": ["kst- kst- kst- kst- XX- XX- trs- XX- TT yu p16 colY TT p16",
          "colY p16.2 yu p16",
          "down.6 colY down.4 home- down.2 down down.5 p16.2 yu down p16 home- XC.2 XC out out zn0"],
}

SB, F32, BF, F16, I32, U16 = "sbuf", "float32", "bfloat16", "float16", "int32", "uint16"
SCRATCH = {}
for _d, _l in ((I32, "kst 3584 fsd 64 bsd 16 trs 224 ci 8 R 544 Di 32"),
               (F32, "KN 5152 ID 3584 nup 256 TT 3856 trf 224 trt 224 trh 224 ftf 64 onef 128 tmpc 256 cf 40 cw 96 c17 16 d0 272 "
                     "ain 40 aout 40 acc 8 colY 256 dq 256 yrow 256 nrow 256 KS 256 "
                     "KWn 512 bb 256 thr 16 Pf 256 w 512 q0 128 q1 128 q2 128 o0 64 o1 64 o2 64"),
               (BF, "XX 7424 ones 272 BO 128 BL 128 Dq 256 Ib 128 Ih 128 In 128 I8 128 BD 48 CK 544 CB 272 "
                    "RE 64 Pm 128 zp 256 cq 128 tmpb 272 zin 1280 x0b 2048 x1b 2048 m0b 2048 m1b 2048 "
                    "xs 256 D 32 Z 1152 E 4352 XS 256 XWn 2560 xp 256 mp 256 lv 16 c64 24 ZN 1088"),
               (F16, "Qh 144 HC 256 If 144 Im 128 I0 128 I1 128 SH 16 SF 8 PH 272 PH0 272 PF 136 PF0 136 "
                     "g16 512 e16 512 v16 256 t16 256 p16 256 c16 256 nW 64 brow 256 b16 16 fw 16"),
               (U16, "cu 4 bin 80 oin 80 bU 32 bO 80 cU 256 u 256 sl 320")):
    _l = _l.split()
    for _n, _c in zip(_l[::2], _l[1::2]):
        SCRATCH[_n] = (SB, [128, int(_c)], _d)
for _n in ("tin", "tback"):
    SCRATCH[_n] = ("dram", [128, 224], F32)
for _n in ("pk0", "pk1", "pz0", "pz1", "pd", "pw", "pc", "pn"):
    SCRATCH[_n] = ("psum", [128, 512], F32)
SEMAPHORES = ["eV", "eS", "eP", "eG", "sent"] + ["d%d" % i for i in range(80)] + ["r%d" % i for i in range(36)]


def build(T, topo, core, rank):
    ops = []
    tag = [None, -1]
    N = len(T.cores)
    nxt, prv = T.cores[(rank + 1) % N], T.cores[(rank - 1) % N]

    def A(name, a=0, b=None, s=1, p=None):
        if b is None:
            b = SCRATCH[name][1][1]
        ps = slice(None) if p is None else slice(*p)
        ap = T[name][ps, a:b] if s == 1 else T[name][ps, a:b:s]
        return (ap, [(name, a, b)], len(range(a, b, s)), SCRATCH[name][2], False)

    def I(win, off):
        return (win[0].indirect(off[0]), win[1] + off[1], off[2] * 16, win[3], True, off[1])

    def parts(ap, names, a, b):
        return (ap[0], [(n, a, b) for n in names]) + ap[2:]

    def add(eng, fn, r, w, kind="c", extra=None):
        ops.append({"e": eng, "f": [fn], "r": r, "w": w, "k": kind, "x": extra,
                    "b": tag[0] or (w or r)[0][0], "v": tag[1]})
        return len(ops) - 1

    def at(name, t=None):
        tag[0] = name
        if t is not None:
            tag[1] = t

    def merge(n):
        o = ops[-n]
        for p in ops[len(ops) - n + 1:]:
            o["f"] = o["f"] + p["f"]
            o["r"] = o["r"] + [x for x in p["r"] if x not in o["r"]]
            o["w"] = o["w"] + [x for x in p["w"] if x not in o["w"]]
        del ops[len(ops) - n + 1:]

    def rw(out, ins):
        r = []
        for i in ins:
            if isinstance(i, tuple):
                r = r + i[1]
        return (r + out[5], out[1][:1]) if out[4] else (r, out[1])

    def sv(s):
        return s[0] if isinstance(s, tuple) else s

    def cp(out, in_):
        add("V", lambda q: q.tensor_copy(out[0], in_[0]), *rw(out, [in_]))

    def tt(out, in0, in1, op):
        add("V", lambda q: q.tensor_tensor(out[0], in0[0], in1[0], op), *rw(out, [in0, in1]))

    def ts(out, in0, s1, op0, s2=None, op1=None):
        if op1 is None:
            f = lambda q: q.tensor_scalar(out[0], in0[0], sv(s1), None, op0)
        else:
            f = lambda q: q.tensor_scalar(out[0], in0[0], sv(s1), sv(s2), op0, op1)
        add("V", f, *rw(out, [in0, s1, s2]))

    def ms(out, val):
        add("V", lambda q: q.memset(out[0], val), [], out[1])

    def scan(out, a, b, op0, op1):
        add("V", lambda q: q.tensor_tensor_scan(out[0], a[0], b[0], 0.0, op0, op1), *rw(out, [a, b]))

    def act(out, in_, bias=0.0, scale=1.0, func=ACT.Identity, accum=None):
        r, w = rw(out, [in_, bias, scale])
        if out[4]:
            f = lambda q: q.activation(out[0], in_[0], func)
        elif accum is None:
            f = lambda q: q.activation(out[0], in_[0], func, bias=sv(bias), scale=sv(scale))
        else:
            w = w + accum[1]
            f = lambda q: q.activation(out[0], in_[0], func, bias=sv(bias), scale=sv(scale), accum_out=accum[0])
        add("S", f, r, w)

    def mm(out, lhsT, rhs, start, stop):
        add("P", lambda q: q.matmul(out[0], lhsT[0], rhs[0], start, stop), lhsT[1] + rhs[1], out[1])

    def iota(out, pat, base, cm):
        if out[3] == I32:
            f = lambda q: q.iota(out[0], pat, base, cm)
        else:
            f = lambda q: q.iota(out[0], pat, base, cm, allow_small_or_imprecise_dtypes=True)
        add("G", f, [], out[1])

    def asel(out, in_, pat, base, cm, op=ALU.is_equal, other=0.0):
        add("G", lambda q: q.affine_select(out[0], in_[0], pat, op, other, base, cm), in_[1], out[1])

    def dma(eng, out, in_):
        add(eng, lambda q: q.dma_start(out[0], in_[0]), in_[1], out[1], "d")

    def ext(name, a=None, b=None, rows=slice(None)):
        if a is None:
            return (T[name][:], [(name, 0, 1)])
        return (T[name][rows, a:b], [(name, a, b)])

    nr = [0]

    def send(dst, pairs):
        rid, pid, _ = topo.addr(dst)
        eng = topo.engines(core, dst)
        k = len(eng) // len(pairs)
        sems = []
        r = []
        for o, i in pairs:
            sems.append("r%d" % nr[0])
            nr[0] += 1
            r = r + i[1]
        if len(pairs) == 1:
            o, i = pairs[0]
            f = lambda q: q.remote_dma(o[0], i[0], T.sem[sems[0]], T.sem.sent, pid, rid, topo.mask(core, dst))
        else:
            def f(q):
                tr = []
                for j, (o, i) in enumerate(pairs):
                    m = sum(1 << e for e in eng[j * k:(j + 1) * k])
                    tr.append(RemoteDMATransfer(dst_ids=[DstId(rid=rid, pnc=pid)], dma_engine_mask=m,
                                                remote_sem=T.sem[sems[j]], src=i[0], dst=o[0]))
                return q.remote_dma_fused(tr, local_sem=T.sem.sent)
        s = add("G", f, r, [], "s", k * len(pairs))
        for j, (o, i) in enumerate(pairs):
            add("R", None, [], o[1], "r", (sems[j], k, s))

    EQ, LT, GT, MUL, ADD, SUB, MAX, MIN = (ALU.is_equal, ALU.is_lt, ALU.is_gt, ALU.mult, ALU.add, ALU.subtract, ALU.max, ALU.min)
    row0 = (0, 128, 16)
    KIN, KINS, FEET = A("KN", 0, W_), A("KN", 0, F0), A("KN", F0, F0 + FW)
    X = lambda a=0, b=W_: A("XX", a, b)
    XC = lambda a=0, b=W_: A("XX", W_ + a, W_ + b)
    home = B_ + L_ * rank

    def lin(name, out, in_, bias=0.0, scale=1.0):
        if name in SCALAR.split():
            act(out, in_, bias=bias, scale=scale)
        elif scale != 1.0:
            ts(out, in_, scale, MUL, bias, ADD)
        elif bias != 0.0:
            ts(out, in_, bias, ADD)
        else:
            cp(out, in_)

    def scatter(name, out, in_):
        if name in SCALAR.split():
            act(out, in_, func=ACT.Silu)
        else:
            cp(out, in_)

    def fill(out, val, func=ACT.Identity):
        if out[1][0][0] in GFILL.split():
            iota(out, [[0, out[2]]], int(val), 0)
        else:
            act(out, A("ones", 0, out[2]), scale=val, func=func)

    ms(A("ones"), 1.0)
    dma("S", A("bsd"), ext("bs"))
    dma("S", A("fsd"), ext("ft"))
    for a, b in zip(KCUT[::2], KCUT[1::2]):
        dma("Y", A("kst", a, b), ext("kn", a, b))
        lin("kn%d" % a, A("KN", a, b), A("kst", a, b))
    dma("S", A("zin", 0, 256), ext("z0"))
    dma("Y", A("XX", 2 * W_, 2 * W_ + L_), ext("x0", home, home + L_))
    for a, b in ((0, home), (home + L_, W_)):
        if a < b:
            dma("Y", XC(a, b), ext("x0", a, b))
    merge(2 if home + L_ < W_ else 1)
    dma("Y", A("trs"), ext("tr"))
    dma("Y", X(), ext("x0"))
    lin("trf", A("trf"), A("trs"), float(UP))
    send(nxt, [(ext("tin"), A("trf"))])
    for a in range(W_, F0 + FW, 272):
        fill(A("KN", a, min(a + 272, F0 + FW)), -1.0)
    ts(A("ftf"), A("fsd"), float(UP), ADD)
    dma("S", A("KN", FB + B_, FB + W_, 1, row0), A("ftf"))
    ms(A("t16"), 0.0)
    ts(A("b16"), A("bsd"), MID, SUB)
    dma("S", A("t16", 0, 256, 1, row0), A("b16"))

    fill(A("onef"), -1.0)
    asel(A("Qh"), A("ones", 0, 144), [[-16, 9], [-1000, 16]], 16, 1)
    asel(A("If"), A("ones", 0, 144), [[-1, 144]], 0, 1)
    If = A("If", 0, 128)
    cp(A("Ib"), If)
    act(A("Ih"), If, scale=0.5)
    act(A("In"), If, scale=-1.0)
    act(A("I8"), If, scale=-8192.0)
    iota(A("ci", 0, 1), [[0, 1]], 0, 1)
    ts(A("ci", 1, 2), A("ci", 0, 1), 15, ALU.bitwise_and)
    ts(A("ci", 2, 3), A("ci", 0, 1), 4, ALU.arith_shift_right)
    merge(2)
    cp(A("cf", 0, 2), A("ci", 1, 3))
    cR, cG, m0, m1, sgn, sgm, mid0, far0 = [A("cf", j, j + 1) for j in (0, 1, 8, 9, 32, 33, 34, 35)]
    ts(m0, cR, 0.5, GT)
    ts(m1, cR, 0.5, LT)
    merge(2)
    act(sgn, m0, scale=2.0, bias=-1.0)
    act(sgm, m0, scale=2 * MID, bias=-MID)
    act(far0, m0, scale=float(W_), bias=MID)
    act(mid0, m0, scale=-MID - 32768.0, bias=32768.0)
    merge(4)
    act(A("Im"), If, scale=-1.0)
    act(A("I0"), If, scale=m0)
    act(A("I1"), If, scale=m1)
    ts(A("cf", 10, 11), cR, 7.5, GT, 16.0, MUL)
    ts(A("cf", 11, 12), cR, 16.0, MUL, A("cf", 10, 11), ADD)
    ts(A("cf", 12, 13), cG, 2.0, MUL, 1.0, ADD)
    zl = [A("cu", 0, 1), A("cu", 2, 3)]
    ts(zl[0], cG, 8.0, ADD, A("cf", 11, 12), ADD)
    ts(zl[1], A("cf", 12, 13), A("cf", 11, 12), ADD)
    merge(2)
    ts(A("cf", 14, 15), cR, 8.0, MUL, cG, ADD)
    iota(A("tmpc", 0, 128), [[1, 128]], 0, 0)
    ts(A("Pm"), A("tmpc", 0, 128), A("cf", 14, 15), EQ)
    act(A("Pf", 0, 128), A("Pm"), scale=WT)
    act(A("Pf", 128, 256), A("Pm"), scale=-1.0)
    iota(A("tmpc", 208, 224), [[1, 2], [2, 8]], 0, 0)
    for s, a in enumerate((208, 0)):
        ts(A("RE", 32 * s, 32 * s + 16), A("tmpc", a, a + 16), cR, EQ, 32.0, MUL)
        ts(A("RE", 32 * s + 16, 32 * s + 32), A("tmpc", a, a + 16), cR, EQ)
    merge(4)
    iW, spM = A("cw", 0, 16), A("cw", 64, 96)
    iota(A("tmpc", 160, 176), [[16, 16]], 0, 0)
    ts(iW, A("tmpc", 160, 176), cR, ADD)
    act(A("cw", 64, 80), iW, bias=DK - MID)
    act(A("cw", 80, 96), iW, bias=DF + FO - MID)
    merge(2)
    for j in range(N):
        act(A("nW", 16 * j, 16 * j + 16), iW, MID - B_ - L_ * j, -1.0)
    merge(N)
    for name in ("o0", "q0"):
        fill(A(name), 0.0)
    act(A("o1", 1, 32, 2), iW, bias=float(DK))
    act(A("o1", 33, 64, 2), iW, bias=float(DF))
    merge(2)
    fill(A("q1", 0, 32, 2), 256.0)
    for a, v in ((1, -MID), (33, DK - MID), (65, DF - MID), (97, DK - MID)):
        act(A("q1", a, a + 31, 2), iW, bias=v)
    merge(5)
    fill(A("c17"), WT, ACT.Silu)
    fill(A("c64", 0, 16), 64.0)
    fill(A("c64", 16, 24), -33 * 64.0 / 128)
    merge(2)
    iota(A("tmpc", 192, 208), [[0, 2], [1, 8]], 0, 0)
    two, neg, one = A("BD", 0, 16), A("BD", 16, 32), A("BD", 32, 48)
    for o, v in ((two, 2 * WT), (neg, -WT), (one, WT)):
        ts(o, A("tmpc", 192, 208), cG, EQ, v, MUL)
    merge(3)
    asel(A("tmpb"), A("ones"), [[0, 2], [-16, 8], [-1, 17]], 1, 1)
    ms(A("tmpb", 0, 272, 17), 0.0)
    cp(A("PF"), A("tmpb", 0, 136))
    ts(A("PF0"), A("PF"), m0, MUL)
    ts(A("PH", 0, 136), A("tmpb", 0, 136), 1.0 / 32, MUL)
    ts(A("PH", 136, 272), A("tmpb", 136, 272), -1.0, MUL)
    merge(2)
    asel(A("PH0", 0, 136), A("PH", 0, 136), [[-16, 8], [0, 17]], 0, 1, ALU.not_equal, BIG / 32768)
    asel(A("PH0", 136, 272), A("PH", 136, 272), [[-16, 8], [0, 17]], 0, 1, ALU.not_equal, BIG / 1024)
    asel(A("SF"), A("ones", 0, 8), [[-16, 8]], 0, 1)
    act(A("SH", 0, 8), A("SF"), scale=1.0 / 32)
    act(A("SH", 8, 16), A("SF"), scale=-1.0)
    merge(2)
    ms(A("CK", 0, 544, 1, (0, 32)), 0.0)
    ms(A("CK", 0, 544, 1, (32, 64)), 16 * WT)
    merge(2)
    iota(A("CK", 0, 544, 1, (0, 1)), [[0, 32], [128, 17]], -1088, 0)
    for a in range(0, 544, 136):
        ms(A("CK", a, a + 136, 1, (64, 128)), -BIG * (32 if a % 272 else 1) / 64)
    merge(4)
    fill(A("CB", 0, 136), BIG / 128)
    fill(A("CB", 136, 272), BIG / 4)
    merge(2)
    ms(A("CK", 1, 272, 17), 0.0)
    ms(A("CK", 272, 544, 17), 0.0)
    merge(2)
    ms(A("CK", 272, 544, 17, (0, 1)), -1152.0)
    fill(A("CB", 0, 272, 17), 0.0)
    fill(A("d0"), 0.0)
    fill(A("d0", 0, 272, 17), 67108864.0)
    for a in range(0, 1152, 288):
        ms(A("Z", a, a + 288), 0.0)
    iota(A("dq", 0, 128), [[1, 8], [0, 16]], 0, 0)
    ts(A("BO"), A("dq", 0, 128), cG, EQ)
    asel(A("BL"), A("BO"), [[1, 128]], 0, -1, GT)
    iota(A("dq"), [[0, 16], [1, 16]], 0, 0)
    ts(A("Dq"), A("dq"), cR, ALU.not_equal, 2.0 ** 22, MUL)
    fill(A("dq"), 0.0)
    fill(A("dq", 0, 256, 16), 2.0 ** 23)
    fill(A("cq", 0, 128), -0.25 / 128)
    fill(A("aout"), 0.0)
    fill(A("nrow"), 0.0)
    for a in range(0, W_, 512):
        iota(A("ID", a, a + 512), [[1, 512]], a, 0)
    ID = lambda a, b, p=None: parts(A("ID", a, b, 1, p), ["ID"], 0, W_)

    kcol = lambda s, k: k + 1 if s or k else 0
    zneg = {}
    for s, ks in sorted(set((s, ks) for split in SPLIT for s in range(2) for nv, ks in split[s])):
        zneg[s, ks] = A("ZN", 272 * len(zneg), 272 * len(zneg) + 272)
        cols = [kcol(s, k) for k in range(16) if k % 4 < 4 - ks]
        mm(A("pd", 0, 272), A("Z", 0, 128), A("ones"), True, False)
        for c in cols:
            mm(A("pd", c, 272, 17), A("Ib"), neg, False, c == cols[-1])
        merge(1 + len(cols))
        act(zneg[s, ks], A("pd", 0, 272))

    def conv(bank, c0, name, n, start=True, a=0, stop=True):
        for r in range(16):
            mm(A(bank, c0, c0 + n // 16), A("Qh", 16 - r, 144 - r), A(name, a + r, a + n, 16), start and r == 0, stop and r == 15)
        merge(16)

    def kin(s, h, t):
        a, b, bu = 128 * h, 128 * h + 128, A("bU", 16 * s + 8 * h, 16 * s + 8 * h + 8)
        at("kin%d%d" % (s, h))
        if s == 0:
            lin("kin0%d" % h, A("c16", a, b), I(KIN, bu), mid0, m0)
            pu = A("pk%d" % h, 288, 416)
            mm(pu, A("I1"), A("t16", a, b), True, False)
            if t == 0:
                mm(pu, A("I1"), A("v16", a, b), False, False)
                merge(2)
            mm(pu, A("I0"), A("c16", a, b), False, True)
            ts(A("cU", a, b), pu, far0 if t else MID, ADD)
        else:
            cp(A("cU", a, b), I(KIN, bu))
            ts(A("c16", a, b), A("cU", a, b), MID, SUB)

    def starts(h):
        conv("pk%d" % h, 0, "t16", 128, a=128 * h)
        ts(A("bU", 8 * h, 8 * h + 8), A("pk%d" % h, 0, 8), MID, ADD)

    def early_kin(t):
        lo = B_ + L_ * ((rank - t) % N)
        at("far")
        iota(XC(lo, lo + 256), [[0, 256]], 8192, 0)
        kin(0, 1, t)

    act(A("e16", 0, 256), A("t16"), bias=MID - home - 127.5, func=ACT.Abs)
    ts(A("v16"), A("e16", 0, 256), 128.0, LT, float(W_ - home), MUL)
    for h in (1, 0):
        at("t%d" % h)
        starts(h)
    early_kin(0)
    wv = lambda j, n=16: A("w", 16 * j, 16 * j + n)
    uv = lambda j, n=16: A("u", 16 * j, 16 * j + n)

    for t in range(VIS):
        last = t == VIS - 1
        r_ = (rank - t) % N
        lo = B_ + L_ * r_
        fl = FB + lo
        z = lambda a=0, b=256: A("zin", 256 * t + a, 256 * t + b)
        xw = 512 * t
        others = [(r_ + d) % N for d in range(1, N)]
        at("yu", t)
        kin(0, 0, t)
        at("yu")
        dma("Y", A("yrow"), A("KN", fl, fl + 256))
        lin("gu", A("g16", 256, 512), A("KN", lo, lo + 256), -MID)
        lin("gy", A("g16", 0, 256), A("KN", fl, fl + 256), -MID - UP)
        conv("pw", 96, "g16", 512)
        yu = lambda a, b: A("pw", 96 + a, 96 + b)
        ts(uv(0, 32), yu(0, 32), MID, ADD)
        tt(A("o1", 0, 64, 2), yu(0, 32), spM, SUB)
        at("live")
        act(wv(0, 32), yu(0, 32), bias=MID - lo - 127.5, func=ACT.Abs)
        tt(wv(4), wv(0), wv(1), MIN)
        live = A("lv")
        ts(live, wv(4), 128.0, GT)
        at("wts")
        lin("lvN", wv(14), live, -MID, float(W_))
        lin("wt", wv(16), live, 1.0, MID - 1)
        tt(wv(15), yu(0, 16), wv(14), MAX)
        at("py")
        lin("py", A("e16", 0, 256), I(KINS, uv(0)), -MID)
        at("fu")
        lin("fu", A("e16", 256, 512), I(A("KN", FB), uv(1)), -MID - UP)
        at("colY")
        mm(A("pz0", 0, 256), A("I1"), A("g16", 256, 512), True, False)
        mm(A("pz0", 0, 256), A("I0"), A("e16", 0, 256), False, True)
        lin("colY", A("colY"), A("pz0", 0, 256), MID)
        dma("Y", A("XWn", xw, xw + 256), X(lo, lo + 256))
        at("held")
        conv("pc", 0, "e16", 512, stop=False)
        for a in (0, 16):
            mm(A("pc", a, a + 16), If, A("nW", 16 * r_, 16 * r_ + 16), False, False)
        mm(A("pc", 0, 16), A("ones", 0, 128), A("c64", 0, 16), False, False)
        mm(A("pc", 0, 16), A("I8"), live, False, True)
        merge(4)
        ts(A("o0", 1, 64, 2), A("pc", 0, 32), 0.0, EQ)
        scan(A("o2", 0, 32), A("o0", 0, 32), A("o1", 0, 32), MUL, ADD)
        cp(uv(2), A("o2", 1, 32, 2))
        cp(I(KINS, uv(2)), A("colY"))
        at("turn")
        tt(A("o0", 33, 64, 2), A("o0", 33, 64, 2), A("o0", 1, 32, 2), MUL)
        scan(A("o2", 32, 64), A("o0", 32, 64), A("o1", 32, 64), MUL, ADD)
        cp(uv(3), A("o2", 33, 64, 2))
        scatter("turn", I(FEET, uv(3)), A("yrow"))
        at("p16")
        lin("p16", A("p16"), I(KIN, A("bU", 0, 16)), -MID)
        dma("Y", A("KWn", 0, 256), A("KN", lo, lo + 256))
        dma("Y", A("nrow", 0, 256, 1, row0), ID(lo, lo + 256, row0))
        if t == 0:
            at("TT")
            dma("Y", A("TT"), KINS)
            dma("Y", A("TT", 0, W_, 1, row0), ext("tin"))
        if last:
            at("down")
            for a in (B_, B_ + 512):
                lin("down", A("KN", FB + a, FB + a + 512), A("KN", FB + a, FB + a + 512), -float(UP))
            for j in others:
                a = B_ + 256 * j
                dma("Y", ext("yk", 256 * j, 256 * j + 256), A("KN", a, a + 256))
                dma("Y", ext("yx", 256 * j, 256 * j + 256), X(a, a + 256))
        at("Ain")
        if t > 0:
            a0 = A("ain", 8 * t, 8 * t + 1)
            ts(A("acc", 2, 3), a0, 402653184.0, ADD, 402653184.0, SUB)
            act(A("acc", 3, 4), A("acc", 2, 3), scale=-1.0, bias=a0)
            act(A("d0", 1, 272, 17), A("c17"), scale=A("acc", 3, 4), bias=15.5 * WT)
        for h in (1, 0):
            at("zp%d" % h)
            for c in range(8):
                asel(parts(A("zp", 128 * h + c, 128 * h + 128, 8), ["zp"], 128 * h + 16 * c, 128 * h + 16 * c + 16),
                     z(128 * h + 16 * c, 128 * h + 16 * c + 16), [[0, 16]], 0, 0)
                if c % 2:
                    merge(2)
        if not last:
            at("nup")
            iota(A("nup"), [[1, 256]], lo + UP, 0)
        at("p16")
        conv("pc", 48, "p16", 256)
        ts(uv(10), A("pc", 48, 64), MID, ADD)
        at("xp")
        tt(A("xp"), I(XC(), uv(10)), z(), SUB)
        ts(A("mp"), A("xp"), 0.0, MAX)
        for s in range(2):
            for h in (1, 0):
                on = lambda name: at("%s%d%d" % (name, s, h))
                hs = 128 * h
                H = lambda name: A(name, hs, hs + 128)
                zz = lambda: H("zp") if s else z(hs, hs + 128)
                pz, pk, xn, mn, zo = "pz%d" % h, "pk%d" % h, "x%db" % h, "m%db" % h, 288 * (2 * s + h)
                win = XC() if s else A("XX", 0, 2 * W_) if t else A("XX", W_)
                nv, ks = SPLIT[t > 0][s][1 - h]
                if s == 1:
                    kin(1, h, t)
                if s == 1 and h == 1:
                    at("stay")
                    asel(A("D"), A("Di"), [[0, 32]], 0, 0)
                    ts(wv(22, 32), A("R", 16, 544, 17), 1.0 / WT, MUL, BIG, ADD)
                    lin("stay", wv(24, 32), wv(22, 32), -BIG)
                    tt(wv(26, 32), A("R", 16, 544, 17), A("R", 0, 544, 17), SUB)
                    ts(wv(28, 32), wv(26, 32), A("d0", 1, 2), ALU.is_ge, A("d0", 1, 2), MUL)
                on("z")
                for j in range(4):
                    mm(A(pz, j, 512, 4), A("Ib"), zz(), True, True)
                merge(4)
                on("gv")
                for a in range(0, nv, CUT[0]):
                    b = min(nv, a + CUT[0])
                    cp(A(xn, 16 * a, 16 * b), I(win, A("cU", hs + a, hs + b)))
                on("gs")
                for a in range(nv, 128, CUT[1]):
                    b = min(128, a + CUT[1])
                    act(A(xn, 16 * a, 16 * b), I(win, A("cU", hs + a, hs + b)))
                for j in range(4):
                    on("ABCD"[j])
                    xj, mj = A(xn, j, 2048, 4), A(mn, 512 * j, 512 * j + 512)
                    if j < 4 - ks:
                        tt(mj, xj, A(pz), MAX)
                        continue
                    pd = BANKS[s][1 - h][3 - j]
                    for i in range(4):
                        mm(A(pd, i, 512, 4), A("In"), zz(), i == 0, False)
                    merge(4)
                    mm(A(pd), A("Ib"), xj, False, True)
                    act(mj, A(pd), func=ACT.Abs)
                on("key")
                key = A(pk, 0, 272)
                col = lambda j: A(pk, j, 272, 17)
                if s:
                    mm(key, A("ones", 0, 128), A("CB"), True, False)
                mm(key, H("c16"), A("PH" if s else "PH0"), s == 0, False)
                if s == 0:
                    mm(col(0), H("t16"), A("SH"), False, False)
                mm(key, A("ones", 0, 128), A("CK", 272 * s, 272 * s + 272), False, False)
                mm(A(pk, 136, 272), H("c16"), A("PF" if s else "PF0"), False, False)
                if s == 0:
                    mm(col(136), H("t16"), A("SF"), False, False)
                merge(5 - 2 * s)
                if s:
                    mm(col(0), A("Pf", 0, 128), wv(24 + h), False, False)
                    mm(col(0), A("Pf", 128, 256), wv(28 + h), False, False)
                    mm(col(0), A("Pm"), A("D", 16 * h, 16 * h + 16), False, False)
                    merge(3)
                on("neg")
                mm(key, zz(), zneg[s, ks], False, False)
                kv = [k for k in range(16) if k % 4 < 4 - ks]
                for k in kv:
                    mm(col(kcol(s, k)), A(xn, k, 2048, 16), neg, False, False)
                merge(len(kv))
                turn = sorted(range(4), key=lambda j: (j if j < 4 - ks else j - 4 + ks, j))
                for j in turn:
                    on("ABCD"[j])
                    for i in range(4):
                        mm(col(kcol(s, 4 * i + j)), A(mn, 512 * j + i, 512 * j + 512, 4), two if j < 4 - ks else one,
                           False, s == 1 and j == turn[-1] and i == 3)
                    merge(4)
                if s == 0:
                    on("par")
                    mm(col(1), H("p16"), A("SH"), False, False)
                    mm(col(1), A("ones", 0, 128), A("CK", 273, 544, 17), False, False)
                    mm(col(137), H("p16"), A("SF"), False, False)
                    merge(3)
                    on("dec")
                    mm(col(1), H("xp"), neg, False, False)
                    mm(col(1), H("mp"), two, False, True)
                    merge(2)
                on("dec")
                scan(A("R", 272 * h, 272 * h + 272), A("d0"), key, ADD, MIN)
                dd = A("Di", 16 * h, 16 * h + 16)
                ts(dd, A("R", 272 * h + 16, 272 * h + 272, 17), 127, ALU.bitwise_and)
                cp(I(A("Z", zo, zo + 288), zl[s]), dd)
                bP = A(pk, 288, 296)
                mm(bP, A("ones", 0, 128), A("c64", 16, 24), True, False)
                for v in range(2):
                    for e in range(2):
                        a, c = zo + 144 * v + (1 - e) * (1 if s else 8), 32 * s + 16 * v + 8 * e
                        mm(bP, A("Z", a, a + 128), A("RE", c, c + 8), False, v + e == 2)
                merge(4)
                if s == 0:
                    ts(A("bU", 16 + 8 * h, 24 + 8 * h), bP, MID, ADD)
                    continue
                boh = A("bO", 16 * t + 8 * h, 16 * t + 8 * h + 8)
                ts(boh, bP, MID, ADD)
                send(prv if last else nxt, [(A("bin", 16 * t + 8 * h, 16 * t + 8 * h + 8), boh)])
                at("zn%d" % h)
                lin("xs%d" % h, H("xs"), I(X(), boh))
                mm(A(pz, 0, 128), A("ones", 0, 128), A("cq", 0, 128), True, False)
                mm(A(pz, 0, 128), A("Ih"), z(hs, hs + 128), False, False)
                merge(2)
                zn = A("XWn", xw + 256 + hs, xw + 384 + hs)
                mm(A(pz, 0, 128), A("Ih"), H("xs"), False, True)
                ts(zn, A(pz, 0, 128), BIG, ADD, BIG, SUB)
                if not last:
                    send(nxt, [(A("zin", 256 * t + 256 + hs, 256 * t + 384 + hs), zn)])
                at("brow%d" % h)
                lin("brow%d" % h, H("brow"), I(ID(0, W_), boh), -MID)
                at("v%d" % h)
                lin("v%d" % h, H("v16"), I(KIN, boh), -MID)
                if h == 0:
                    act(A("KWn", 256, 512), A("v16"), bias=sgm, scale=sgn)
                at("E8")
                if h == 1:
                    mm(A("pn", 0, 256), A("Ib"), A("Dq"), True, False)
                for c0, c1 in ((8, 12), (12, 16)) if h else ((0, 3), (3, 6), (6, 8)):
                    at("E%d" % c0)
                    for c in range(c0, c1):
                        ts(A("E", 272 * c, 256 * c + 256), A("brow", 16 * c, 256), A(pk, 288 + c % 8, 289 + c % 8),
                           EQ, A("w", 256 + c, 257 + c), MUL)
                    merge(c1 - c0)
                    for c in range(c0, c1):
                        mm(A("pn", 16 * c, 16 * c + 16), A("BL"), A("E", 272 * c, 272 * c + 16), False, False)
                        if c < 15:
                            mm(A("pn", 16 * c + 16, 256), A("BO"), A("E", 272 * c + 16, 256 * c + 256), False, c == 7)
                    merge(2 * (c1 - c0) - (c1 == 16))
        at("zn0")
        bi = lambda h: A("bin", 16 * t + 8 * h, 16 * t + 8 * h + 8)
        if last:
            dma("Y", ext("yz"), A("XWn", xw + 256, xw + 512))
        if 0 < t < VIS - 1:
            for h in (1, 0):
                at("T%d" % h)
                bb = A("bb", 128 * h, 128 * h + 128)
                lin("bb%d" % h, bb, A("brow", 128 * h, 128 * h + 128), MID + UP)
                scatter("T%d" % h, I(A("TT"), A("oin", 16 * t + 8 * h, 16 * t + 8 * h + 8)), bb)
        if not last:
            for h in (1, 0):
                at("t%d" % h)
                lin("t%d" % h, A("t16", 128 * h, 128 * h + 128), I(A("TT", 0, W_), bi(h)), -MID - UP)
                starts(h)
        if t == VIS - 2:
            at("home")
            dma("Y", A("trt"), A("TT", 0, W_, 1, row0))
            lin("home", A("trh"), A("trt"), -float(UP))
            send(prv, [(ext("tback"), A("trh"))])
            dma("Y", A("TT", 0, W_, 1, row0), ext("tback"))
        at("may")
        bW = wv(30)
        ts(bW, A("bO", 16 * t, 16 * t + 16), MID, SUB)
        act(wv(18), bW, bias=MID - lo - 127.5, func=ACT.Abs)
        tt(A("q1", 32, 64, 2), bW, A("cw", 64, 80), SUB)
        act(wv(19), wv(18), bias=-131072.0, scale=1024.0)
        tt(A("thr"), wv(19), wv(14), MIN)
        if not last:
            asel(A("q1", 96, 128, 2), A("q1", 32, 64, 2), [[0, 16]], 0, 0)
        at("vl")
        conv("pd", 0, "v16", 256)
        ts(uv(5), A("pd", 0, 16), MID - FO, ADD)
        tt(A("q1", 64, 96, 2), A("pd", 0, 16), A("cw", 80, 96), SUB)
        at("hit")
        lin("hit", A("HC"), I(FEET, uv(5)), -MID if last else -MID - UP)
        conv("pd", 16, "HC", 256)
        tt(wv(17), A("pd", 16, 32), bW, EQ)
        at("cnt")
        scan(A("tmpc"), A("dq"), A("pn", 0, 256), ADD, MIN)
        cnt = A("tmpc", 15, 256, 16)
        at("seat")
        n = 96 if last else 128
        tt(A("q0", 1, 32, 2), cnt, A("thr"), LT)
        tt(A("q0", 33, 64, 2), cnt, A("thr"), LT)
        merge(2)
        if not last:
            ts(A("q0", 97, 128, 2), cnt, 0.5, LT)
        tt(A("q0", 65, 96, 2), wv(17), A("q0", 1, 32, 2), MUL)
        scan(A("q2", 0, n), A("q0", 0, n), A("q1", 0, n), MUL, ADD)
        ts(A("sl", 64 * t, 64 * t + n // 2), A("q2", 1, n, 2), MID, ADD)
        sl = lambda j: A("sl", 64 * t + 16 * j, 64 * t + 16 * j + 16)
        at("par")
        tt(I(KINS, sl(1)), A("KWn", 256, 512), A("nrow"), MAX)
        at("KN")
        act(A("KS") if last else A("KN", lo, lo + 256), I(A("KWn"), sl(0)), func=ACT.Abs)
        at("XC")
        if last:
            lin("XS", A("XS"), I(A("XWn", xw, xw + 512), sl(0)))
            dma("Y", ext("yk", 256 * r_, 256 * r_ + 256), A("KS"))
            dma("Y", ext("yx", 256 * r_, 256 * r_ + 256), A("XS"))
        else:
            lin("XC", XC(lo, lo + 256), I(A("XWn", xw, xw + 512), sl(0)))
            asel(X(lo, lo + 256), XC(lo, lo + 256), [[0, 256]], 0, 0)
            early_kin(t + 1)
        at("FT")
        tt(A("fw"), wv(15), A("q2", 33, 64, 2), MIN)
        mm(A("pn", 0, 256), A("Im"), A("g16", 0, 256), True, False)
        for r in range(16):
            mm(A("pn", r, 256, 16), A("If", r, r + 128), A("fw"), False, r == 15)
        merge(16)
        at("foot")
        scatter("foot", I(FEET, sl(2)), ID(lo, lo + 256) if last else A("nup"))
        at("FT")
        tt(A("KN", fl, fl + 256), A("KN", fl, fl + 256), A("pn", 0, 256), ADD)
        at("Aout")
        if not last:
            mm(A("pc", 32, 48), A("ones", 0, 128), live, True, False)
            mm(A("pc", 32, 48), A("onef"), A("q0", 1, 32, 2), False, True)
            merge(2)
            act(wv(21), A("pc", 32, 48), bias=-15.5 / 16, accum=A("aout", 8 * t, 8 * t + 1))
            pa = (A("ain", 8 * t + 8, 8 * t + 16), A("aout", 8 * t, 8 * t + 8))
            send(nxt, [pa] if t == VIS - 2 else [pa, (A("oin", 16 * t + 16, 16 * t + 32), sl(3))])
        else:
            for h in (1, 0):
                at("T%d" % h)
                bb, a = A("bb", 128 * h, 128 * h + 128), 64 * t - 16 + 8 * h
                act(bb, I(ID(0, W_), bi(h)))
                cp(I(A("TT"), A("sl", a, a + 8)), bb)
            at("out")
            dma("Y", ext("yt"), A("TT", 0, W_, 1, row0))
            dma("S", ext("yp"), A("KN", 0, B_, 1, row0))
            for j in others:
                dma("S", ext("yk", 256 * j, 256 * j + 256, slice(*row0)),
                    A("KN", B_ + 256 * j, B_ + 256 * j + 256, 1, row0))
            dma("Y", ext("yf"), A("KN", FB + B_, FB + W_, 1, row0))
    return ops


def depend(ops):
    hist = {}
    bank = lambda name: name in SCRATCH and SCRATCH[name][0] == "psum"
    for i, o in enumerate(ops):
        dep = {}
        for acc, wr in ((o["r"], False), (o["w"], True)):
            for name, a, b in acc:
                for j, wj, aj, bj in hist.get(name, ()):
                    other = ops[j]["e"] != o["e"] or ops[j]["k"] != "c" or o["k"] != "c"
                    if bank(name) and other:
                        dep[j] = True
                    elif a < bj and aj < b and (wr or wj):
                        dep[j] = dep.get(j, False) or other or o["e"] != "P"
                    elif bank(name):
                        dep[j] = dep.get(j, False)
        for acc, wr in ((o["r"], False), (o["w"], True)):
            for name, a, b in acc:
                h = hist.setdefault(name, [])
                if bank(name):
                    h[:] = []
                elif wr:
                    h[:] = [e for e in h if not (a <= e[2] and e[3] <= b)]
                h.append((i, wr, a, b))
        dep.pop(i, None)
        if o["k"] == "r":
            dep = {o["x"][2]: False}
        o["dep"] = dep


def arrange(ops):
    named = {}
    for i, o in enumerate(ops):
        named.setdefault((o["e"], o["b"], o["v"]), []).append(i)
    need = [set(o["dep"]) for o in ops]
    for e, lists in ORDER.items():
        before, done = None, set()
        for v in range(VIS):
            for word in lists[(v > 0) + (v == VIS - 1)].split():
                name, _, nth = word.partition(".")
                calls = named.get((e, name.rstrip("-"), v - name.endswith("-")), [])
                calls = calls[int(nth) - 1:int(nth)] if nth else [i for i in calls if i not in done]
                if calls:
                    done.add(calls[0])
                    need[calls[0]].add(before)
                    before = calls[0]
    order, placed = [], {None}
    while len(order) < len(ops):
        ready = [i for i in range(len(ops)) if i not in placed and need[i] <= placed]
        assert ready
        order += ready
        placed.update(ready)
    return order


def emit(g, T, ops, order):
    queue = {"V": g.vector, "S": g.scalar, "P": g.tensor, "G": g, "Y": g.sync}
    place = {}
    seq = {}
    for i in order:
        if ops[i]["k"] == "c":
            seq[ops[i]["e"]] = seq.get(ops[i]["e"], 0) + 1
            place[i] = seq[ops[i]["e"]]
    known = {e: {} for e in queue}
    clock = {}
    waits = {}
    marked = set()
    for i in order:
        o = ops[i]
        if o["k"] == "r":
            clock[i] = {("o", i): 1}
            continue
        kn = known[o["e"]]
        sign = lambda j: (ops[j]["e"], place[j]) if ops[j]["k"] == "c" else (("o", j), 1)
        covers = lambda seen, j: seen.get(sign(j)[0], 0) >= sign(j)[1]
        wl = [j for j in o["dep"] if o["dep"][j] and not covers(kn, j)]
        wl = [j for j in wl if not any(k != j and covers(clock[k], j) for k in wl)]
        for j in wl:
            marked.add(j)
            for k2, v2 in clock[j].items():
                if kn.get(k2, 0) < v2:
                    kn[k2] = v2
        waits[i] = wl
        c = dict(kn)
        if o["k"] == "c":
            c[o["e"]] = place[i]
        else:
            c[("o", i)] = 1
        clock[i] = c
    count = {}
    target = {}
    nd = 0
    sent = 0
    for i in order:
        o = ops[i]
        if o["k"] == "r":
            target[i] = (o["x"][0], o["x"][1])
        elif o["k"] == "d":
            target[i] = ("d%d" % nd, 16 * len(o["f"]))
            nd += 1
        elif o["k"] == "c" and i in marked:
            count[o["e"]] = count.get(o["e"], 0) + 1
            target[i] = ("e" + o["e"], count[o["e"]])
    for i in order:
        o = ops[i]
        if o["k"] == "r":
            continue
        q = queue[o["e"]]
        for j in waits[i]:
            q.wait_ge(T.sem[target[j][0]], target[j][1])
        for f in o["f"]:
            ins = f(q)
            if o["k"] == "d":
                ins.then_inc(T.sem[target[i][0]], 16)
        if o["k"] == "d":
            continue
        if o["k"] == "s":
            sent += o["x"]
        elif i in marked:
            ins.then_inc(T.sem[target[i][0]], 1)
    g.wait_ge(T.sem.sent, sent)
    for i in order:
        if ops[i]["k"] in ("d", "r") and i not in marked:
            g.sync.wait_ge(T.sem[target[i][0]], target[i][1])


def rank_program(g, core, T, topo):
    rank = T.rank_of(core)
    if rank is None:
        return
    ops = build(T, topo, core, rank)
    depend(ops)
    emit(g, T, ops, arrange(ops))
